import numpy as np
import ml_dtypes


def mxq(x, axis, fmt="e4m3"):
    dtype, down = {"e4m3": (ml_dtypes.float8_e4m3fn, 7), "e5m2": (ml_dtypes.float8_e5m2, 14)}[fmt]
    v = np.moveaxis(np.asarray(x, np.float32).astype(ml_dtypes.bfloat16).astype(np.float64), axis, -1)
    blocks = v.reshape(v.shape[:-1] + (-1, 32))
    amax = np.abs(blocks).max(-1, keepdims=True)
    byte = np.maximum(np.where(amax > 0, np.frexp(amax)[1] - 1 + 127, 0) - down, 1)
    scale = np.exp2(byte - 127.0)
    codes = (blocks / scale).astype(np.float32).astype(dtype).astype(np.float64)
    return np.moveaxis((codes * scale).reshape(v.shape), -1, axis)


WIDE = False


def mx_kscale(k):
    if not WIDE:
        return np.ones(k)
    levels = np.array([18, -18])
    if k % 512:
        return np.exp2(np.random.permutation(np.resize(levels, k // 32))).repeat(32)
    a = np.empty((k // 512, 16))
    for p in range(k // 512):
        a[p, :8] = np.random.permutation(np.resize(levels, 8))
        for g in range(8):
            far = levels[np.abs(levels - a[p, g]) >= 10]
            a[p, g + 8] = far[np.random.randint(len(far))]
    return np.exp2(a.ravel()).repeat(32)


def f64(x):
    return np.asarray(x).astype(np.float64)


def striped(idx):
    return np.tile(np.asarray(idx).reshape(-1, 16).T, (8, 1)).astype(np.uint16)


def unstriped(offs):
    return offs[:16].T.reshape(-1).astype(np.int64)


E2M1 = np.array([0.0, 0.5, 1.0, 1.5, 2.0, 3.0, 4.0, 6.0, -0.0, -0.5, -1.0, -1.5, -2.0, -3.0, -4.0, -6.0])


def pack_weight(w, fmt):
    k, n = w.shape
    w = f64(np.asarray(w, np.float32).astype(ml_dtypes.bfloat16)).reshape(k // 32, 32, n)
    amax = np.abs(w).max(1)
    if fmt == "e4m3":
        byte = np.frexp(amax)[1] - 1 + 127 - 7
    else:
        mant, ex = np.frexp(amax / 6.0)
        byte = np.where(mant > 0.5, ex, ex - 1) + 127
    byte = np.clip(np.where(amax > 0, byte, 1), 1, 254)
    scaled = (w * np.exp2(127.0 - byte)[:, None, :]).reshape(k, n).astype(np.float32)
    by_word = np.ascontiguousarray(scaled.reshape(k // 512, 128, 4, n).transpose(0, 1, 3, 2))
    if fmt == "e4m3":
        words = by_word.astype(ml_dtypes.float8_e4m3fn).view(np.uint8)
    else:
        c = by_word.astype(ml_dtypes.float4_e2m1fn).view(np.uint8) & 0xF
        words = (c[..., 0::2] | (c[..., 1::2] << 4)).reshape(k // 512, 128, 2 * n)
    return np.ascontiguousarray(words), np.ascontiguousarray(byte.astype(np.uint8).reshape(k // 512, 16, n))


def unpack_weight(words, scales, fmt):
    g, _, n = scales.shape
    words = np.ascontiguousarray(words).reshape(g, 128, n, -1)
    if fmt == "e4m3":
        vals = words.view(ml_dtypes.float8_e4m3fn).astype(np.float64)
    else:
        nib = np.empty((g, 128, n, 4), np.uint8)
        nib[..., 0::2] = words & 0xF
        nib[..., 1::2] = words >> 4
        vals = E2M1[nib]
    vals = vals * np.repeat(np.exp2(scales.astype(np.float64) - 127.0), 8, axis=1)[..., None]
    return vals.transpose(0, 1, 3, 2).reshape(g * 512, n)


def setup_inputs():
    n = np.random.standard_normal
    uni = np.random.uniform
    idx = np.random.permutation(2048)[:512]
    f_e = mx_kscale(512)
    f_i = np.ones(2048)
    f_i[idx] = mx_kscale(512)
    f_r = mx_kscale(1024)
    Bt_ = pack_weight(n((512, 2048)) / np.sqrt(512) / f_e[:, None], "e4m3")
    return {
        "xT": (n((512, 1024)) * f_r[None, :]).astype(np.float32),
        "A": (n((512, 2048)) / np.sqrt(512) * f_i[None, :]).astype(np.float32),
        "dyT": (n((512, 1024)) * f_e[:, None]).astype(np.float32),
        "Bt_words": Bt_[0],
        "Bt_scales": Bt_[1],
        "us": (uni(0.75, 1.3, (1024, 1))).astype(np.float32),
        "sc": np.tile(uni(0.75, 1.3, 2048) / f_i, (128, 1)).astype(np.float32),
        "wt": (uni(0.75, 1.3, (1024, 1)) / np.sqrt(1024) / f_r[:, None]).astype(np.float32),
        "offs": striped(idx),
    }


def reference(xT, A, dyT, Bt_words, Bt_scales, us, sc, wt, offs):
    idx = unstriped(offs)
    A_i = f64(A)[:, idx]
    Bt = unpack_weight(Bt_words, Bt_scales, "e4m3")
    Bt_i = Bt[:, idx]
    sc_i = f64(sc)[:1][:, idx]
    v = mxq(f64(dyT), 0, "e5m2").T @ Bt_i
    v2 = f64(wt) * f64(us) * sc_i * v
    da = mxq(f64(xT), 1, "e4m3") @ mxq(v2, 0, "e5m2")
    out_0 = np.zeros((512, 2048))
    out_0[:, idx] = da
    out_1 = mxq(v2, 1, "e5m2") @ mxq(A_i, 1, "e4m3").T
    return out_0, out_1

@@ -1,0 +1,257 @@
+from contextlib import ExitStack
+
+import concourse.mybir as mybir
+from concourse.masks import make_identity
+
+D, E, R, SLOTS, T = 512, 512, 1024, 512, 2048
+FLOPS = 2 * (E * R * SLOTS + R * D * SLOTS + SLOTS * R * D)
+
+F32 = mybir.dt.float32
+BF16 = mybir.dt.bfloat16
+I32 = mybir.dt.int32
+U32 = mybir.dt.uint32
+U16 = mybir.dt.uint16
+U8 = mybir.dt.uint8
+E4M3 = mybir.dt.float8_e4m3fn_x4
+E5M2 = mybir.dt.float8_e5m2_x4
+MULT = mybir.AluOpType.mult
+
+P = 128
+PACK = 4
+K_PASS = P * PACK
+ROW_PASSES = R // K_PASS
+D_BLOCKS = D // P
+WINDOWS = 3
+
+
+def tile_attend_glora_ax_kernel(
+    tc, xT, A, dyT, Bt_words, Bt_scales, us, sc, wt, offs, out_0, out_1
+):
+    nc = tc.nc
+    with ExitStack() as ctx:
+        keep = ctx.enter_context(tc.tile_pool(name="keep", bufs=1))
+        psum = ctx.enter_context(tc.psum_pool(name="psum", bufs=1))
+        banks = [psum.tile([P, K_PASS], F32, name="bank%d" % n) for n in range(8)]
+
+        def quarters(bank):
+            return bank[:].rearrange("p (c m) -> p c m", c=PACK)
+
+        def sbuf(name, shape, dtype):
+            return keep.tile(shape, dtype, name=name, align_bytes=64)
+
+        def quantize(name, grouped, fmt):
+            width = grouped.shape[1] // PACK
+            codes = sbuf(name + "_codes", [P, width], U32)
+            scales = sbuf(name + "_scales", [P, width], U8)
+            nc.vector.quantize_mx(out=codes[:].bitcast(fmt), scales=scales[:], in_=grouped)
+            return codes, scales
+
+        offsets = keep.tile([P, SLOTS // 16], U16, name="offsets")
+        nc.sync.dma_start(offsets[:], offs)
+
+        sc_pool = sbuf("sc_pool", [P, T], F32)
+        nc.vector.memset(sc_pool[0:96, :].bitcast(I32), 0)
+        nc.sync.dma_start(sc_pool[96:P, :], sc[96:P, :])
+        bt_scale_pool = sbuf("bt_scale_pool", [P, T], U8)
+        for q in range(4):
+            rows = Bt_scales[0, 4 * q : 4 * q + 4, :].bitcast(I32)
+            nc.sync.dma_start(
+                bt_scale_pool[32 * q : 32 * q + 32, :].bitcast(I32),
+                rows.unsqueeze(0).broadcast_to([8, 4, T // 4]),
+            )
+
+        def load_dy(name, r0, r1):
+            raw = sbuf(name, [P, PACK, r1 - r0], F32)
+            nc.sync.dma_start(raw[:], dyT[:, r0:r1].rearrange("(p j) r -> p j r", j=PACK))
+            return raw
+
+        dy_raw0 = load_dy("dy_raw0", 0, K_PASS)
+        bt_word_pool = sbuf("bt_word_pool", [P, T], I32)
+        nc.sync.dma_start(bt_word_pool[:], Bt_words[0].rearrange("p n t -> p (n t)").bitcast(I32))
+        us_cols = sbuf("us_cols", [P, ROW_PASSES, PACK], F32)
+        wt_cols = sbuf("wt_cols", [P, ROW_PASSES, PACK], F32)
+        nc.sync.dma_start(us_cols[:], us.rearrange("(g p t) o -> p g (t o)", g=ROW_PASSES, t=PACK))
+        nc.sync.dma_start(wt_cols[:], wt.rearrange("(g p t) o -> p g (t o)", g=ROW_PASSES, t=PACK))
+        dy_raw1a = load_dy("dy_raw1a", K_PASS, K_PASS + 256)
+        dy_raw1b = load_dy("dy_raw1b", K_PASS + 256, R)
+
+        x_raw = [sbuf("x_raw%d" % j, [P, R], F32) for j in range(D_BLOCKS)]
+        a_pool = [sbuf("a_pool%d" % j, [P, T], F32) for j in range(D_BLOCKS)]
+        nc.sync.dma_start(x_raw[0][:], xT[0:P, :])
+        for j in (0, 1):
+            nc.sync.dma_start(a_pool[j][:], A[j * P : (j + 1) * P, :])
+        nc.sync.dma_start(x_raw[1][:], xT[P : 2 * P, :])
+        for j in (2, 3):
+            nc.sync.dma_start(a_pool[j][:], A[j * P : (j + 1) * P, :])
+        for j in (2, 3):
+            nc.sync.dma_start(x_raw[j][:], xT[j * P : (j + 1) * P, :])
+
+        ident = sbuf("ident", [P, P], F32)
+        make_identity(nc, ident[:])
+        windows = [sbuf("window%d" % n, [P, T], F32) for n in range(WINDOWS)]
+
+        sc_row = sbuf("sc_row", [P, SLOTS], F32)
+        nc.vector.tensor_copy(sc_row[:], sc_pool[:].indirect(offsets[:]))
+        sc_turned = quarters(banks[0])
+        for c in range(PACK):
+            nc.tensor.transpose(sc_turned[:, c, :], sc_row[:, c * P : (c + 1) * P], ident[:])
+        sc_cols = sbuf("sc_cols", [P, PACK], F32)
+        nc.scalar.copy(sc_cols[:], sc_turned[:, :, P - 1])
+        sc_spread = quarters(banks[1])
+        for c in range(PACK):
+            nc.tensor.transpose(sc_spread[:, c, :], sc_cols[:, c : c + 1].to_broadcast([P, P]), ident[:])
+        sc_all = sbuf("sc_all", [P, SLOTS], F32)
+        nc.scalar.copy(sc_all[:], banks[1][:])
+
+        bt_scales = sbuf("bt_scales", [P, SLOTS], U8)
+        nc.vector.tensor_copy(bt_scales[:], bt_scale_pool[:].indirect(offsets[:]))
+        bt_codes = sbuf("bt_codes", [P, SLOTS], U32)
+
+        row_factor = sbuf("row_factor", [P, ROW_PASSES, PACK], F32)
+        nc.gpsimd.tensor_tensor(row_factor[:], us_cols[:], wt_cols[:], MULT)
+
+        def group_dy(copy, raw, m0, m1, grouped):
+            copy(
+                grouped[:].rearrange("p (t m j) -> p m t j", t=PACK, j=PACK)[:, m0:m1],
+                raw.rearrange("p j (m t) -> p m t j", t=PACK),
+            )
+
+        v2_tiles = [sbuf("v2_%d" % g, [P, PACK * SLOTS], BF16) for g in range(ROW_PASSES)]
+
+        def first_product(g, dy_codes, dy_scales, into, places):
+            v2 = v2_tiles[g]
+            for t in places:
+                v = banks[into[t]]
+                cols = slice(t * P, (t + 1) * P)
+                nc.tensor.matmul_mx(
+                    out=v[:], lhsT=dy_codes[:, cols].bitcast(E5M2), lhsT_scale=dy_scales[:, cols],
+                    rhs=bt_codes[:].bitcast(E4M3), rhs_scale=bt_scales[:], start=True, stop=True,
+                )
+                nc.vector.scalar_tensor_tensor(
+                    v2[:, t * SLOTS : (t + 1) * SLOTS], v[:], row_factor[:, g, t : t + 1], sc_all[:], MULT, MULT
+                )
+
+        def group_v2_rows(g, v2):
+            grouped = sbuf("v2_rows%d" % g, [P, SLOTS * PACK], BF16)
+            nc.scalar.copy(
+                grouped[:].rearrange("p (c n t) -> p c t n", n=4, t=PACK),
+                v2[:].rearrange("p (t c n) -> p c t n", n=4, t=PACK),
+            )
+            return grouped
+
+        def turn_words(src, blocks, grouped, into):
+            words = src.bitcast(F32)
+            out_words = grouped.bitcast(F32)
+            for b0 in range(0, blocks, 2):
+                bank = banks[into[b0 // 2]][:].rearrange("p (b u m) -> p b u m", b=2, u=2)
+                for b in range(2):
+                    for u in range(2):
+                        w0 = (b0 + b) * 256
+                        nc.tensor.transpose(bank[:, b, u, :], words[:, w0 + u : w0 + 256 : 2], ident[:])
+                nc.scalar.copy(
+                    out_words[:, b0 * 256 : (b0 + 2) * 256].rearrange("p (b m u) -> p b m u", b=2, u=2),
+                    bank.rearrange("p b u m -> p b m u"),
+                )
+
+        def turn_x(j, into):
+            grouped = sbuf("x_grouped%d" % j, [P, ROW_PASSES * K_PASS], BF16)
+            for g in range(ROW_PASSES):
+                bank = quarters(banks[into[g]])
+                for t in range(PACK):
+                    nc.tensor.transpose(bank[:, t, :], x_raw[j][:, g * K_PASS + t : (g + 1) * K_PASS : PACK], ident[:])
+                nc.scalar.copy(
+                    grouped[:, g * K_PASS : (g + 1) * K_PASS].rearrange("p (d t) -> p d t", t=PACK),
+                    bank.rearrange("p t d -> p d t"),
+                )
+            return grouped
+
+        def second_product(j, x_q, v2_rows_q, into, da_sb):
+            x_codes, x_scales = x_q
+            da = banks[into]
+            for g in range(ROW_PASSES):
+                cols = slice(g * P, (g + 1) * P)
+                nc.tensor.matmul_mx(
+                    out=da[:], lhsT=x_codes[:, cols].bitcast(E4M3), lhsT_scale=x_scales[:, cols],
+                    rhs=v2_rows_q[g][0][:].bitcast(E5M2), rhs_scale=v2_rows_q[g][1][:],
+                    start=(g == 0), stop=(g == ROW_PASSES - 1),
+                )
+            nc.scalar.copy(da_sb, da[:])
+            return da_sb
+
+        def scatter_and_store(j, da_sb):
+            window = windows[j % WINDOWS]
+            nc.vector.tensor_copy(window[:].indirect(offsets[:]), da_sb)
+            nc.sync.dma_start(out_0[j * P : (j + 1) * P, :], window[:])
+
+        def gather_a(j, dst):
+            nc.vector.tensor_copy(dst, a_pool[j][:].indirect(offsets[:]))
+
+        dy_grouped = [sbuf("dy_grouped%d" % g, [P, K_PASS * PACK], BF16) for g in range(ROW_PASSES)]
+        group_dy(nc.scalar.copy, dy_raw0[:, :, 0 : PACK * 48], 0, 48, dy_grouped[0])
+        group_dy(nc.vector.tensor_copy, dy_raw0[:, :, PACK * 48 : K_PASS], 48, P, dy_grouped[0])
+        dy_q0 = quantize("dy0", dy_grouped[0][:], E5M2)
+        nc.vector.tensor_copy(bt_codes[:], bt_word_pool[:].bitcast(U32).indirect(offsets[:]))
+        group_dy(nc.scalar.copy, dy_raw1a[:], 0, P // 2, dy_grouped[1])
+        group_dy(nc.scalar.copy, dy_raw1b[:], P // 2, P, dy_grouped[1])
+        v2_0, v2_1 = v2_tiles
+        first_product(0, *dy_q0, into=(2, 3, 4, 5), places=(0, 1))
+        dy_q1 = quantize("dy1", dy_grouped[1][:], E5M2)
+        first_product(0, *dy_q0, into=(2, 3, 4, 5), places=(2, 3))
+        first_product(1, *dy_q1, into=(6, 7, 0, 1), places=range(PACK))
+        v2_rows0 = group_v2_rows(0, v2_0)
+        x_grouped0 = turn_x(0, into=(2, 5))
+        v2_rows1 = group_v2_rows(1, v2_1)
+        v2_rows_q = [quantize("v2_rows0", v2_rows0[:], E5M2)]
+        x_q0 = quantize("x0", x_grouped0[:], E4M3)
+        a_low = sc_all[:].bitcast(BF16)
+        gather_a(0, a_low[:, 0:SLOTS])
+        gather_a(1, a_low[:, SLOTS : 2 * SLOTS])
+        a_high = sbuf("a_high", [P, 2 * SLOTS], BF16)
+        v2_rows_q.append(quantize("v2_rows1", v2_rows1[:], E5M2))
+        gather_a(2, a_high[:, 0:SLOTS])
+        gather_a(3, a_high[:, SLOTS : 2 * SLOTS])
+        for window in windows:
+            for c in range(2):
+                nc.vector.memset(window[:, c * T // 2 : (c + 1) * T // 2].bitcast(I32), 0)
+        x_grouped1 = turn_x(1, into=(0, 1))
+        x_q = [x_q0, quantize("x1", x_grouped1[:], E4M3)]
+        v2_slots = [sbuf("v2_slots%d" % g, [P, K_PASS * PACK], BF16) for g in range(ROW_PASSES)]
+        turn_words(v2_0[:], PACK, v2_slots[0][:], into=(3, 4))
+        turn_words(v2_1[:], PACK, v2_slots[1][:], into=(6, 7))
+        a_slots = sbuf("a_slots", [P, D * PACK], BF16)
+        turn_words(a_low, 2, a_slots[:, 0 : 2 * K_PASS], into=(5,))
+        turn_words(a_high[:], 2, a_slots[:, 2 * K_PASS : 4 * K_PASS], into=(3,))
+        v2_slots_q = [quantize("v2_slots%d" % g, v2_slots[g][:], E5M2) for g in range(ROW_PASSES)]
+        a_codes, a_scales = quantize("a", a_slots[:], E4M3)
+        da_sb = [sbuf("da_sb%d" % j, [P, SLOTS], F32) for j in range(D_BLOCKS)]
+        second_product(0, x_q0, v2_rows_q, 2, da_sb[0][:])
+        scatter_and_store(0, da_sb[0][:])
+        x_grouped2 = turn_x(2, into=(6, 7))
+        x_q.append(quantize("x2", x_grouped2[:], E4M3))
+        second_product(1, x_q[1], v2_rows_q, 1, da_sb[1][:])
+
+        def third_product(g, h, into):
+            dx = sbuf("dx%d_%d" % (g, h), [P, 2, D], F32)
+            for e in range(2):
+                t = 2 * h + e
+                cols = slice(t * P, (t + 1) * P)
+                acc = banks[into[e]]
+                nc.tensor.matmul_mx(
+                    out=acc[:], lhsT=v2_slots_q[g][0][:, cols].bitcast(E5M2), lhsT_scale=v2_slots_q[g][1][:, cols],
+                    rhs=a_codes[:].bitcast(E4M3), rhs_scale=a_scales[:], start=True, stop=True,
+                )
+                nc.scalar.copy(dx[:, e, :], acc[:])
+            rows = out_1[g * K_PASS : (g + 1) * K_PASS, :].rearrange("(m t) d -> m t d", t=PACK)
+            nc.scalar.dma_start(rows[:, 2 * h : 2 * h + 2, :], dx[:])
+
+        third_product(0, 0, into=(3, 4))
+        x_grouped3 = turn_x(3, into=(0, 1))
+        x_q.append(quantize("x3", x_grouped3[:], E4M3))
+        scatter_and_store(1, da_sb[1][:])
+        third_product(0, 1, into=(5, 2))
+        second_product(2, x_q[2], v2_rows_q, 1, da_sb[2][:])
+        third_product(1, 0, into=(6, 7))
+        second_product(3, x_q[3], v2_rows_q, 0, da_sb[3][:])
+        third_product(1, 1, into=(3, 4))
+        scatter_and_store(2, da_sb[2][:])
+        scatter_and_store(3, da_sb[3][:])

@@ -36,12 +36,12 @@ def tile_attend_glora_ax_kernel(
         def quarters(bank):
             return bank[:].rearrange("p (c m) -> p c m", c=PACK)
 
-        def sbuf(name, shape, dtype):
-            return keep.tile(shape, dtype, name=name, align_bytes=64)
+        def sbuf(name, shape, dtype, reuses=None):
+            return keep.tile(shape, dtype, name=name, tag=reuses or name, align_bytes=64)
 
-        def quantize(name, grouped, fmt):
+        def quantize(name, grouped, fmt, reuses=None):
             width = grouped.shape[1] // PACK
-            codes = sbuf(name + "_codes", [P, width], U32)
+            codes = sbuf(name + "_codes", [P, width], U32, reuses)
             scales = sbuf(name + "_scales", [P, width], U8)
             nc.vector.quantize_mx(out=codes[:].bitcast(fmt), scales=scales[:], in_=grouped)
             return codes, scales
@@ -51,11 +51,11 @@ def tile_attend_glora_ax_kernel(
 
         sc_pool = sbuf("sc_pool", [P, T], F32)
         nc.vector.memset(sc_pool[0:96, :].bitcast(I32), 0)
-        nc.sync.dma_start(sc_pool[96:P, :], sc[96:P, :])
+        nc.scalar.dma_start(sc_pool[96:P, :], sc[96:P, :])
         bt_scale_pool = sbuf("bt_scale_pool", [P, T], U8)
         for q in range(4):
             rows = Bt_scales[0, 4 * q : 4 * q + 4, :].bitcast(I32)
-            nc.sync.dma_start(
+            (nc.scalar if q < 3 else nc.sync).dma_start(
                 bt_scale_pool[32 * q : 32 * q + 32, :].bitcast(I32),
                 rows.unsqueeze(0).broadcast_to([8, 4, T // 4]),
             )
@@ -66,25 +66,14 @@ def tile_attend_glora_ax_kernel(
             return raw
 
         dy_raw0 = load_dy("dy_raw0", 0, K_PASS)
+        dy_raw1a = load_dy("dy_raw1a", K_PASS, K_PASS + 256)
         bt_word_pool = sbuf("bt_word_pool", [P, T], I32)
         nc.sync.dma_start(bt_word_pool[:], Bt_words[0].rearrange("p n t -> p (n t)").bitcast(I32))
         us_cols = sbuf("us_cols", [P, ROW_PASSES, PACK], F32)
         wt_cols = sbuf("wt_cols", [P, ROW_PASSES, PACK], F32)
-        nc.sync.dma_start(us_cols[:], us.rearrange("(g p t) o -> p g (t o)", g=ROW_PASSES, t=PACK))
-        nc.sync.dma_start(wt_cols[:], wt.rearrange("(g p t) o -> p g (t o)", g=ROW_PASSES, t=PACK))
-        dy_raw1a = load_dy("dy_raw1a", K_PASS, K_PASS + 256)
+        nc.scalar.dma_start(us_cols[:], us.rearrange("(g p t) o -> p g (t o)", g=ROW_PASSES, t=PACK))
+        nc.scalar.dma_start(wt_cols[:], wt.rearrange("(g p t) o -> p g (t o)", g=ROW_PASSES, t=PACK))
         dy_raw1b = load_dy("dy_raw1b", K_PASS + 256, R)
-
-        x_raw = [sbuf("x_raw%d" % j, [P, R], F32) for j in range(D_BLOCKS)]
-        a_pool = [sbuf("a_pool%d" % j, [P, T], F32) for j in range(D_BLOCKS)]
-        nc.sync.dma_start(x_raw[0][:], xT[0:P, :])
-        for j in (0, 1):
-            nc.sync.dma_start(a_pool[j][:], A[j * P : (j + 1) * P, :])
-        nc.sync.dma_start(x_raw[1][:], xT[P : 2 * P, :])
-        for j in (2, 3):
-            nc.sync.dma_start(a_pool[j][:], A[j * P : (j + 1) * P, :])
-        for j in (2, 3):
-            nc.sync.dma_start(x_raw[j][:], xT[j * P : (j + 1) * P, :])
 
         ident = sbuf("ident", [P, P], F32)
         make_identity(nc, ident[:])
@@ -139,30 +128,23 @@ def tile_attend_glora_ax_kernel(
             )
             return grouped
 
-        def turn_words(src, blocks, grouped, into):
+        def turn_words(src, grouped, into):
+            blocks = src.shape[1] // K_PASS
             words = src.bitcast(F32)
-            out_words = grouped.bitcast(F32)
-            for b0 in range(0, blocks, 2):
-                bank = banks[into[b0 // 2]][:].rearrange("p (b u m) -> p b u m", b=2, u=2)
-                for b in range(2):
-                    for u in range(2):
-                        w0 = (b0 + b) * 256
-                        nc.tensor.transpose(bank[:, b, u, :], words[:, w0 + u : w0 + 256 : 2], ident[:])
-                nc.scalar.copy(
-                    out_words[:, b0 * 256 : (b0 + 2) * 256].rearrange("p (b m u) -> p b m u", b=2, u=2),
-                    bank.rearrange("p b u m -> p b m u"),
-                )
+            bank = banks[into][:, 0 : blocks * 2 * P].rearrange("p (b u m) -> p b u m", b=blocks, u=2)
+            for b in range(blocks):
+                for u in range(2):
+                    nc.tensor.transpose(bank[:, b, u, :], words[:, b * 2 * P + u : (b + 1) * 2 * P : 2], ident[:])
+            nc.scalar.copy(
+                grouped.bitcast(F32).rearrange("p (b m u) -> p b m u", b=blocks, u=2),
+                bank.rearrange("p b u m -> p b m u"),
+            )
 
         def turn_x(j, into):
+            rounded = sbuf("x_rounded%d" % j, [P, R], BF16)
+            nc.gpsimd.tensor_copy(rounded[:], x_raw[j])
             grouped = sbuf("x_grouped%d" % j, [P, ROW_PASSES * K_PASS], BF16)
-            for g in range(ROW_PASSES):
-                bank = quarters(banks[into[g]])
-                for t in range(PACK):
-                    nc.tensor.transpose(bank[:, t, :], x_raw[j][:, g * K_PASS + t : (g + 1) * K_PASS : PACK], ident[:])
-                nc.scalar.copy(
-                    grouped[:, g * K_PASS : (g + 1) * K_PASS].rearrange("p (d t) -> p d t", t=PACK),
-                    bank.rearrange("p t d -> p d t"),
-                )
+            turn_words(rounded[:], grouped[:], into)
             return grouped
 
         def second_product(j, x_q, v2_rows_q, into, da_sb):
@@ -187,71 +169,96 @@ def tile_attend_glora_ax_kernel(
             nc.vector.tensor_copy(dst, a_pool[j][:].indirect(offsets[:]))
 
         dy_grouped = [sbuf("dy_grouped%d" % g, [P, K_PASS * PACK], BF16) for g in range(ROW_PASSES)]
-        group_dy(nc.scalar.copy, dy_raw0[:, :, 0 : PACK * 48], 0, 48, dy_grouped[0])
-        group_dy(nc.vector.tensor_copy, dy_raw0[:, :, PACK * 48 : K_PASS], 48, P, dy_grouped[0])
+        group_dy(nc.scalar.copy, dy_raw0[:], 0, P, dy_grouped[0])
         dy_q0 = quantize("dy0", dy_grouped[0][:], E5M2)
         nc.vector.tensor_copy(bt_codes[:], bt_word_pool[:].bitcast(U32).indirect(offsets[:]))
         group_dy(nc.scalar.copy, dy_raw1a[:], 0, P // 2, dy_grouped[1])
         group_dy(nc.scalar.copy, dy_raw1b[:], P // 2, P, dy_grouped[1])
+        a_pool = []
+
+        def load_a(j, reuses):
+            pool = sbuf("a_pool%d" % j, [P, T], F32, reuses)
+            nc.sync.dma_start(pool[:], A[j * P : (j + 1) * P, :])
+            a_pool.append(pool)
+
+        load_a(0, None)
+        x_raw = []
+
+        def load_x(j0, j1, queue, reuses):
+            blocks = sbuf("x_raw%d" % j0, [P, j1 - j0, R], F32, reuses)
+            queue.dma_start(blocks[:], xT[j0 * P : j1 * P, :].rearrange("(j p) r -> p j r", j=j1 - j0))
+            x_raw.extend(blocks[:, j, :] for j in range(j1 - j0))
+
+        load_x(0, 2, nc.scalar, "dy_raw0")
+        load_a(1, "bt_word_pool")
         v2_0, v2_1 = v2_tiles
         first_product(0, *dy_q0, into=(2, 3, 4, 5), places=(0, 1))
         dy_q1 = quantize("dy1", dy_grouped[1][:], E5M2)
         first_product(0, *dy_q0, into=(2, 3, 4, 5), places=(2, 3))
+        load_a(2, "dy_grouped1")
         first_product(1, *dy_q1, into=(6, 7, 0, 1), places=range(PACK))
+        load_x(2, 3, nc.sync, "dy1_codes")
+        load_a(3, "bt_codes")
+        load_x(3, 4, nc.sync, "dy1_scales")
         v2_rows0 = group_v2_rows(0, v2_0)
-        x_grouped0 = turn_x(0, into=(2, 5))
+        x_grouped0 = turn_x(0, into=2)
         v2_rows1 = group_v2_rows(1, v2_1)
         v2_rows_q = [quantize("v2_rows0", v2_rows0[:], E5M2)]
         x_q0 = quantize("x0", x_grouped0[:], E4M3)
         a_low = sc_all[:].bitcast(BF16)
         gather_a(0, a_low[:, 0:SLOTS])
         gather_a(1, a_low[:, SLOTS : 2 * SLOTS])
+        v2_rows_q.append(quantize("v2_rows1", v2_rows1[:], E5M2, None))
+        x_q = [x_q0] + [quantize("x%d" % j, turn_x(j, into=2 + j)[:], E4M3) for j in (1, 2)]
         a_high = sbuf("a_high", [P, 2 * SLOTS], BF16)
-        v2_rows_q.append(quantize("v2_rows1", v2_rows1[:], E5M2))
         gather_a(2, a_high[:, 0:SLOTS])
         gather_a(3, a_high[:, SLOTS : 2 * SLOTS])
         for window in windows:
             for c in range(2):
                 nc.vector.memset(window[:, c * T // 2 : (c + 1) * T // 2].bitcast(I32), 0)
-        x_grouped1 = turn_x(1, into=(0, 1))
-        x_q = [x_q0, quantize("x1", x_grouped1[:], E4M3)]
-        v2_slots = [sbuf("v2_slots%d" % g, [P, K_PASS * PACK], BF16) for g in range(ROW_PASSES)]
-        turn_words(v2_0[:], PACK, v2_slots[0][:], into=(3, 4))
-        turn_words(v2_1[:], PACK, v2_slots[1][:], into=(6, 7))
+        v2_slots = sbuf("v2_slots", [P, R * PACK], BF16)
+        for g, into in enumerate(((6, 7), (0, 1))):
+            for h in range(2):
+                cols = slice(2 * h * K_PASS, 2 * (h + 1) * K_PASS)
+                turn_words(v2_tiles[g][:, cols], v2_slots[:, g * K_PASS * PACK :][:, cols], into[h])
+        v2_slots_codes, v2_slots_scales = quantize("v2_slots", v2_slots[:], E5M2, "bt_codes")
         a_slots = sbuf("a_slots", [P, D * PACK], BF16)
-        turn_words(a_low, 2, a_slots[:, 0 : 2 * K_PASS], into=(5,))
-        turn_words(a_high[:], 2, a_slots[:, 2 * K_PASS : 4 * K_PASS], into=(3,))
-        v2_slots_q = [quantize("v2_slots%d" % g, v2_slots[g][:], E5M2) for g in range(ROW_PASSES)]
-        a_codes, a_scales = quantize("a", a_slots[:], E4M3)
-        da_sb = [sbuf("da_sb%d" % j, [P, SLOTS], F32) for j in range(D_BLOCKS)]
-        second_product(0, x_q0, v2_rows_q, 2, da_sb[0][:])
-        scatter_and_store(0, da_sb[0][:])
-        x_grouped2 = turn_x(2, into=(6, 7))
-        x_q.append(quantize("x2", x_grouped2[:], E4M3))
-        second_product(1, x_q[1], v2_rows_q, 1, da_sb[1][:])
+        a_codes = sbuf("a_codes", [P, D], U32)
+        a_scales = sbuf("a_scales", [P, D], U8)
+        for src, j0, j1, into in ((a_low, 0, 2, 5), (a_high[:, 0:SLOTS], 2, 3, 2), (a_high[:, SLOTS:], 3, 4, 5)):
+            grouped = a_slots[:, j0 * K_PASS : j1 * K_PASS]
+            turn_words(src, grouped, into)
+            cols = slice(j0 * P, j1 * P)
+            nc.vector.quantize_mx(out=a_codes[:, cols].bitcast(E4M3), scales=a_scales[:, cols], in_=grouped)
+        da_first = sbuf("da_first", [P, SLOTS], F32, "a_high")
+        second_product(0, x_q[0], v2_rows_q, 3, da_first[:])
+        scatter_and_store(0, da_first[:])
 
-        def third_product(g, h, into):
-            dx = sbuf("dx%d_%d" % (g, h), [P, 2, D], F32)
-            for e in range(2):
-                t = 2 * h + e
-                cols = slice(t * P, (t + 1) * P)
+        def third_product(g, t0, into):
+            count = len(into)
+            dx = sbuf("dx%d_%d" % (g, t0), [P, count, D], F32)
+            for e in range(count):
+                cols = slice(g * K_PASS + (t0 + e) * P, g * K_PASS + (t0 + e + 1) * P)
                 acc = banks[into[e]]
                 nc.tensor.matmul_mx(
-                    out=acc[:], lhsT=v2_slots_q[g][0][:, cols].bitcast(E5M2), lhsT_scale=v2_slots_q[g][1][:, cols],
+                    out=acc[:], lhsT=v2_slots_codes[:, cols].bitcast(E5M2), lhsT_scale=v2_slots_scales[:, cols],
                     rhs=a_codes[:].bitcast(E4M3), rhs_scale=a_scales[:], start=True, stop=True,
                 )
                 nc.scalar.copy(dx[:, e, :], acc[:])
             rows = out_1[g * K_PASS : (g + 1) * K_PASS, :].rearrange("(m t) d -> m t d", t=PACK)
-            nc.scalar.dma_start(rows[:, 2 * h : 2 * h + 2, :], dx[:])
+            nc.scalar.dma_start(rows[:, t0 : t0 + count, :], dx[:])
 
-        third_product(0, 0, into=(3, 4))
-        x_grouped3 = turn_x(3, into=(0, 1))
-        x_q.append(quantize("x3", x_grouped3[:], E4M3))
-        scatter_and_store(1, da_sb[1][:])
-        third_product(0, 1, into=(5, 2))
-        second_product(2, x_q[2], v2_rows_q, 1, da_sb[2][:])
-        third_product(1, 0, into=(6, 7))
-        second_product(3, x_q[3], v2_rows_q, 0, da_sb[3][:])
-        third_product(1, 1, into=(3, 4))
-        scatter_and_store(2, da_sb[2][:])
-        scatter_and_store(3, da_sb[3][:])
+        def da_block(j, into, reuses):
+            da_sb = sbuf("da_sb%d" % j, [P, SLOTS], F32, reuses)
+            second_product(j, x_q[j], v2_rows_q, into, da_sb[:])
+            scatter_and_store(j, da_sb[:])
+
+        third_product(0, 0, into=(6,))
+        third_product(0, 1, into=(7,))
+        da_block(1, 5, None)
+        third_product(0, 2, into=(0, 1))
+        x_q.append(quantize("x3", turn_x(3, into=3)[:], E4M3))
+        da_block(2, 6, "x_rounded3")
+        third_product(1, 0, into=(4, 2))
+        third_product(1, 2, into=(7, 0))
+        da_block(3, 1, None)

@@ -15,6 +15,7 @@ U8 = mybir.dt.uint8
 E4M3 = mybir.dt.float8_e4m3fn_x4
 E5M2 = mybir.dt.float8_e5m2_x4
 MULT = mybir.AluOpType.mult
+ADD = mybir.AluOpType.add
 
 P = 128
 PACK = 4
@@ -55,7 +56,7 @@ def tile_attend_glora_ax_kernel(
         bt_scale_pool = sbuf("bt_scale_pool", [P, T], U8)
         for q in range(4):
             rows = Bt_scales[0, 4 * q : 4 * q + 4, :].bitcast(I32)
-            (nc.scalar if q < 3 else nc.sync).dma_start(
+            (nc.scalar if q < 2 else nc.sync).dma_start(
                 bt_scale_pool[32 * q : 32 * q + 32, :].bitcast(I32),
                 rows.unsqueeze(0).broadcast_to([8, 4, T // 4]),
             )
@@ -78,6 +79,8 @@ def tile_attend_glora_ax_kernel(
         ident = sbuf("ident", [P, P], F32)
         make_identity(nc, ident[:])
         windows = [sbuf("window%d" % n, [P, T], F32) for n in range(WINDOWS)]
+        for window in windows[1:]:
+            nc.gpsimd.memset(window[:], 0.0)
 
         sc_row = sbuf("sc_row", [P, SLOTS], F32)
         nc.vector.tensor_copy(sc_row[:], sc_pool[:].indirect(offsets[:]))
@@ -92,7 +95,7 @@ def tile_attend_glora_ax_kernel(
         sc_all = sbuf("sc_all", [P, SLOTS], F32)
         nc.scalar.copy(sc_all[:], banks[1][:])
 
-        bt_scales = sbuf("bt_scales", [P, SLOTS], U8)
+        bt_scales = sbuf("bt_scales", [P, SLOTS], U8, "sc_pool")
         nc.vector.tensor_copy(bt_scales[:], bt_scale_pool[:].indirect(offsets[:]))
         bt_codes = sbuf("bt_codes", [P, SLOTS], U32)
 
@@ -142,7 +145,7 @@ def tile_attend_glora_ax_kernel(
 
         def turn_x(j, into):
             rounded = sbuf("x_rounded%d" % j, [P, R], BF16)
-            nc.gpsimd.tensor_copy(rounded[:], x_raw[j])
+            nc.gpsimd.tensor_scalar(rounded[:], x_raw[j], 1.0, 0.0, MULT, ADD)
             grouped = sbuf("x_grouped%d" % j, [P, ROW_PASSES * K_PASS], BF16)
             turn_words(rounded[:], grouped[:], into)
             return grouped
@@ -195,11 +198,11 @@ def tile_attend_glora_ax_kernel(
         first_product(0, *dy_q0, into=(2, 3, 4, 5), places=(0, 1))
         dy_q1 = quantize("dy1", dy_grouped[1][:], E5M2)
         first_product(0, *dy_q0, into=(2, 3, 4, 5), places=(2, 3))
-        load_a(2, "dy_grouped1")
+        load_a(2, "dy_raw1b")
+        load_x(2, 3, nc.sync, "dy0_codes")
+        load_a(3, "dy_grouped1")
         first_product(1, *dy_q1, into=(6, 7, 0, 1), places=range(PACK))
-        load_x(2, 3, nc.sync, "dy1_codes")
-        load_a(3, "bt_codes")
-        load_x(3, 4, nc.sync, "dy1_scales")
+        load_x(3, 4, nc.sync, "bt_codes")
         v2_rows0 = group_v2_rows(0, v2_0)
         x_grouped0 = turn_x(0, into=2)
         v2_rows1 = group_v2_rows(1, v2_1)
@@ -213,23 +216,18 @@ def tile_attend_glora_ax_kernel(
         a_high = sbuf("a_high", [P, 2 * SLOTS], BF16)
         gather_a(2, a_high[:, 0:SLOTS])
         gather_a(3, a_high[:, SLOTS : 2 * SLOTS])
-        for window in windows:
-            for c in range(2):
-                nc.vector.memset(window[:, c * T // 2 : (c + 1) * T // 2].bitcast(I32), 0)
+        for c in range(2):
+            nc.vector.memset(windows[0][:, c * T // 2 : (c + 1) * T // 2].bitcast(I32), 0)
         v2_slots = sbuf("v2_slots", [P, R * PACK], BF16)
         for g, into in enumerate(((6, 7), (0, 1))):
             for h in range(2):
                 cols = slice(2 * h * K_PASS, 2 * (h + 1) * K_PASS)
                 turn_words(v2_tiles[g][:, cols], v2_slots[:, g * K_PASS * PACK :][:, cols], into[h])
-        v2_slots_codes, v2_slots_scales = quantize("v2_slots", v2_slots[:], E5M2, "bt_codes")
+        v2_slots_codes, v2_slots_scales = quantize("v2_slots", v2_slots[:], E5M2, "dy_grouped1")
         a_slots = sbuf("a_slots", [P, D * PACK], BF16)
-        a_codes = sbuf("a_codes", [P, D], U32)
-        a_scales = sbuf("a_scales", [P, D], U8)
         for src, j0, j1, into in ((a_low, 0, 2, 5), (a_high[:, 0:SLOTS], 2, 3, 2), (a_high[:, SLOTS:], 3, 4, 5)):
-            grouped = a_slots[:, j0 * K_PASS : j1 * K_PASS]
-            turn_words(src, grouped, into)
-            cols = slice(j0 * P, j1 * P)
-            nc.vector.quantize_mx(out=a_codes[:, cols].bitcast(E4M3), scales=a_scales[:, cols], in_=grouped)
+            turn_words(src, a_slots[:, j0 * K_PASS : j1 * K_PASS], into)
+        a_codes, a_scales = quantize("a", a_slots[:], E4M3)
         da_first = sbuf("da_first", [P, SLOTS], F32, "a_high")
         second_product(0, x_q[0], v2_rows_q, 3, da_first[:])
         scatter_and_store(0, da_first[:])

@@ -15,7 +15,6 @@ U8 = mybir.dt.uint8
 E4M3 = mybir.dt.float8_e4m3fn_x4
 E5M2 = mybir.dt.float8_e5m2_x4
 MULT = mybir.AluOpType.mult
-ADD = mybir.AluOpType.add
 
 P = 128
 PACK = 4
@@ -143,12 +142,10 @@ def tile_attend_glora_ax_kernel(
                 bank.rearrange("p b u m -> p b m u"),
             )
 
-        def turn_x(j, into):
-            rounded = sbuf("x_rounded%d" % j, [P, R], BF16)
-            nc.gpsimd.tensor_scalar(rounded[:], x_raw[j], 1.0, 0.0, MULT, ADD)
+        def turn_x(j, rounded, into):
             grouped = sbuf("x_grouped%d" % j, [P, ROW_PASSES * K_PASS], BF16)
-            turn_words(rounded[:], grouped[:], into)
-            return grouped
+            turn_words(rounded, grouped[:], into)
+            return quantize("x%d" % j, grouped[:], E4M3)
 
         def second_product(j, x_q, v2_rows_q, into, da_sb):
             x_codes, x_scales = x_q
@@ -184,35 +181,38 @@ def tile_attend_glora_ax_kernel(
             nc.sync.dma_start(pool[:], A[j * P : (j + 1) * P, :])
             a_pool.append(pool)
 
+        def load_x(j0, j1, reuses):
+            raw = sbuf("x_raw%d" % j0, [P, j1 - j0, R], F32, reuses)
+            nc.sync.dma_start(raw[:], xT[j0 * P : j1 * P, :].rearrange("(j p) r -> p j r", j=j1 - j0))
+            return raw
+
+        def round_x(name, raw, copy):
+            rounded = sbuf(name, [P, raw.shape[1] * R], BF16)
+            copy(rounded[:], raw[:].rearrange("p j r -> p (j r)"))
+            return rounded
+
+        x_rounded01 = round_x("x_rounded01", load_x(0, 2, None), nc.scalar.copy)
         load_a(0, None)
-        x_raw = []
-
-        def load_x(j0, j1, queue, reuses):
-            blocks = sbuf("x_raw%d" % j0, [P, j1 - j0, R], F32, reuses)
-            queue.dma_start(blocks[:], xT[j0 * P : j1 * P, :].rearrange("(j p) r -> p j r", j=j1 - j0))
-            x_raw.extend(blocks[:, j, :] for j in range(j1 - j0))
-
-        load_x(0, 2, nc.scalar, "dy_raw0")
         load_a(1, "bt_word_pool")
         v2_0, v2_1 = v2_tiles
         first_product(0, *dy_q0, into=(2, 3, 4, 5), places=(0, 1))
         dy_q1 = quantize("dy1", dy_grouped[1][:], E5M2)
         first_product(0, *dy_q0, into=(2, 3, 4, 5), places=(2, 3))
-        load_a(2, "dy_raw1b")
-        load_x(2, 3, nc.sync, "dy0_codes")
+        x_raw2 = load_x(2, 3, "dy_raw1b")
+        load_a(2, "dy0_codes")
         load_a(3, "dy_grouped1")
         first_product(1, *dy_q1, into=(6, 7, 0, 1), places=range(PACK))
-        load_x(3, 4, nc.sync, "bt_codes")
+        x_raw3 = load_x(3, 4, "bt_codes")
         v2_rows0 = group_v2_rows(0, v2_0)
-        x_grouped0 = turn_x(0, into=2)
-        v2_rows1 = group_v2_rows(1, v2_1)
         v2_rows_q = [quantize("v2_rows0", v2_rows0[:], E5M2)]
-        x_q0 = quantize("x0", x_grouped0[:], E4M3)
+        x_q = [turn_x(0, x_rounded01[:, 0:R], 2)]
+        v2_rows1 = group_v2_rows(1, v2_1)
         a_low = sc_all[:].bitcast(BF16)
         gather_a(0, a_low[:, 0:SLOTS])
         gather_a(1, a_low[:, SLOTS : 2 * SLOTS])
         v2_rows_q.append(quantize("v2_rows1", v2_rows1[:], E5M2, None))
-        x_q = [x_q0] + [quantize("x%d" % j, turn_x(j, into=2 + j)[:], E4M3) for j in (1, 2)]
+        x_q.append(turn_x(1, x_rounded01[:, R : 2 * R], 3))
+        x_q.append(turn_x(2, round_x("x_rounded2", x_raw2, nc.vector.tensor_copy)[:], 4))
         a_high = sbuf("a_high", [P, 2 * SLOTS], BF16)
         gather_a(2, a_high[:, 0:SLOTS])
         gather_a(3, a_high[:, SLOTS : 2 * SLOTS])
@@ -255,7 +255,7 @@ def tile_attend_glora_ax_kernel(
         third_product(0, 1, into=(7,))
         da_block(1, 5, None)
         third_product(0, 2, into=(0, 1))
-        x_q.append(quantize("x3", turn_x(3, into=3)[:], E4M3))
+        x_q.append(turn_x(3, round_x("x_rounded3", x_raw3, nc.scalar.copy)[:], 3))
         da_block(2, 6, "x_rounded3")
         third_product(1, 0, into=(4, 2))
         third_product(1, 2, into=(7, 0))

@@ -20,7 +20,9 @@ P = 128
 PACK = 4
 K_PASS = P * PACK
 ROW_PASSES = R // K_PASS
-D_BLOCKS = D // P
+BANKS = 8
+QUADRANT = 32
+LIST_ROWS = 16
 WINDOWS = 3
 
 
@@ -31,7 +33,7 @@ def tile_attend_glora_ax_kernel(
     with ExitStack() as ctx:
         keep = ctx.enter_context(tc.tile_pool(name="keep", bufs=1))
         psum = ctx.enter_context(tc.psum_pool(name="psum", bufs=1))
-        banks = [psum.tile([P, K_PASS], F32, name="bank%d" % n) for n in range(8)]
+        banks = [psum.tile([P, K_PASS], F32, name="bank%d" % n) for n in range(BANKS)]
 
         def quarters(bank):
             return bank[:].rearrange("p (c m) -> p c m", c=PACK)
@@ -46,18 +48,20 @@ def tile_attend_glora_ax_kernel(
             nc.vector.quantize_mx(out=codes[:].bitcast(fmt), scales=scales[:], in_=grouped)
             return codes, scales
 
-        offsets = keep.tile([P, SLOTS // 16], U16, name="offsets")
+        offsets = keep.tile([P, SLOTS // LIST_ROWS], U16, name="offsets")
         nc.sync.dma_start(offsets[:], offs)
 
         sc_pool = sbuf("sc_pool", [P, T], F32)
-        nc.vector.memset(sc_pool[0:96, :].bitcast(I32), 0)
-        nc.scalar.dma_start(sc_pool[96:P, :], sc[96:P, :])
+        nc.vector.memset(sc_pool[0 : P - 1, :].bitcast(I32), 0)
+        nc.scalar.dma_start(sc_pool[P - 1 : P, :], sc[P - 1 : P, :])
+
         bt_scale_pool = sbuf("bt_scale_pool", [P, T], U8)
-        for q in range(4):
-            rows = Bt_scales[0, 4 * q : 4 * q + 4, :].bitcast(I32)
-            (nc.scalar if q < 2 else nc.sync).dma_start(
-                bt_scale_pool[32 * q : 32 * q + 32, :].bitcast(I32),
-                rows.unsqueeze(0).broadcast_to([8, 4, T // 4]),
+        for q in range(P // QUADRANT):
+            rows = Bt_scales[0, PACK * q : PACK * (q + 1), :].bitcast(I32)
+            queue = nc.scalar if q < 2 else nc.sync
+            queue.dma_start(
+                bt_scale_pool[QUADRANT * q : QUADRANT * (q + 1), :].bitcast(I32),
+                rows.unsqueeze(0).broadcast_to([QUADRANT // PACK, PACK, T // 4]),
             )
 
         def load_dy(name, r0, r1):
@@ -66,14 +70,16 @@ def tile_attend_glora_ax_kernel(
             return raw
 
         dy_raw0 = load_dy("dy_raw0", 0, K_PASS)
-        dy_raw1a = load_dy("dy_raw1a", K_PASS, K_PASS + 256)
+        dy_raw1a = load_dy("dy_raw1a", K_PASS, K_PASS + K_PASS // 2)
         bt_word_pool = sbuf("bt_word_pool", [P, T], I32)
         nc.sync.dma_start(bt_word_pool[:], Bt_words[0].rearrange("p n t -> p (n t)").bitcast(I32))
-        us_cols = sbuf("us_cols", [P, ROW_PASSES, PACK], F32)
-        wt_cols = sbuf("wt_cols", [P, ROW_PASSES, PACK], F32)
-        nc.scalar.dma_start(us_cols[:], us.rearrange("(g p t) o -> p g (t o)", g=ROW_PASSES, t=PACK))
-        nc.scalar.dma_start(wt_cols[:], wt.rearrange("(g p t) o -> p g (t o)", g=ROW_PASSES, t=PACK))
-        dy_raw1b = load_dy("dy_raw1b", K_PASS + 256, R)
+        us_tile = sbuf("us_tile", [P, ROW_PASSES, 2 * PACK], F32)
+        us_cols = us_tile[:, :, 0:PACK]
+        wt_tile = sbuf("wt_tile", [P, ROW_PASSES, 2 * PACK], F32)
+        wt_cols = wt_tile[:, :, 0:PACK]
+        nc.scalar.dma_start(us_cols, us.rearrange("(g p t) o -> p g (t o)", g=ROW_PASSES, t=PACK))
+        nc.scalar.dma_start(wt_cols, wt.rearrange("(g p t) o -> p g (t o)", g=ROW_PASSES, t=PACK))
+        dy_raw1b = load_dy("dy_raw1b", K_PASS + K_PASS // 2, R)
 
         ident = sbuf("ident", [P, P], F32)
         make_identity(nc, ident[:])
@@ -94,23 +100,23 @@ def tile_attend_glora_ax_kernel(
         sc_all = sbuf("sc_all", [P, SLOTS], F32)
         nc.scalar.copy(sc_all[:], banks[1][:])
 
-        bt_scales = sbuf("bt_scales", [P, SLOTS], U8, "sc_pool")
+        bt_scales = sbuf("bt_scales", [P, SLOTS], U8, reuses="sc_pool")
         nc.vector.tensor_copy(bt_scales[:], bt_scale_pool[:].indirect(offsets[:]))
         bt_codes = sbuf("bt_codes", [P, SLOTS], U32)
 
         row_factor = sbuf("row_factor", [P, ROW_PASSES, PACK], F32)
-        nc.gpsimd.tensor_tensor(row_factor[:], us_cols[:], wt_cols[:], MULT)
+        nc.gpsimd.tensor_tensor(row_factor[:], us_cols, wt_cols, MULT)
 
-        def group_dy(copy, raw, m0, m1, grouped):
-            copy(
+        def group_dy(raw, m0, m1, grouped):
+            nc.scalar.copy(
                 grouped[:].rearrange("p (t m j) -> p m t j", t=PACK, j=PACK)[:, m0:m1],
-                raw.rearrange("p j (m t) -> p m t j", t=PACK),
+                raw[:].rearrange("p j (m t) -> p m t j", t=PACK),
             )
 
         v2_tiles = [sbuf("v2_%d" % g, [P, PACK * SLOTS], BF16) for g in range(ROW_PASSES)]
 
-        def first_product(g, dy_codes, dy_scales, into, places):
-            v2 = v2_tiles[g]
+        def first_product(g, dy_q, into, places):
+            dy_codes, dy_scales = dy_q
             for t in places:
                 v = banks[into[t]]
                 cols = slice(t * P, (t + 1) * P)
@@ -119,144 +125,139 @@ def tile_attend_glora_ax_kernel(
                     rhs=bt_codes[:].bitcast(E4M3), rhs_scale=bt_scales[:], start=True, stop=True,
                 )
                 nc.vector.scalar_tensor_tensor(
-                    v2[:, t * SLOTS : (t + 1) * SLOTS], v[:], row_factor[:, g, t : t + 1], sc_all[:], MULT, MULT
+                    v2_tiles[g][:, t * SLOTS : (t + 1) * SLOTS], v[:], row_factor[:, g, t : t + 1], sc_all[:],
+                    MULT, MULT,
                 )
 
-        def group_v2_rows(g, v2):
+        def group_v2_rows(g):
             grouped = sbuf("v2_rows%d" % g, [P, SLOTS * PACK], BF16)
             nc.scalar.copy(
                 grouped[:].rearrange("p (c n t) -> p c t n", n=4, t=PACK),
-                v2[:].rearrange("p (t c n) -> p c t n", n=4, t=PACK),
+                v2_tiles[g][:].rearrange("p (t c n) -> p c t n", n=4, t=PACK),
             )
             return grouped
 
-        def turn_words(src, grouped, into):
-            blocks = src.shape[1] // K_PASS
+        def turn_pairs(src, grouped, into):
+            stretches = src.shape[1] // K_PASS
             words = src.bitcast(F32)
-            bank = banks[into][:, 0 : blocks * 2 * P].rearrange("p (b u m) -> p b u m", b=blocks, u=2)
-            for b in range(blocks):
+            bank = banks[into][:, 0 : stretches * 2 * P].rearrange("p (b u m) -> p b u m", b=stretches, u=2)
+            for b in range(stretches):
                 for u in range(2):
                     nc.tensor.transpose(bank[:, b, u, :], words[:, b * 2 * P + u : (b + 1) * 2 * P : 2], ident[:])
             nc.scalar.copy(
-                grouped.bitcast(F32).rearrange("p (b m u) -> p b m u", b=blocks, u=2),
+                grouped.bitcast(F32).rearrange("p (b m u) -> p b m u", b=stretches, u=2),
                 bank.rearrange("p b u m -> p b m u"),
             )
 
-        def turn_x(j, rounded, into):
+        def load_x(j, reuses=None):
+            raw = sbuf("x_raw%d" % j, [P, R], F32, reuses)
+            nc.sync.dma_start(raw[:], xT[j * P : (j + 1) * P, :])
+            return raw
+
+        def round_x(j, raw, copy):
+            rounded = sbuf("x_rounded%d" % j, [P, R], BF16)
+            copy(rounded[:], raw[:])
+            return rounded
+
+        def quantize_x(j, rounded, into):
             grouped = sbuf("x_grouped%d" % j, [P, ROW_PASSES * K_PASS], BF16)
-            turn_words(rounded, grouped[:], into)
+            turn_pairs(rounded[:], grouped[:], into)
             return quantize("x%d" % j, grouped[:], E4M3)
 
-        def second_product(j, x_q, v2_rows_q, into, da_sb):
+        def load_a(j, reuses=None):
+            pool = sbuf("a_pool%d" % j, [P, T], F32, reuses)
+            nc.sync.dma_start(pool[:], A[j * P : (j + 1) * P, :])
+            return pool
+
+        def gather_a(pool, listed):
+            nc.vector.tensor_copy(listed, pool[:].indirect(offsets[:]))
+
+        def second_product(j, x_q, v2_rows_q, into, reuses=None):
+            da_sb = sbuf("da_sb%d" % j, [P, SLOTS], F32, reuses)
             x_codes, x_scales = x_q
             da = banks[into]
             for g in range(ROW_PASSES):
                 cols = slice(g * P, (g + 1) * P)
+                v2_codes, v2_scales = v2_rows_q[g]
                 nc.tensor.matmul_mx(
                     out=da[:], lhsT=x_codes[:, cols].bitcast(E4M3), lhsT_scale=x_scales[:, cols],
-                    rhs=v2_rows_q[g][0][:].bitcast(E5M2), rhs_scale=v2_rows_q[g][1][:],
+                    rhs=v2_codes[:].bitcast(E5M2), rhs_scale=v2_scales[:],
                     start=(g == 0), stop=(g == ROW_PASSES - 1),
                 )
-            nc.scalar.copy(da_sb, da[:])
-            return da_sb
-
-        def scatter_and_store(j, da_sb):
+            nc.scalar.copy(da_sb[:], da[:])
             window = windows[j % WINDOWS]
-            nc.vector.tensor_copy(window[:].indirect(offsets[:]), da_sb)
+            nc.vector.tensor_copy(window[:].indirect(offsets[:]), da_sb[:])
             nc.sync.dma_start(out_0[j * P : (j + 1) * P, :], window[:])
 
-        def gather_a(j, dst):
-            nc.vector.tensor_copy(dst, a_pool[j][:].indirect(offsets[:]))
+        def third_product(g, t0, v2_slots_q, a_q, into):
+            v2_codes, v2_scales = v2_slots_q
+            a_codes, a_scales = a_q
+            count = len(into)
+            dx = sbuf("dx%d_%d" % (g, t0), [P, count, D], F32)
+            for n in range(count):
+                cols = slice(g * K_PASS + (t0 + n) * P, g * K_PASS + (t0 + n + 1) * P)
+                acc = banks[into[n]]
+                nc.tensor.matmul_mx(
+                    out=acc[:], lhsT=v2_codes[:, cols].bitcast(E5M2), lhsT_scale=v2_scales[:, cols],
+                    rhs=a_codes[:].bitcast(E4M3), rhs_scale=a_scales[:], start=True, stop=True,
+                )
+                nc.scalar.copy(dx[:, n, :], acc[:])
+            rows = out_1[g * K_PASS : (g + 1) * K_PASS, :].rearrange("(m t) d -> m t d", t=PACK)
+            nc.scalar.dma_start(rows[:, t0 : t0 + count, :], dx[:])
 
         dy_grouped = [sbuf("dy_grouped%d" % g, [P, K_PASS * PACK], BF16) for g in range(ROW_PASSES)]
-        group_dy(nc.scalar.copy, dy_raw0[:], 0, P, dy_grouped[0])
+        group_dy(dy_raw0, 0, P, dy_grouped[0])
         dy_q0 = quantize("dy0", dy_grouped[0][:], E5M2)
         nc.vector.tensor_copy(bt_codes[:], bt_word_pool[:].bitcast(U32).indirect(offsets[:]))
-        group_dy(nc.scalar.copy, dy_raw1a[:], 0, P // 2, dy_grouped[1])
-        group_dy(nc.scalar.copy, dy_raw1b[:], P // 2, P, dy_grouped[1])
-        a_pool = []
-
-        def load_a(j, reuses):
-            pool = sbuf("a_pool%d" % j, [P, T], F32, reuses)
-            nc.sync.dma_start(pool[:], A[j * P : (j + 1) * P, :])
-            a_pool.append(pool)
-
-        def load_x(j0, j1, reuses):
-            raw = sbuf("x_raw%d" % j0, [P, j1 - j0, R], F32, reuses)
-            nc.sync.dma_start(raw[:], xT[j0 * P : j1 * P, :].rearrange("(j p) r -> p j r", j=j1 - j0))
-            return raw
-
-        def round_x(name, raw, copy):
-            rounded = sbuf(name, [P, raw.shape[1] * R], BF16)
-            copy(rounded[:], raw[:].rearrange("p j r -> p (j r)"))
-            return rounded
-
-        x_rounded01 = round_x("x_rounded01", load_x(0, 2, None), nc.scalar.copy)
-        load_a(0, None)
-        load_a(1, "bt_word_pool")
-        v2_0, v2_1 = v2_tiles
-        first_product(0, *dy_q0, into=(2, 3, 4, 5), places=(0, 1))
+        group_dy(dy_raw1a, 0, P // 2, dy_grouped[1])
+        group_dy(dy_raw1b, P // 2, P, dy_grouped[1])
+        x_rounded0 = round_x(0, load_x(0), nc.scalar.copy)
+        x_raw1 = load_x(1)
+        a_pool0 = load_a(0)
+        a_pool1 = load_a(1, reuses="bt_word_pool")
+        first_product(0, dy_q0, into=(2, 3, 4, 5), places=(0, 1))
         dy_q1 = quantize("dy1", dy_grouped[1][:], E5M2)
-        first_product(0, *dy_q0, into=(2, 3, 4, 5), places=(2, 3))
-        x_raw2 = load_x(2, 3, "dy_raw1b")
-        load_a(2, "dy0_codes")
-        load_a(3, "dy_grouped1")
-        first_product(1, *dy_q1, into=(6, 7, 0, 1), places=range(PACK))
-        x_raw3 = load_x(3, 4, "bt_codes")
-        v2_rows0 = group_v2_rows(0, v2_0)
-        v2_rows_q = [quantize("v2_rows0", v2_rows0[:], E5M2)]
-        x_q = [turn_x(0, x_rounded01[:, 0:R], 2)]
-        v2_rows1 = group_v2_rows(1, v2_1)
+        first_product(0, dy_q0, into=(2, 3, 4, 5), places=(2, 3))
+        a_pool2 = load_a(2, reuses="dy_raw1b")
+        a_pool3 = load_a(3, reuses="dy_grouped1")
+        first_product(1, dy_q1, into=(6, 7, 0, 1), places=range(PACK))
+        x_raw2 = load_x(2, reuses="dy1_codes")
+        x_raw3 = load_x(3, reuses="bt_codes")
+
+        v2_rows_q = [quantize("v2_rows0", group_v2_rows(0)[:], E5M2)]
+        x_q0 = quantize_x(0, x_rounded0, into=2)
+        v2_rows1 = group_v2_rows(1)
         a_low = sc_all[:].bitcast(BF16)
-        gather_a(0, a_low[:, 0:SLOTS])
-        gather_a(1, a_low[:, SLOTS : 2 * SLOTS])
-        v2_rows_q.append(quantize("v2_rows1", v2_rows1[:], E5M2, None))
-        x_q.append(turn_x(1, x_rounded01[:, R : 2 * R], 3))
-        x_q.append(turn_x(2, round_x("x_rounded2", x_raw2, nc.vector.tensor_copy)[:], 4))
+        gather_a(a_pool0, a_low[:, 0:SLOTS])
+        gather_a(a_pool1, a_low[:, SLOTS : 2 * SLOTS])
+        v2_rows_q.append(quantize("v2_rows1", v2_rows1[:], E5M2))
+        x_q1 = quantize_x(1, round_x(1, x_raw1, nc.scalar.copy), into=3)
         a_high = sbuf("a_high", [P, 2 * SLOTS], BF16)
-        gather_a(2, a_high[:, 0:SLOTS])
-        gather_a(3, a_high[:, SLOTS : 2 * SLOTS])
-        for c in range(2):
-            nc.vector.memset(windows[0][:, c * T // 2 : (c + 1) * T // 2].bitcast(I32), 0)
+        gather_a(a_pool2, a_high[:, 0:SLOTS])
+        gather_a(a_pool3, a_high[:, SLOTS : 2 * SLOTS])
+        for half in range(2):
+            nc.vector.memset(windows[0][:, half * T // 2 : (half + 1) * T // 2].bitcast(I32), 0)
+
         v2_slots = sbuf("v2_slots", [P, R * PACK], BF16)
         for g, into in enumerate(((6, 7), (0, 1))):
             for h in range(2):
                 cols = slice(2 * h * K_PASS, 2 * (h + 1) * K_PASS)
-                turn_words(v2_tiles[g][:, cols], v2_slots[:, g * K_PASS * PACK :][:, cols], into[h])
-        v2_slots_codes, v2_slots_scales = quantize("v2_slots", v2_slots[:], E5M2, "dy_grouped1")
+                turn_pairs(v2_tiles[g][:, cols], v2_slots[:, g * K_PASS * PACK :][:, cols], into[h])
+        v2_slots_q = quantize("v2_slots", v2_slots[:], E5M2, reuses="dy_grouped1")
         a_slots = sbuf("a_slots", [P, D * PACK], BF16)
-        for src, j0, j1, into in ((a_low, 0, 2, 5), (a_high[:, 0:SLOTS], 2, 3, 2), (a_high[:, SLOTS:], 3, 4, 5)):
-            turn_words(src, a_slots[:, j0 * K_PASS : j1 * K_PASS], into)
-        a_codes, a_scales = quantize("a", a_slots[:], E4M3)
-        da_first = sbuf("da_first", [P, SLOTS], F32, "a_high")
-        second_product(0, x_q[0], v2_rows_q, 3, da_first[:])
-        scatter_and_store(0, da_first[:])
+        turn_pairs(a_low, a_slots[:, 0 : 2 * K_PASS], into=5)
+        turn_pairs(a_high[:, 0:SLOTS], a_slots[:, 2 * K_PASS : 3 * K_PASS], into=2)
+        turn_pairs(a_high[:, SLOTS:], a_slots[:, 3 * K_PASS : 4 * K_PASS], into=5)
+        a_q = quantize("a", a_slots[:], E4M3)
 
-        def third_product(g, t0, into):
-            count = len(into)
-            dx = sbuf("dx%d_%d" % (g, t0), [P, count, D], F32)
-            for e in range(count):
-                cols = slice(g * K_PASS + (t0 + e) * P, g * K_PASS + (t0 + e + 1) * P)
-                acc = banks[into[e]]
-                nc.tensor.matmul_mx(
-                    out=acc[:], lhsT=v2_slots_codes[:, cols].bitcast(E5M2), lhsT_scale=v2_slots_scales[:, cols],
-                    rhs=a_codes[:].bitcast(E4M3), rhs_scale=a_scales[:], start=True, stop=True,
-                )
-                nc.scalar.copy(dx[:, e, :], acc[:])
-            rows = out_1[g * K_PASS : (g + 1) * K_PASS, :].rearrange("(m t) d -> m t d", t=PACK)
-            nc.scalar.dma_start(rows[:, t0 : t0 + count, :], dx[:])
-
-        def da_block(j, into, reuses):
-            da_sb = sbuf("da_sb%d" % j, [P, SLOTS], F32, reuses)
-            second_product(j, x_q[j], v2_rows_q, into, da_sb[:])
-            scatter_and_store(j, da_sb[:])
-
-        third_product(0, 0, into=(6,))
-        third_product(0, 1, into=(7,))
-        da_block(1, 5, None)
-        third_product(0, 2, into=(0, 1))
-        x_q.append(turn_x(3, round_x("x_rounded3", x_raw3, nc.scalar.copy)[:], 3))
-        da_block(2, 6, "x_rounded3")
-        third_product(1, 0, into=(4, 2))
-        third_product(1, 2, into=(7, 0))
-        da_block(3, 1, None)
+        second_product(0, x_q0, v2_rows_q, into=3, reuses="a_high")
+        third_product(0, 0, v2_slots_q, a_q, into=(6,))
+        third_product(0, 1, v2_slots_q, a_q, into=(7,))
+        x_q2 = quantize_x(2, round_x(2, x_raw2, nc.scalar.copy), into=4)
+        second_product(1, x_q1, v2_rows_q, into=5, reuses="x_rounded2")
+        third_product(0, 2, v2_slots_q, a_q, into=(0, 1))
+        x_q3 = quantize_x(3, round_x(3, x_raw3, nc.vector.tensor_copy), into=3)
+        second_product(2, x_q2, v2_rows_q, into=6, reuses="x_rounded3")
+        third_product(1, 0, v2_slots_q, a_q, into=(4, 2))
+        third_product(1, 2, v2_slots_q, a_q, into=(7, 0))
+        second_product(3, x_q3, v2_rows_q, into=1)

@@ -32,6 +32,7 @@ def tile_attend_glora_ax_kernel(
     nc = tc.nc
     with ExitStack() as ctx:
         keep = ctx.enter_context(tc.tile_pool(name="keep", bufs=1))
+        placed = ctx.enter_context(tc.tile_pool(name="placed", bufs=1))
         psum = ctx.enter_context(tc.psum_pool(name="psum", bufs=1))
         banks = [psum.tile([P, K_PASS], F32, name="bank%d" % n) for n in range(BANKS)]
 
@@ -39,6 +40,8 @@ def tile_attend_glora_ax_kernel(
             return bank[:].rearrange("p (c m) -> p c m", c=PACK)
 
         def sbuf(name, shape, dtype, reuses=None):
+            if isinstance(reuses, int):
+                return placed.tile(shape, dtype, name=name, align_bytes=64, offset=reuses)
             return keep.tile(shape, dtype, name=name, tag=reuses or name, align_bytes=64)
 
         def quantize(name, grouped, fmt, reuses=None):
@@ -50,70 +53,101 @@ def tile_attend_glora_ax_kernel(
 
         offsets = keep.tile([P, SLOTS // LIST_ROWS], U16, name="offsets")
         nc.sync.dma_start(offsets[:], offs)
-
-        sc_pool = sbuf("sc_pool", [P, T], F32)
-        nc.vector.memset(sc_pool[0 : P - 1, :].bitcast(I32), 0)
-        nc.scalar.dma_start(sc_pool[P - 1 : P, :], sc[P - 1 : P, :])
-
         bt_scale_pool = sbuf("bt_scale_pool", [P, T], U8)
         for q in range(P // QUADRANT):
             rows = Bt_scales[0, PACK * q : PACK * (q + 1), :].bitcast(I32)
-            queue = nc.scalar if q < 2 else nc.sync
-            queue.dma_start(
+            nc.scalar.dma_start(
                 bt_scale_pool[QUADRANT * q : QUADRANT * (q + 1), :].bitcast(I32),
                 rows.unsqueeze(0).broadcast_to([QUADRANT // PACK, PACK, T // 4]),
             )
-
-        def load_dy(name, r0, r1):
-            raw = sbuf(name, [P, PACK, r1 - r0], F32)
-            nc.sync.dma_start(raw[:], dyT[:, r0:r1].rearrange("(p j) r -> p j r", j=PACK))
-            return raw
-
-        dy_raw0 = load_dy("dy_raw0", 0, K_PASS)
-        dy_raw1a = load_dy("dy_raw1a", K_PASS, K_PASS + K_PASS // 2)
-        bt_word_pool = sbuf("bt_word_pool", [P, T], I32)
-        nc.sync.dma_start(bt_word_pool[:], Bt_words[0].rearrange("p n t -> p (n t)").bitcast(I32))
         us_tile = sbuf("us_tile", [P, ROW_PASSES, 2 * PACK], F32)
         us_cols = us_tile[:, :, 0:PACK]
         wt_tile = sbuf("wt_tile", [P, ROW_PASSES, 2 * PACK], F32)
         wt_cols = wt_tile[:, :, 0:PACK]
         nc.scalar.dma_start(us_cols, us.rearrange("(g p t) o -> p g (t o)", g=ROW_PASSES, t=PACK))
         nc.scalar.dma_start(wt_cols, wt.rearrange("(g p t) o -> p g (t o)", g=ROW_PASSES, t=PACK))
+
+        sc_pool = sbuf("sc_pool", [P, T], F32)
+        nc.vector.memset(sc_pool[0 : P - 1, :].bitcast(I32), 0)
+        nc.sync.dma_start(sc_pool[P - 1 : P, :], sc[P - 1 : P, :])
+        bt_word_pool = sbuf("bt_word_pool", [P, T], I32)
+        nc.sync.dma_start(bt_word_pool[:], Bt_words[0].rearrange("p n t -> p (n t)").bitcast(I32))
+
+        def load_dy(name, r0, r1):
+            raw = sbuf(name, [P, PACK, r1 - r0], F32)
+            nc.sync.dma_start(raw[:], dyT[:, r0:r1].rearrange("(p j) r -> p j r", j=PACK))
+            return raw
+
+        def load_x(j, reuses=None):
+            raw = sbuf("x_raw%d" % j, [P, R], F32, reuses)
+            nc.sync.dma_start(raw[:], xT[j * P : (j + 1) * P, :])
+            return raw
+
+        def load_a(j, reuses=None):
+            pool = sbuf("a_pool%d" % j, [P, T], F32, reuses)
+            nc.sync.dma_start(pool[:], A[j * P : (j + 1) * P, :])
+            return pool
+
+        dy_raw0 = load_dy("dy_raw0", 0, K_PASS)
+        dy_raw1a = load_dy("dy_raw1a", K_PASS, K_PASS + K_PASS // 2)
         dy_raw1b = load_dy("dy_raw1b", K_PASS + K_PASS // 2, R)
+        x_raw0 = load_x(0)
+        a_pool0 = load_a(0)
+        x_raw1 = load_x(1)
+        a_pool1 = load_a(1)
+        a_pool2 = load_a(2)
+        a_pool3 = load_a(3, reuses=0)
+        x_raw2 = load_x(2)
+        x_raw3 = load_x(3)
 
         ident = sbuf("ident", [P, P], F32)
         make_identity(nc, ident[:])
-        windows = [sbuf("window%d" % n, [P, T], F32) for n in range(WINDOWS)]
-        for window in windows[1:]:
+
+        def zeroed_window(n, reuses=None):
+            window = sbuf("window%d" % n, [P, T], F32, reuses)
             nc.gpsimd.memset(window[:], 0.0)
+            return window
+
+        windows = [zeroed_window(0)]
 
         sc_row = sbuf("sc_row", [P, SLOTS], F32)
         nc.vector.tensor_copy(sc_row[:], sc_pool[:].indirect(offsets[:]))
         sc_turned = quarters(banks[0])
-        for c in range(PACK):
-            nc.tensor.transpose(sc_turned[:, c, :], sc_row[:, c * P : (c + 1) * P], ident[:])
+        for t in range(PACK):
+            nc.tensor.transpose(sc_turned[:, t, :], sc_row[:, t:SLOTS:PACK], ident[:])
         sc_cols = sbuf("sc_cols", [P, PACK], F32)
         nc.scalar.copy(sc_cols[:], sc_turned[:, :, P - 1])
-        sc_spread = quarters(banks[1])
-        for c in range(PACK):
-            nc.tensor.transpose(sc_spread[:, c, :], sc_cols[:, c : c + 1].to_broadcast([P, P]), ident[:])
-        sc_all = sbuf("sc_all", [P, SLOTS], F32)
-        nc.scalar.copy(sc_all[:], banks[1][:])
 
-        bt_scales = sbuf("bt_scales", [P, SLOTS], U8, reuses="sc_pool")
-        nc.vector.tensor_copy(bt_scales[:], bt_scale_pool[:].indirect(offsets[:]))
+        bt_scales_listed = sbuf("bt_scales_listed", [P, SLOTS], U8, reuses="sc_pool")
+        nc.vector.tensor_copy(bt_scales_listed[:], bt_scale_pool[:].indirect(offsets[:]))
         bt_codes = sbuf("bt_codes", [P, SLOTS], U32)
+        nc.vector.tensor_copy(
+            bt_codes[:].rearrange("p (t m) -> p m t", t=PACK), bt_word_pool[:].bitcast(U32).indirect(offsets[:])
+        )
+        bt_scales = sbuf("bt_scales", [P, SLOTS], U8)
+        nc.vector.tensor_copy(
+            bt_scales[:].rearrange("p (t m) -> p t m", t=PACK),
+            bt_scales_listed[:].rearrange("p (m t) -> p t m", t=PACK),
+        )
 
-        row_factor = sbuf("row_factor", [P, ROW_PASSES, PACK], F32)
-        nc.gpsimd.tensor_tensor(row_factor[:], us_cols, wt_cols, MULT)
+        factor_cols = sbuf("factor_cols", [P, ROW_PASSES, PACK], F32)
+        nc.gpsimd.tensor_tensor(factor_cols[:], us_cols, wt_cols, MULT)
+        row_factor = []
+        for g in range(ROW_PASSES):
+            spread = quarters(banks[1 + g])
+            for t in range(PACK):
+                nc.tensor.transpose(spread[:, t, :], factor_cols[:, g, t : t + 1].to_broadcast([P, P]), ident[:])
+            factor = sbuf("row_factor%d" % g, [P, K_PASS], F32)
+            nc.scalar.copy(factor[:].rearrange("p (m t) -> p m t", t=PACK), spread.rearrange("p t m -> p m t"))
+            row_factor.append(factor)
 
-        def group_dy(raw, m0, m1, grouped):
-            nc.scalar.copy(
-                grouped[:].rearrange("p (t m j) -> p m t j", t=PACK, j=PACK)[:, m0:m1],
-                raw[:].rearrange("p j (m t) -> p m t j", t=PACK),
+        def group_dy(raw, c0, c1, grouped, r0, copy):
+            copy(
+                grouped[:, PACK * (r0 + c0) : PACK * (r0 + c1)].rearrange("p (c n j) -> p c j n", n=4, j=PACK),
+                raw[:, :, c0:c1].rearrange("p j (c n) -> p c j n", n=4),
             )
 
-        v2_tiles = [sbuf("v2_%d" % g, [P, PACK * SLOTS], BF16) for g in range(ROW_PASSES)]
+        v2_tiles = [sbuf("v2_%d" % g, [P, PACK * K_PASS], BF16) for g in range(ROW_PASSES)]
 
         def first_product(g, dy_q, into, places):
             dy_codes, dy_scales = dy_q
@@ -121,21 +155,20 @@ def tile_attend_glora_ax_kernel(
                 v = banks[into[t]]
                 cols = slice(t * P, (t + 1) * P)
                 nc.tensor.matmul_mx(
-                    out=v[:], lhsT=dy_codes[:, cols].bitcast(E5M2), lhsT_scale=dy_scales[:, cols],
-                    rhs=bt_codes[:].bitcast(E4M3), rhs_scale=bt_scales[:], start=True, stop=True,
+                    out=v[:], lhsT=bt_codes[:, cols].bitcast(E4M3), lhsT_scale=bt_scales[:, cols],
+                    rhs=dy_codes[:].bitcast(E5M2), rhs_scale=dy_scales[:], start=True, stop=True,
                 )
                 nc.vector.scalar_tensor_tensor(
-                    v2_tiles[g][:, t * SLOTS : (t + 1) * SLOTS], v[:], row_factor[:, g, t : t + 1], sc_all[:],
+                    v2_tiles[g][:, t * K_PASS : (t + 1) * K_PASS], v[:], sc_cols[:, t : t + 1], row_factor[g][:],
                     MULT, MULT,
                 )
 
-        def group_v2_rows(g):
-            grouped = sbuf("v2_rows%d" % g, [P, SLOTS * PACK], BF16)
+        def group_v2_slots(g, h, grouped):
+            rows = slice(h * K_PASS // 2, (h + 1) * K_PASS // 2)
             nc.scalar.copy(
-                grouped[:].rearrange("p (c n t) -> p c t n", n=4, t=PACK),
-                v2_tiles[g][:].rearrange("p (t c n) -> p c t n", n=4, t=PACK),
+                grouped[:].rearrange("p (r t) -> p r t", t=PACK)[:, rows].rearrange("p (c n) t -> p c t n", n=4),
+                v2_tiles[g][:].rearrange("p (t r) -> p t r", t=PACK)[:, :, rows].rearrange("p t (c n) -> p c t n", n=4),
             )
-            return grouped
 
         def turn_pairs(src, grouped, into):
             stretches = src.shape[1] // K_PASS
@@ -149,25 +182,23 @@ def tile_attend_glora_ax_kernel(
                 bank.rearrange("p b u m -> p b m u"),
             )
 
-        def load_x(j, reuses=None):
-            raw = sbuf("x_raw%d" % j, [P, R], F32, reuses)
-            nc.sync.dma_start(raw[:], xT[j * P : (j + 1) * P, :])
-            return raw
 
-        def round_x(j, raw, copy):
-            rounded = sbuf("x_rounded%d" % j, [P, R], BF16)
-            copy(rounded[:], raw[:])
+        def round_x(j, raw, reuses=None):
+            rounded = sbuf("x_rounded%d" % j, [P, R], BF16, reuses)
+            nc.scalar.copy(rounded[:], raw[:])
             return rounded
 
-        def quantize_x(j, rounded, into):
+        def group_x(j, rounded, into):
             grouped = sbuf("x_grouped%d" % j, [P, ROW_PASSES * K_PASS], BF16)
             turn_pairs(rounded[:], grouped[:], into)
-            return quantize("x%d" % j, grouped[:], E4M3)
+            return grouped
 
-        def load_a(j, reuses=None):
-            pool = sbuf("a_pool%d" % j, [P, T], F32, reuses)
-            nc.sync.dma_start(pool[:], A[j * P : (j + 1) * P, :])
-            return pool
+        def group_v2_rows(g, into):
+            grouped = sbuf("v2_rows%d" % g, [P, SLOTS * PACK], BF16)
+            for h in range(2):
+                cols = slice(2 * h * K_PASS, 2 * (h + 1) * K_PASS)
+                turn_pairs(v2_tiles[g][:, cols], grouped[:, cols], into[h])
+            return grouped
 
         def gather_a(pool, listed):
             nc.vector.tensor_copy(listed, pool[:].indirect(offsets[:]))
@@ -184,80 +215,77 @@ def tile_attend_glora_ax_kernel(
                     rhs=v2_codes[:].bitcast(E5M2), rhs_scale=v2_scales[:],
                     start=(g == 0), stop=(g == ROW_PASSES - 1),
                 )
-            nc.scalar.copy(da_sb[:], da[:])
+            nc.scalar.copy(da_sb[:].rearrange("p (m t) -> p m t", t=PACK), quarters(da).rearrange("p t m -> p m t"))
+            return da_sb
+
+        def scatter(j, da_sb):
             window = windows[j % WINDOWS]
             nc.vector.tensor_copy(window[:].indirect(offsets[:]), da_sb[:])
             nc.sync.dma_start(out_0[j * P : (j + 1) * P, :], window[:])
 
-        def third_product(g, t0, v2_slots_q, a_q, into):
-            v2_codes, v2_scales = v2_slots_q
+        def third_product(c0, v2_slots_q, a_q, into):
+            v2_codes, v2_scales = v2_slots_q[c0 // PACK]
             a_codes, a_scales = a_q
             count = len(into)
-            dx = sbuf("dx%d_%d" % (g, t0), [P, count, D], F32)
+            dx = sbuf("dx%d" % c0, [P, count, D], F32)
             for n in range(count):
-                cols = slice(g * K_PASS + (t0 + n) * P, g * K_PASS + (t0 + n + 1) * P)
+                cols = slice((c0 % PACK + n) * P, (c0 % PACK + n + 1) * P)
                 acc = banks[into[n]]
                 nc.tensor.matmul_mx(
                     out=acc[:], lhsT=v2_codes[:, cols].bitcast(E5M2), lhsT_scale=v2_scales[:, cols],
                     rhs=a_codes[:].bitcast(E4M3), rhs_scale=a_scales[:], start=True, stop=True,
                 )
                 nc.scalar.copy(dx[:, n, :], acc[:])
-            rows = out_1[g * K_PASS : (g + 1) * K_PASS, :].rearrange("(m t) d -> m t d", t=PACK)
-            nc.scalar.dma_start(rows[:, t0 : t0 + count, :], dx[:])
+            rows = out_1[c0 * P : (c0 + count) * P, :].rearrange("(n m) d -> m n d", m=P)
+            nc.scalar.dma_start(rows, dx[:])
 
         dy_grouped = [sbuf("dy_grouped%d" % g, [P, K_PASS * PACK], BF16) for g in range(ROW_PASSES)]
-        group_dy(dy_raw0, 0, P, dy_grouped[0])
+        group_dy(dy_raw0, 0, 192, dy_grouped[0], 0, nc.scalar.copy)
+        group_dy(dy_raw0, 192, K_PASS, dy_grouped[0], 0, nc.vector.tensor_copy)
         dy_q0 = quantize("dy0", dy_grouped[0][:], E5M2)
-        nc.vector.tensor_copy(bt_codes[:], bt_word_pool[:].bitcast(U32).indirect(offsets[:]))
-        group_dy(dy_raw1a, 0, P // 2, dy_grouped[1])
-        group_dy(dy_raw1b, P // 2, P, dy_grouped[1])
-        x_rounded0 = round_x(0, load_x(0), nc.scalar.copy)
-        x_raw1 = load_x(1)
-        a_pool0 = load_a(0)
-        a_pool1 = load_a(1, reuses="bt_word_pool")
-        first_product(0, dy_q0, into=(2, 3, 4, 5), places=(0, 1))
+        windows.append(zeroed_window(1, reuses="dy_grouped0"))
+        group_dy(dy_raw1a, 0, K_PASS // 2, dy_grouped[1], 0, nc.scalar.copy)
+        group_dy(dy_raw1b, 0, K_PASS // 2, dy_grouped[1], K_PASS // 2, nc.scalar.copy)
+        first_product(0, dy_q0, into=(3, 4, 5, 6), places=range(PACK))
         dy_q1 = quantize("dy1", dy_grouped[1][:], E5M2)
-        first_product(0, dy_q0, into=(2, 3, 4, 5), places=(2, 3))
-        a_pool2 = load_a(2, reuses="dy_raw1b")
-        a_pool3 = load_a(3, reuses="dy_grouped1")
-        first_product(1, dy_q1, into=(6, 7, 0, 1), places=range(PACK))
-        x_raw2 = load_x(2, reuses="dy1_codes")
-        x_raw3 = load_x(3, reuses="bt_codes")
-
-        v2_rows_q = [quantize("v2_rows0", group_v2_rows(0)[:], E5M2)]
-        x_q0 = quantize_x(0, x_rounded0, into=2)
-        v2_rows1 = group_v2_rows(1)
-        a_low = sc_all[:].bitcast(BF16)
-        gather_a(a_pool0, a_low[:, 0:SLOTS])
-        gather_a(a_pool1, a_low[:, SLOTS : 2 * SLOTS])
+        windows.append(zeroed_window(2, reuses="dy_grouped1"))
+        first_product(1, dy_q1, into=(7, 0, 1, 2), places=range(PACK))
+        v2_rows0 = group_v2_rows(0, into=(3, 5))
+        x_grouped0 = group_x(0, round_x(0, x_raw0), into=4)
+        v2_slots = [sbuf("v2_slots0", [P, K_PASS * PACK], BF16)]
+        v2_rows1 = group_v2_rows(1, into=(7, 1))
+        group_v2_slots(0, 0, v2_slots[0])
+        group_v2_slots(0, 1, v2_slots[0])
+        v2_rows_q = [quantize("v2_rows0", v2_rows0[:], E5M2)]
+        x_q0 = quantize("x0", x_grouped0[:], E4M3)
         v2_rows_q.append(quantize("v2_rows1", v2_rows1[:], E5M2))
-        x_q1 = quantize_x(1, round_x(1, x_raw1, nc.scalar.copy), into=3)
-        a_high = sbuf("a_high", [P, 2 * SLOTS], BF16)
+        a_low = sbuf("a_low", [P, 2 * SLOTS], BF16)
+        a_high = sbuf("a_high", [P, 2 * SLOTS], BF16, reuses=10176)
+        gather_a(a_pool0, a_low[:, 0:SLOTS])
+        gather_a(a_pool1, a_low[:, SLOTS:])
         gather_a(a_pool2, a_high[:, 0:SLOTS])
-        gather_a(a_pool3, a_high[:, SLOTS : 2 * SLOTS])
-        for half in range(2):
-            nc.vector.memset(windows[0][:, half * T // 2 : (half + 1) * T // 2].bitcast(I32), 0)
-
-        v2_slots = sbuf("v2_slots", [P, R * PACK], BF16)
-        for g, into in enumerate(((6, 7), (0, 1))):
-            for h in range(2):
-                cols = slice(2 * h * K_PASS, 2 * (h + 1) * K_PASS)
-                turn_pairs(v2_tiles[g][:, cols], v2_slots[:, g * K_PASS * PACK :][:, cols], into[h])
-        v2_slots_q = quantize("v2_slots", v2_slots[:], E5M2, reuses="dy_grouped1")
+        gather_a(a_pool3, a_high[:, SLOTS:])
         a_slots = sbuf("a_slots", [P, D * PACK], BF16)
-        turn_pairs(a_low, a_slots[:, 0 : 2 * K_PASS], into=5)
-        turn_pairs(a_high[:, 0:SLOTS], a_slots[:, 2 * K_PASS : 3 * K_PASS], into=2)
-        turn_pairs(a_high[:, SLOTS:], a_slots[:, 3 * K_PASS : 4 * K_PASS], into=5)
+        turn_pairs(a_high[:, SLOTS:], a_slots[:, 3 * K_PASS :], into=7)
+        x_grouped1 = group_x(1, round_x(1, x_raw1, reuses="x_grouped0"), into=0)
+        turn_pairs(a_high[:, 0:SLOTS], a_slots[:, 2 * K_PASS : 3 * K_PASS], into=5)
+        turn_pairs(a_low[:], a_slots[:, 0 : 2 * K_PASS], into=3)
+        v2_slots.append(sbuf("v2_slots1", [P, K_PASS * PACK], BF16, reuses="x_raw1"))
+        group_v2_slots(1, 0, v2_slots[1])
+        group_v2_slots(1, 1, v2_slots[1])
+        x_q1 = quantize("x1", x_grouped1[:], E4M3, reuses=4096)
+        v2_slots_q = [quantize("v2_slots0", v2_slots[0][:], E5M2, reuses=0)]
+        v2_slots_q.append(quantize("v2_slots1", v2_slots[1][:], E5M2, reuses=2048))
         a_q = quantize("a", a_slots[:], E4M3)
-
-        second_product(0, x_q0, v2_rows_q, into=3, reuses="a_high")
-        third_product(0, 0, v2_slots_q, a_q, into=(6,))
-        third_product(0, 1, v2_slots_q, a_q, into=(7,))
-        x_q2 = quantize_x(2, round_x(2, x_raw2, nc.scalar.copy), into=4)
-        second_product(1, x_q1, v2_rows_q, into=5, reuses="x_rounded2")
-        third_product(0, 2, v2_slots_q, a_q, into=(0, 1))
-        x_q3 = quantize_x(3, round_x(3, x_raw3, nc.vector.tensor_copy), into=3)
-        second_product(2, x_q2, v2_rows_q, into=6, reuses="x_rounded3")
-        third_product(1, 0, v2_slots_q, a_q, into=(4, 2))
-        third_product(1, 2, v2_slots_q, a_q, into=(7, 0))
-        second_product(3, x_q3, v2_rows_q, into=1)
+        scatter(0, second_product(0, x_q0, v2_rows_q, into=6, reuses=8192))
+        x_q2 = quantize("x2", group_x(2, round_x(2, x_raw2, reuses=10176 + 1984), into=4)[:], E4M3)
+        scatter(1, second_product(1, x_q1, v2_rows_q, into=2, reuses=10176 + 3968))
+        third_product(0, v2_slots_q, a_q, into=(5,))
+        third_product(1, v2_slots_q, a_q, into=(7,))
+        x_q3 = quantize("x3", group_x(3, round_x(3, x_raw3, reuses=10176 + 64), into=1)[:], E4M3)
+        scatter(2, second_product(2, x_q2, v2_rows_q, into=0, reuses=10176 + 64))
+        third_product(2, v2_slots_q, a_q, into=(4, 2))
+        third_product(4, v2_slots_q, a_q, into=(1, 0))
+        da3 = second_product(3, x_q3, v2_rows_q, into=3)
+        third_product(6, v2_slots_q, a_q, into=(4, 2))
+        scatter(3, da3)

@@ -15,6 +15,7 @@ U8 = mybir.dt.uint8
 E4M3 = mybir.dt.float8_e4m3fn_x4
 E5M2 = mybir.dt.float8_e5m2_x4
 MULT = mybir.AluOpType.mult
+ADD = mybir.AluOpType.add
 
 P = 128
 PACK = 4
@@ -92,12 +93,12 @@ def tile_attend_glora_ax_kernel(
         dy_raw1a = load_dy("dy_raw1a", K_PASS, K_PASS + K_PASS // 2)
         dy_raw1b = load_dy("dy_raw1b", K_PASS + K_PASS // 2, R)
         x_raw0 = load_x(0)
-        a_pool0 = load_a(0)
+        a_pool0 = load_a(0, reuses=16384)
         x_raw1 = load_x(1)
+        x_raw2 = load_x(2)
         a_pool1 = load_a(1)
         a_pool2 = load_a(2)
         a_pool3 = load_a(3, reuses=0)
-        x_raw2 = load_x(2)
         x_raw3 = load_x(3)
 
         ident = sbuf("ident", [P, P], F32)
@@ -109,6 +110,8 @@ def tile_attend_glora_ax_kernel(
             return window
 
         windows = [zeroed_window(0)]
+        last_window = sbuf("window2", [P, T], F32)
+        nc.vector.memset(last_window[:].bitcast(I32), 0)
 
         sc_row = sbuf("sc_row", [P, SLOTS], F32)
         nc.vector.tensor_copy(sc_row[:], sc_pool[:].indirect(offsets[:]))
@@ -183,9 +186,12 @@ def tile_attend_glora_ax_kernel(
             )
 
 
-        def round_x(j, raw, reuses=None):
+        def round_x(j, raw, reuses=None, on_gpsimd=False):
             rounded = sbuf("x_rounded%d" % j, [P, R], BF16, reuses)
-            nc.scalar.copy(rounded[:], raw[:])
+            if on_gpsimd:
+                nc.gpsimd.tensor_scalar(rounded[:], raw[:], 1.0, 0.0, MULT, ADD)
+            else:
+                nc.scalar.copy(rounded[:], raw[:])
             return rounded
 
         def group_x(j, rounded, into):
@@ -203,18 +209,21 @@ def tile_attend_glora_ax_kernel(
         def gather_a(pool, listed):
             nc.vector.tensor_copy(listed, pool[:].indirect(offsets[:]))
 
-        def second_product(j, x_q, v2_rows_q, into, reuses=None):
-            da_sb = sbuf("da_sb%d" % j, [P, SLOTS], F32, reuses)
+        def second_product(x_q, v2_rows_q, into, first=0):
             x_codes, x_scales = x_q
             da = banks[into]
             for g in range(ROW_PASSES):
-                cols = slice(g * P, (g + 1) * P)
+                cols = slice(first + g * P, first + (g + 1) * P)
                 v2_codes, v2_scales = v2_rows_q[g]
                 nc.tensor.matmul_mx(
                     out=da[:], lhsT=x_codes[:, cols].bitcast(E4M3), lhsT_scale=x_scales[:, cols],
                     rhs=v2_codes[:].bitcast(E5M2), rhs_scale=v2_scales[:],
                     start=(g == 0), stop=(g == ROW_PASSES - 1),
                 )
+            return da
+
+        def fetch(j, da, reuses=None):
+            da_sb = sbuf("da_sb%d" % j, [P, SLOTS], F32, reuses)
             nc.scalar.copy(da_sb[:].rearrange("p (m t) -> p m t", t=PACK), quarters(da).rearrange("p t m -> p m t"))
             return da_sb
 
@@ -223,11 +232,10 @@ def tile_attend_glora_ax_kernel(
             nc.vector.tensor_copy(window[:].indirect(offsets[:]), da_sb[:])
             nc.sync.dma_start(out_0[j * P : (j + 1) * P, :], window[:])
 
-        def third_product(c0, v2_slots_q, a_q, into):
+        def third_product(c0, v2_slots_q, a_q, into, dx):
             v2_codes, v2_scales = v2_slots_q[c0 // PACK]
             a_codes, a_scales = a_q
             count = len(into)
-            dx = sbuf("dx%d" % c0, [P, count, D], F32)
             for n in range(count):
                 cols = slice((c0 % PACK + n) * P, (c0 % PACK + n + 1) * P)
                 acc = banks[into[n]]
@@ -237,7 +245,7 @@ def tile_attend_glora_ax_kernel(
                 )
                 nc.scalar.copy(dx[:, n, :], acc[:])
             rows = out_1[c0 * P : (c0 + count) * P, :].rearrange("(n m) d -> m n d", m=P)
-            nc.scalar.dma_start(rows, dx[:])
+            nc.scalar.dma_start(rows, dx)
 
         dy_grouped = [sbuf("dy_grouped%d" % g, [P, K_PASS * PACK], BF16) for g in range(ROW_PASSES)]
         group_dy(dy_raw0, 0, 192, dy_grouped[0], 0, nc.scalar.copy)
@@ -248,7 +256,11 @@ def tile_attend_glora_ax_kernel(
         group_dy(dy_raw1b, 0, K_PASS // 2, dy_grouped[1], K_PASS // 2, nc.scalar.copy)
         first_product(0, dy_q0, into=(3, 4, 5, 6), places=range(PACK))
         dy_q1 = quantize("dy1", dy_grouped[1][:], E5M2)
-        windows.append(zeroed_window(2, reuses="dy_grouped1"))
+        windows.append(last_window)
+        a_low = sbuf("a_low", [P, 2 * SLOTS], BF16)
+        gather_a(a_pool0, a_low[:, 0:SLOTS])
+        x_rounded1 = round_x(1, x_raw1, reuses=16384, on_gpsimd=True)
+        x_rounded2 = round_x(2, x_raw2, reuses=16384 + 2048, on_gpsimd=True)
         first_product(1, dy_q1, into=(7, 0, 1, 2), places=range(PACK))
         v2_rows0 = group_v2_rows(0, into=(3, 5))
         x_grouped0 = group_x(0, round_x(0, x_raw0), into=4)
@@ -259,33 +271,34 @@ def tile_attend_glora_ax_kernel(
         v2_rows_q = [quantize("v2_rows0", v2_rows0[:], E5M2)]
         x_q0 = quantize("x0", x_grouped0[:], E4M3)
         v2_rows_q.append(quantize("v2_rows1", v2_rows1[:], E5M2))
-        a_low = sbuf("a_low", [P, 2 * SLOTS], BF16)
+        v2_slots_q = [quantize("v2_slots0", v2_slots[0][:], E5M2, reuses="v2_rows0")]
         a_high = sbuf("a_high", [P, 2 * SLOTS], BF16, reuses=10176)
-        gather_a(a_pool0, a_low[:, 0:SLOTS])
         gather_a(a_pool1, a_low[:, SLOTS:])
         gather_a(a_pool2, a_high[:, 0:SLOTS])
         gather_a(a_pool3, a_high[:, SLOTS:])
         a_slots = sbuf("a_slots", [P, D * PACK], BF16)
         turn_pairs(a_high[:, SLOTS:], a_slots[:, 3 * K_PASS :], into=7)
-        x_grouped1 = group_x(1, round_x(1, x_raw1, reuses="x_grouped0"), into=0)
-        turn_pairs(a_high[:, 0:SLOTS], a_slots[:, 2 * K_PASS : 3 * K_PASS], into=5)
-        turn_pairs(a_low[:], a_slots[:, 0 : 2 * K_PASS], into=3)
-        v2_slots.append(sbuf("v2_slots1", [P, K_PASS * PACK], BF16, reuses="x_raw1"))
+        x_grouped12 = sbuf("x_grouped12", [P, 2 * R], BF16)
+        turn_pairs(x_rounded1[:], x_grouped12[:, 0:R], into=0)
+        turn_pairs(x_rounded2[:], x_grouped12[:, R:], into=4)
+        v2_slots.append(sbuf("v2_slots1", [P, K_PASS * PACK], BF16, reuses="x_grouped0"))
         group_v2_slots(1, 0, v2_slots[1])
         group_v2_slots(1, 1, v2_slots[1])
-        x_q1 = quantize("x1", x_grouped1[:], E4M3, reuses=4096)
-        v2_slots_q = [quantize("v2_slots0", v2_slots[0][:], E5M2, reuses=0)]
+        turn_pairs(a_high[:, 0:SLOTS], a_slots[:, 2 * K_PASS : 3 * K_PASS], into=5)
+        turn_pairs(a_low[:], a_slots[:, 0 : 2 * K_PASS], into=3)
+        x_q12 = quantize("x12", x_grouped12[:], E4M3, reuses=4096)
         v2_slots_q.append(quantize("v2_slots1", v2_slots[1][:], E5M2, reuses=2048))
         a_q = quantize("a", a_slots[:], E4M3)
-        scatter(0, second_product(0, x_q0, v2_rows_q, into=6, reuses=8192))
-        x_q2 = quantize("x2", group_x(2, round_x(2, x_raw2, reuses=10176 + 1984), into=4)[:], E4M3)
-        scatter(1, second_product(1, x_q1, v2_rows_q, into=2, reuses=10176 + 3968))
-        third_product(0, v2_slots_q, a_q, into=(5,))
-        third_product(1, v2_slots_q, a_q, into=(7,))
-        x_q3 = quantize("x3", group_x(3, round_x(3, x_raw3, reuses=10176 + 64), into=1)[:], E4M3)
-        scatter(2, second_product(2, x_q2, v2_rows_q, into=0, reuses=10176 + 64))
-        third_product(2, v2_slots_q, a_q, into=(4, 2))
-        third_product(4, v2_slots_q, a_q, into=(1, 0))
-        da3 = second_product(3, x_q3, v2_rows_q, into=3)
-        third_product(6, v2_slots_q, a_q, into=(4, 2))
-        scatter(3, da3)
+        scatter(0, fetch(0, second_product(x_q0, v2_rows_q, into=6), reuses=8192))
+        da1 = second_product(x_q12, v2_rows_q, into=2)
+        da2 = second_product(x_q12, v2_rows_q, into=0, first=2 * P)
+        dx = sbuf("dx", [P, 8, D], F32)
+        third_product(0, v2_slots_q, a_q, (5,), dx[:, 0:1])
+        third_product(1, v2_slots_q, a_q, (7,), dx[:, 1:2])
+        scatter(1, fetch(1, da1, reuses="a_slots"))
+        third_product(2, v2_slots_q, a_q, (3, 4), dx[:, 2:4])
+        x_q3 = quantize("x3", group_x(3, round_x(3, x_raw3, reuses=10176 + 1984), into=1)[:], E4M3, reuses=8192)
+        scatter(2, fetch(2, da2, reuses=10176 + 1984))
+        third_product(4, v2_slots_q, a_q, (6, 5), dx[:, 4:6])
+        third_product(6, v2_slots_q, a_q, (7, 3), dx[:, 6:8])
+        scatter(3, fetch(3, second_product(x_q3, v2_rows_q, into=2)))

@@ -45,10 +45,10 @@ def tile_attend_glora_ax_kernel(
                 return placed.tile(shape, dtype, name=name, align_bytes=64, offset=reuses)
             return keep.tile(shape, dtype, name=name, tag=reuses or name, align_bytes=64)
 
-        def quantize(name, grouped, fmt, reuses=None):
+        def quantize(name, grouped, fmt, reuses=None, scales_reuse=None):
             width = grouped.shape[1] // PACK
             codes = sbuf(name + "_codes", [P, width], U32, reuses)
-            scales = sbuf(name + "_scales", [P, width], U8)
+            scales = sbuf(name + "_scales", [P, width], U8, scales_reuse)
             nc.vector.quantize_mx(out=codes[:].bitcast(fmt), scales=scales[:], in_=grouped)
             return codes, scales
 
@@ -291,14 +291,14 @@ def tile_attend_glora_ax_kernel(
         a_q = quantize("a", a_slots[:], E4M3)
         scatter(0, fetch(0, second_product(x_q0, v2_rows_q, into=6), reuses=8192))
         da1 = second_product(x_q12, v2_rows_q, into=2)
-        da2 = second_product(x_q12, v2_rows_q, into=0, first=2 * P)
+        x_rounded3 = round_x(3, x_raw3, reuses=10176 + 1984)
         dx = sbuf("dx", [P, 8, D], F32)
         third_product(0, v2_slots_q, a_q, (5,), dx[:, 0:1])
         third_product(1, v2_slots_q, a_q, (7,), dx[:, 1:2])
         scatter(1, fetch(1, da1, reuses="a_slots"))
         third_product(2, v2_slots_q, a_q, (3, 4), dx[:, 2:4])
-        x_q3 = quantize("x3", group_x(3, round_x(3, x_raw3, reuses=10176 + 1984), into=1)[:], E4M3, reuses=8192)
-        scatter(2, fetch(2, da2, reuses=10176 + 1984))
-        third_product(4, v2_slots_q, a_q, (6, 5), dx[:, 4:6])
-        third_product(6, v2_slots_q, a_q, (7, 3), dx[:, 6:8])
-        scatter(3, fetch(3, second_product(x_q3, v2_rows_q, into=2)))
+        third_product(4, v2_slots_q, a_q, (6,), dx[:, 4:5])
+        x_q3 = quantize("x3", group_x(3, x_rounded3, into=1)[:], E4M3, reuses=8192)
+        scatter(2, fetch(2, second_product(x_q12, v2_rows_q, into=5, first=2 * P), reuses=10176 + 1984))
+        third_product(5, v2_slots_q, a_q, (0, 7, 3), dx[:, 5:8])
+        scatter(3, fetch(3, second_product(x_q3, v2_rows_q, into=7)))

@@ -23,8 +23,22 @@ K_PASS = P * PACK
 ROW_PASSES = R // K_PASS
 BANKS = 8
 QUADRANT = 32
+SCALE_ROWS = K_PASS // 32
 LIST_ROWS = 16
 WINDOWS = 3
+RUN = 4
+SCALAR_DY_ROWS = 192
+
+UNIT = 2048
+LAP = 64
+LAST_A = 0
+BELOW_A_HIGH = 4 * UNIT
+A_HIGH = BELOW_A_HIGH + UNIT - LAP
+ABOVE_A_HIGH = A_HIGH + UNIT - LAP
+FIRST_A = 8 * UNIT
+A_SLOTS = 12 * UNIT
+FIRST_DY = 18 * UNIT
+V2_GROUPED = 22 * UNIT
 
 
 def tile_attend_glora_ax_kernel(
@@ -45,22 +59,20 @@ def tile_attend_glora_ax_kernel(
                 return placed.tile(shape, dtype, name=name, align_bytes=64, offset=reuses)
             return keep.tile(shape, dtype, name=name, tag=reuses or name, align_bytes=64)
 
-        def quantize(name, grouped, fmt, reuses=None, scales_reuse=None):
+        def quantize(name, grouped, fmt, reuses=None):
             width = grouped.shape[1] // PACK
             codes = sbuf(name + "_codes", [P, width], U32, reuses)
-            scales = sbuf(name + "_scales", [P, width], U8, scales_reuse)
+            scales = sbuf(name + "_scales", [P, width], U8)
             nc.vector.quantize_mx(out=codes[:].bitcast(fmt), scales=scales[:], in_=grouped)
             return codes, scales
 
         offsets = keep.tile([P, SLOTS // LIST_ROWS], U16, name="offsets")
         nc.sync.dma_start(offsets[:], offs)
         bt_scale_pool = sbuf("bt_scale_pool", [P, T], U8)
-        for q in range(P // QUADRANT):
-            rows = Bt_scales[0, PACK * q : PACK * (q + 1), :].bitcast(I32)
-            nc.scalar.dma_start(
-                bt_scale_pool[QUADRANT * q : QUADRANT * (q + 1), :].bitcast(I32),
-                rows.unsqueeze(0).broadcast_to([QUADRANT // PACK, PACK, T // 4]),
-            )
+        nc.vector.memset(bt_scale_pool[0 : P - SCALE_ROWS, :].bitcast(I32), 0)
+        nc.scalar.dma_start(bt_scale_pool[P - SCALE_ROWS : P, :].bitcast(I32), Bt_scales[0].bitcast(I32))
+        bt_scales = sbuf("bt_scales", [P, SLOTS], U8)
+        nc.vector.memset(bt_scales[:].bitcast(I32), 0)
         us_tile = sbuf("us_tile", [P, ROW_PASSES, 2 * PACK], F32)
         us_cols = us_tile[:, :, 0:PACK]
         wt_tile = sbuf("wt_tile", [P, ROW_PASSES, 2 * PACK], F32)
@@ -74,13 +86,13 @@ def tile_attend_glora_ax_kernel(
         bt_word_pool = sbuf("bt_word_pool", [P, T], I32)
         nc.sync.dma_start(bt_word_pool[:], Bt_words[0].rearrange("p n t -> p (n t)").bitcast(I32))
 
-        def load_dy(name, r0, r1):
-            raw = sbuf(name, [P, PACK, r1 - r0], F32)
+        def load_dy(name, r0, r1, reuses=None):
+            raw = sbuf(name, [P, PACK, r1 - r0], F32, reuses)
             nc.sync.dma_start(raw[:], dyT[:, r0:r1].rearrange("(p j) r -> p j r", j=PACK))
             return raw
 
-        def load_x(j, reuses=None):
-            raw = sbuf("x_raw%d" % j, [P, R], F32, reuses)
+        def load_x(j):
+            raw = sbuf("x_raw%d" % j, [P, R], F32)
             nc.sync.dma_start(raw[:], xT[j * P : (j + 1) * P, :])
             return raw
 
@@ -89,16 +101,16 @@ def tile_attend_glora_ax_kernel(
             nc.sync.dma_start(pool[:], A[j * P : (j + 1) * P, :])
             return pool
 
-        dy_raw0 = load_dy("dy_raw0", 0, K_PASS)
+        dy_raw0 = load_dy("dy_raw0", 0, K_PASS, reuses=FIRST_DY)
         dy_raw1a = load_dy("dy_raw1a", K_PASS, K_PASS + K_PASS // 2)
         dy_raw1b = load_dy("dy_raw1b", K_PASS + K_PASS // 2, R)
         x_raw0 = load_x(0)
-        a_pool0 = load_a(0, reuses=16384)
+        a_pool0 = load_a(0, reuses=FIRST_A)
         x_raw1 = load_x(1)
         x_raw2 = load_x(2)
         a_pool1 = load_a(1)
         a_pool2 = load_a(2)
-        a_pool3 = load_a(3, reuses=0)
+        a_pool3 = load_a(3, reuses=LAST_A)
         x_raw3 = load_x(3)
 
         ident = sbuf("ident", [P, P], F32)
@@ -109,9 +121,19 @@ def tile_attend_glora_ax_kernel(
             nc.gpsimd.memset(window[:], 0.0)
             return window
 
-        windows = [zeroed_window(0)]
-        last_window = sbuf("window2", [P, T], F32)
-        nc.vector.memset(last_window[:].bitcast(I32), 0)
+        bt_scales_listed = sbuf("bt_scales_listed", [P, SLOTS], U8)
+        nc.vector.tensor_copy(bt_scales_listed[:], bt_scale_pool[:].indirect(offsets[:]))
+        bt_scales_dealt = sbuf("bt_scales_dealt", [P, SLOTS], U8)
+        nc.vector.tensor_copy(
+            bt_scales_dealt[:].rearrange("p (t m) -> p t m", t=PACK),
+            bt_scales_listed[:].rearrange("p (m t) -> p t m", t=PACK),
+        )
+        for q in range(P // QUADRANT):
+            first = P - SCALE_ROWS + PACK * q
+            nc.scalar.dma_start(
+                bt_scales[QUADRANT * q : QUADRANT * q + PACK, :].bitcast(I32),
+                bt_scales_dealt[first : first + PACK, :].bitcast(I32),
+            )
 
         sc_row = sbuf("sc_row", [P, SLOTS], F32)
         nc.vector.tensor_copy(sc_row[:], sc_pool[:].indirect(offsets[:]))
@@ -121,40 +143,25 @@ def tile_attend_glora_ax_kernel(
         sc_cols = sbuf("sc_cols", [P, PACK], F32)
         nc.scalar.copy(sc_cols[:], sc_turned[:, :, P - 1])
 
-        bt_scales_listed = sbuf("bt_scales_listed", [P, SLOTS], U8, reuses="sc_pool")
-        nc.vector.tensor_copy(bt_scales_listed[:], bt_scale_pool[:].indirect(offsets[:]))
+        bt_codes_listed = sbuf("bt_codes_listed", [P, SLOTS], U32)
+        nc.vector.tensor_copy(bt_codes_listed[:], bt_word_pool[:].bitcast(U32).indirect(offsets[:]))
         bt_codes = sbuf("bt_codes", [P, SLOTS], U32)
         nc.vector.tensor_copy(
-            bt_codes[:].rearrange("p (t m) -> p m t", t=PACK), bt_word_pool[:].bitcast(U32).indirect(offsets[:])
+            bt_codes[:].bitcast(I32).rearrange("p (t c n) -> p c t n", t=PACK, n=RUN),
+            bt_codes_listed[:].bitcast(I32).rearrange("p (c n t) -> p c t n", t=PACK, n=RUN),
         )
-        bt_scales = sbuf("bt_scales", [P, SLOTS], U8)
-        nc.vector.tensor_copy(
-            bt_scales[:].rearrange("p (t m) -> p t m", t=PACK),
-            bt_scales_listed[:].rearrange("p (m t) -> p t m", t=PACK),
-        )
-
-        factor_cols = sbuf("factor_cols", [P, ROW_PASSES, PACK], F32)
-        nc.gpsimd.tensor_tensor(factor_cols[:], us_cols, wt_cols, MULT)
-        row_factor = []
-        for g in range(ROW_PASSES):
-            spread = quarters(banks[1 + g])
-            for t in range(PACK):
-                nc.tensor.transpose(spread[:, t, :], factor_cols[:, g, t : t + 1].to_broadcast([P, P]), ident[:])
-            factor = sbuf("row_factor%d" % g, [P, K_PASS], F32)
-            nc.scalar.copy(factor[:].rearrange("p (m t) -> p m t", t=PACK), spread.rearrange("p t m -> p m t"))
-            row_factor.append(factor)
 
         def group_dy(raw, c0, c1, grouped, r0, copy):
             copy(
-                grouped[:, PACK * (r0 + c0) : PACK * (r0 + c1)].rearrange("p (c n j) -> p c j n", n=4, j=PACK),
-                raw[:, :, c0:c1].rearrange("p j (c n) -> p c j n", n=4),
+                grouped[:, PACK * (r0 + c0) : PACK * (r0 + c1)].rearrange("p (c n j) -> p c j n", n=RUN, j=PACK),
+                raw[:, :, c0:c1].rearrange("p j (c n) -> p c j n", n=RUN),
             )
 
         v2_tiles = [sbuf("v2_%d" % g, [P, PACK * K_PASS], BF16) for g in range(ROW_PASSES)]
 
-        def first_product(g, dy_q, into, places):
+        def first_product(g, dy_q, into):
             dy_codes, dy_scales = dy_q
-            for t in places:
+            for t in range(PACK):
                 v = banks[into[t]]
                 cols = slice(t * P, (t + 1) * P)
                 nc.tensor.matmul_mx(
@@ -169,8 +176,8 @@ def tile_attend_glora_ax_kernel(
         def group_v2_slots(g, h, grouped):
             rows = slice(h * K_PASS // 2, (h + 1) * K_PASS // 2)
             nc.scalar.copy(
-                grouped[:].rearrange("p (r t) -> p r t", t=PACK)[:, rows].rearrange("p (c n) t -> p c t n", n=4),
-                v2_tiles[g][:].rearrange("p (t r) -> p t r", t=PACK)[:, :, rows].rearrange("p t (c n) -> p c t n", n=4),
+                grouped[:].rearrange("p (r t) -> p r t", t=PACK)[:, rows].rearrange("p (c n) t -> p c t n", n=RUN),
+                v2_tiles[g][:].rearrange("p (t r) -> p t r", t=PACK)[:, :, rows].rearrange("p t (c n) -> p c t n", n=RUN),
             )
 
         def turn_pairs(src, grouped, into):
@@ -185,7 +192,6 @@ def tile_attend_glora_ax_kernel(
                 bank.rearrange("p b u m -> p b m u"),
             )
 
-
         def round_x(j, raw, reuses=None, on_gpsimd=False):
             rounded = sbuf("x_rounded%d" % j, [P, R], BF16, reuses)
             if on_gpsimd:
@@ -199,8 +205,8 @@ def tile_attend_glora_ax_kernel(
             turn_pairs(rounded[:], grouped[:], into)
             return grouped
 
-        def group_v2_rows(g, into):
-            grouped = sbuf("v2_rows%d" % g, [P, SLOTS * PACK], BF16)
+        def group_v2_rows(g, into, reuses=None):
+            grouped = sbuf("v2_rows%d" % g, [P, SLOTS * PACK], BF16, reuses)
             for h in range(2):
                 cols = slice(2 * h * K_PASS, 2 * (h + 1) * K_PASS)
                 turn_pairs(v2_tiles[g][:, cols], grouped[:, cols], into[h])
@@ -248,35 +254,46 @@ def tile_attend_glora_ax_kernel(
             nc.scalar.dma_start(rows, dx)
 
         dy_grouped = [sbuf("dy_grouped%d" % g, [P, K_PASS * PACK], BF16) for g in range(ROW_PASSES)]
-        group_dy(dy_raw0, 0, 192, dy_grouped[0], 0, nc.scalar.copy)
-        group_dy(dy_raw0, 192, K_PASS, dy_grouped[0], 0, nc.vector.tensor_copy)
+        group_dy(dy_raw0, 0, SCALAR_DY_ROWS, dy_grouped[0], 0, nc.scalar.copy)
+        group_dy(dy_raw0, SCALAR_DY_ROWS, K_PASS, dy_grouped[0], 0, nc.vector.tensor_copy)
         dy_q0 = quantize("dy0", dy_grouped[0][:], E5M2)
-        windows.append(zeroed_window(1, reuses="dy_grouped0"))
+        factor_cols = sbuf("factor_cols", [P, ROW_PASSES, PACK], F32)
+        nc.gpsimd.tensor_tensor(factor_cols[:], us_cols, wt_cols, MULT)
+        row_factor = []
+        for g in range(ROW_PASSES):
+            spread = quarters(banks[1 + g])
+            for t in range(PACK):
+                nc.tensor.transpose(spread[:, t, :], factor_cols[:, g, t : t + 1].to_broadcast([P, P]), ident[:])
+            factor = sbuf("row_factor%d" % g, [P, K_PASS], F32, reuses=FIRST_DY + UNIT * g)
+            nc.scalar.copy(factor[:].rearrange("p (m t) -> p m t", t=PACK), spread.rearrange("p t m -> p m t"))
+            row_factor.append(factor)
+        second_window = zeroed_window(1, reuses="dy_grouped0")
         group_dy(dy_raw1a, 0, K_PASS // 2, dy_grouped[1], 0, nc.scalar.copy)
         group_dy(dy_raw1b, 0, K_PASS // 2, dy_grouped[1], K_PASS // 2, nc.scalar.copy)
-        first_product(0, dy_q0, into=(3, 4, 5, 6), places=range(PACK))
+        first_product(0, dy_q0, into=(3, 4, 5, 6))
         dy_q1 = quantize("dy1", dy_grouped[1][:], E5M2)
-        windows.append(last_window)
         a_low = sbuf("a_low", [P, 2 * SLOTS], BF16)
         gather_a(a_pool0, a_low[:, 0:SLOTS])
-        x_rounded1 = round_x(1, x_raw1, reuses=16384, on_gpsimd=True)
-        x_rounded2 = round_x(2, x_raw2, reuses=16384 + 2048, on_gpsimd=True)
-        first_product(1, dy_q1, into=(7, 0, 1, 2), places=range(PACK))
+        x_rounded1 = round_x(1, x_raw1, reuses=FIRST_A, on_gpsimd=True)
+        x_rounded2 = round_x(2, x_raw2, reuses=FIRST_A + UNIT, on_gpsimd=True)
+        first_product(1, dy_q1, into=(7, 0, 1, 2))
+
         v2_rows0 = group_v2_rows(0, into=(3, 5))
         x_grouped0 = group_x(0, round_x(0, x_raw0), into=4)
-        v2_slots = [sbuf("v2_slots0", [P, K_PASS * PACK], BF16)]
-        v2_rows1 = group_v2_rows(1, into=(7, 1))
+        v2_slots = [sbuf("v2_slots0", [P, K_PASS * PACK], BF16, reuses=V2_GROUPED + 2 * UNIT)]
+        v2_rows1 = group_v2_rows(1, into=(7, 1), reuses=V2_GROUPED)
         group_v2_slots(0, 0, v2_slots[0])
         group_v2_slots(0, 1, v2_slots[0])
         v2_rows_q = [quantize("v2_rows0", v2_rows0[:], E5M2)]
         x_q0 = quantize("x0", x_grouped0[:], E4M3)
         v2_rows_q.append(quantize("v2_rows1", v2_rows1[:], E5M2))
         v2_slots_q = [quantize("v2_slots0", v2_slots[0][:], E5M2, reuses="v2_rows0")]
-        a_high = sbuf("a_high", [P, 2 * SLOTS], BF16, reuses=10176)
+        windows = [zeroed_window(0, reuses=V2_GROUPED), second_window]
+        a_high = sbuf("a_high", [P, 2 * SLOTS], BF16, reuses=A_HIGH)
         gather_a(a_pool1, a_low[:, SLOTS:])
         gather_a(a_pool2, a_high[:, 0:SLOTS])
         gather_a(a_pool3, a_high[:, SLOTS:])
-        a_slots = sbuf("a_slots", [P, D * PACK], BF16)
+        a_slots = sbuf("a_slots", [P, D * PACK], BF16, reuses=A_SLOTS)
         turn_pairs(a_high[:, SLOTS:], a_slots[:, 3 * K_PASS :], into=7)
         x_grouped12 = sbuf("x_grouped12", [P, 2 * R], BF16)
         turn_pairs(x_rounded1[:], x_grouped12[:, 0:R], into=0)
@@ -286,19 +303,21 @@ def tile_attend_glora_ax_kernel(
         group_v2_slots(1, 1, v2_slots[1])
         turn_pairs(a_high[:, 0:SLOTS], a_slots[:, 2 * K_PASS : 3 * K_PASS], into=5)
         turn_pairs(a_low[:], a_slots[:, 0 : 2 * K_PASS], into=3)
-        x_q12 = quantize("x12", x_grouped12[:], E4M3, reuses=4096)
-        v2_slots_q.append(quantize("v2_slots1", v2_slots[1][:], E5M2, reuses=2048))
+        x_q12 = quantize("x12", x_grouped12[:], E4M3, reuses=LAST_A + 2 * UNIT)
+        v2_slots_q.append(quantize("v2_slots1", v2_slots[1][:], E5M2, reuses=LAST_A + UNIT))
         a_q = quantize("a", a_slots[:], E4M3)
-        scatter(0, fetch(0, second_product(x_q0, v2_rows_q, into=6), reuses=8192))
+
+        scatter(0, fetch(0, second_product(x_q0, v2_rows_q, into=6), reuses=BELOW_A_HIGH))
+        windows.append(zeroed_window(2, reuses=A_SLOTS + UNIT))
         da1 = second_product(x_q12, v2_rows_q, into=2)
-        x_rounded3 = round_x(3, x_raw3, reuses=10176 + 1984)
-        dx = sbuf("dx", [P, 8, D], F32)
+        x_rounded3 = round_x(3, x_raw3, reuses=ABOVE_A_HIGH)
+        dx = sbuf("dx", [P, R // P, D], F32)
         third_product(0, v2_slots_q, a_q, (5,), dx[:, 0:1])
         third_product(1, v2_slots_q, a_q, (7,), dx[:, 1:2])
-        scatter(1, fetch(1, da1, reuses="a_slots"))
+        scatter(1, fetch(1, da1, reuses=A_SLOTS))
         third_product(2, v2_slots_q, a_q, (3, 4), dx[:, 2:4])
         third_product(4, v2_slots_q, a_q, (6,), dx[:, 4:5])
-        x_q3 = quantize("x3", group_x(3, x_rounded3, into=1)[:], E4M3, reuses=8192)
-        scatter(2, fetch(2, second_product(x_q12, v2_rows_q, into=5, first=2 * P), reuses=10176 + 1984))
+        x_q3 = quantize("x3", group_x(3, x_rounded3, into=1)[:], E4M3, reuses=BELOW_A_HIGH)
+        scatter(2, fetch(2, second_product(x_q12, v2_rows_q, into=5, first=2 * P), reuses=ABOVE_A_HIGH))
         third_product(5, v2_slots_q, a_q, (0, 7, 3), dx[:, 5:8])
         scatter(3, fetch(3, second_product(x_q3, v2_rows_q, into=7)))

@@ -25,20 +25,21 @@ BANKS = 8
 QUADRANT = 32
 SCALE_ROWS = K_PASS // 32
 LIST_ROWS = 16
-WINDOWS = 3
-RUN = 4
-SCALAR_DY_ROWS = 192
+CHUNKS = 4
+CHUNK = R // CHUNKS
+COPY = mybir.ActivationFunctionType.Copy
 
-UNIT = 2048
+KIB = 1024
 LAP = 64
-LAST_A = 0
-BELOW_A_HIGH = 4 * UNIT
-A_HIGH = BELOW_A_HIGH + UNIT - LAP
-ABOVE_A_HIGH = A_HIGH + UNIT - LAP
-FIRST_A = 8 * UNIT
-A_SLOTS = 12 * UNIT
-FIRST_DY = 18 * UNIT
-V2_GROUPED = 22 * UNIT
+BT_WORDS = 0
+DY_RAW = (12 * KIB, 16 * KIB, 28 * KIB, 32 * KIB)
+WINDOW1 = 40 * KIB
+SCALES_LISTED = WINDOW1 + 8 * KIB - LAP
+DY0_GROUPED = SCALES_LISTED + SLOTS - LAP
+DY3_GROUPED = 54 * KIB
+X2_GROUPED = 60 * KIB
+A_LOW = X2_GROUPED - 2 * KIB + LAP
+V2_SLOTS = X2_GROUPED + 2 * KIB - LAP
 
 
 def tile_attend_glora_ax_kernel(
@@ -54,17 +55,17 @@ def tile_attend_glora_ax_kernel(
         def quarters(bank):
             return bank[:].rearrange("p (c m) -> p c m", c=PACK)
 
-        def sbuf(name, shape, dtype, reuses=None):
-            if isinstance(reuses, int):
-                return placed.tile(shape, dtype, name=name, align_bytes=64, offset=reuses)
-            return keep.tile(shape, dtype, name=name, tag=reuses or name, align_bytes=64)
+        def sbuf(name, shape, dtype, at=None):
+            if at is None:
+                return keep.tile(shape, dtype, name=name, align_bytes=64)
+            return placed.tile(shape, dtype, name=name, align_bytes=64, offset=at)
 
-        def quantize(name, grouped, fmt, reuses=None):
-            width = grouped.shape[1] // PACK
-            codes = sbuf(name + "_codes", [P, width], U32, reuses)
-            scales = sbuf(name + "_scales", [P, width], U8)
-            nc.vector.quantize_mx(out=codes[:].bitcast(fmt), scales=scales[:], in_=grouped)
-            return codes, scales
+        def mx_tiles(name, width):
+            return sbuf(name + "_codes", [P, width], U32), sbuf(name + "_scales", [P, width], U8)
+
+        def quantize(mx, grouped, fmt, first=0):
+            cols = slice(first, first + grouped.shape[1] // PACK)
+            nc.vector.quantize_mx(out=mx[0][:, cols].bitcast(fmt), scales=mx[1][:, cols], in_=grouped)
 
         offsets = keep.tile([P, SLOTS // LIST_ROWS], U16, name="offsets")
         nc.sync.dma_start(offsets[:], offs)
@@ -79,245 +80,262 @@ def tile_attend_glora_ax_kernel(
         wt_cols = wt_tile[:, :, 0:PACK]
         nc.scalar.dma_start(us_cols, us.rearrange("(g p t) o -> p g (t o)", g=ROW_PASSES, t=PACK))
         nc.scalar.dma_start(wt_cols, wt.rearrange("(g p t) o -> p g (t o)", g=ROW_PASSES, t=PACK))
-
         sc_pool = sbuf("sc_pool", [P, T], F32)
         nc.vector.memset(sc_pool[0 : P - 1, :].bitcast(I32), 0)
         nc.sync.dma_start(sc_pool[P - 1 : P, :], sc[P - 1 : P, :])
-        bt_word_pool = sbuf("bt_word_pool", [P, T], I32)
+        bt_word_pool = sbuf("bt_word_pool", [P, T], I32, at=BT_WORDS)
         nc.sync.dma_start(bt_word_pool[:], Bt_words[0].rearrange("p n t -> p (n t)").bitcast(I32))
 
-        def load_dy(name, r0, r1, reuses=None):
-            raw = sbuf(name, [P, PACK, r1 - r0], F32, reuses)
-            nc.sync.dma_start(raw[:], dyT[:, r0:r1].rearrange("(p j) r -> p j r", j=PACK))
+        def load_dy(c):
+            raw = sbuf("dy_raw%d" % c, [P, PACK, CHUNK], F32, DY_RAW[c])
+            nc.sync.dma_start(raw[:], dyT[:, c * CHUNK : (c + 1) * CHUNK].rearrange("(p j) r -> p j r", j=PACK))
             return raw
 
-        def load_x(j):
-            raw = sbuf("x_raw%d" % j, [P, R], F32)
+        def load_x(j, at):
+            raw = sbuf("x_raw%d" % j, [P, R], F32, at)
             nc.sync.dma_start(raw[:], xT[j * P : (j + 1) * P, :])
             return raw
 
-        def load_a(j, reuses=None):
-            pool = sbuf("a_pool%d" % j, [P, T], F32, reuses)
+        def load_a(j, at):
+            pool = sbuf("a_pool%d" % j, [P, T], F32, at)
             nc.sync.dma_start(pool[:], A[j * P : (j + 1) * P, :])
             return pool
 
-        dy_raw0 = load_dy("dy_raw0", 0, K_PASS, reuses=FIRST_DY)
-        dy_raw1a = load_dy("dy_raw1a", K_PASS, K_PASS + K_PASS // 2)
-        dy_raw1b = load_dy("dy_raw1b", K_PASS + K_PASS // 2, R)
-        x_raw0 = load_x(0)
-        a_pool0 = load_a(0, reuses=FIRST_A)
-        x_raw1 = load_x(1)
-        x_raw2 = load_x(2)
-        a_pool1 = load_a(1)
-        a_pool2 = load_a(2)
-        a_pool3 = load_a(3, reuses=LAST_A)
-        x_raw3 = load_x(3)
+        dy_raw = [load_dy(c) for c in range(CHUNKS)]
 
         ident = sbuf("ident", [P, P], F32)
         make_identity(nc, ident[:])
 
-        def zeroed_window(n, reuses=None):
-            window = sbuf("window%d" % n, [P, T], F32, reuses)
-            nc.gpsimd.memset(window[:], 0.0)
+        def zeroed_window(n, engine, at=None):
+            window = sbuf("window%d" % n, [P, T], F32, at)
+            engine.memset(window[:].bitcast(I32), 0)
             return window
 
-        bt_scales_listed = sbuf("bt_scales_listed", [P, SLOTS], U8)
+        window0 = zeroed_window(0, nc.vector)
+        window2 = zeroed_window(2, nc.vector)
+
+        bt_scales_listed = sbuf("bt_scales_listed", [P, SLOTS], U8, at=SCALES_LISTED)
         nc.vector.tensor_copy(bt_scales_listed[:], bt_scale_pool[:].indirect(offsets[:]))
         bt_scales_dealt = sbuf("bt_scales_dealt", [P, SLOTS], U8)
         nc.vector.tensor_copy(
             bt_scales_dealt[:].rearrange("p (t m) -> p t m", t=PACK),
             bt_scales_listed[:].rearrange("p (m t) -> p t m", t=PACK),
         )
+        sc_row = sbuf("sc_row", [P, SLOTS], F32)
+        nc.scalar.activation(sc_row[:], sc_pool[:].indirect(offsets[:]), COPY)
         for q in range(P // QUADRANT):
             first = P - SCALE_ROWS + PACK * q
             nc.scalar.dma_start(
                 bt_scales[QUADRANT * q : QUADRANT * q + PACK, :].bitcast(I32),
                 bt_scales_dealt[first : first + PACK, :].bitcast(I32),
             )
+        factor_cols = sbuf("factor_cols", [P, ROW_PASSES, PACK], F32)
+        nc.gpsimd.tensor_tensor(factor_cols[:], us_cols, wt_cols, MULT)
+        window1 = zeroed_window(1, nc.gpsimd, at=WINDOW1)
 
-        sc_row = sbuf("sc_row", [P, SLOTS], F32)
-        nc.vector.tensor_copy(sc_row[:], sc_pool[:].indirect(offsets[:]))
-        sc_turned = quarters(banks[0])
+        sc_turned = quarters(banks[4])
         for t in range(PACK):
             nc.tensor.transpose(sc_turned[:, t, :], sc_row[:, t:SLOTS:PACK], ident[:])
         sc_cols = sbuf("sc_cols", [P, PACK], F32)
         nc.scalar.copy(sc_cols[:], sc_turned[:, :, P - 1])
 
-        bt_codes_listed = sbuf("bt_codes_listed", [P, SLOTS], U32)
-        nc.vector.tensor_copy(bt_codes_listed[:], bt_word_pool[:].bitcast(U32).indirect(offsets[:]))
         bt_codes = sbuf("bt_codes", [P, SLOTS], U32)
         nc.vector.tensor_copy(
-            bt_codes[:].bitcast(I32).rearrange("p (t c n) -> p c t n", t=PACK, n=RUN),
-            bt_codes_listed[:].bitcast(I32).rearrange("p (c n t) -> p c t n", t=PACK, n=RUN),
+            bt_codes[:].rearrange("p (t m) -> p m t", t=PACK), bt_word_pool[:].bitcast(U32).indirect(offsets[:])
         )
+        x_raw0 = load_x(0, BT_WORDS)
+        x_raw1 = load_x(1, BT_WORDS + 4 * KIB)
 
-        def group_dy(raw, c0, c1, grouped, r0, copy):
-            copy(
-                grouped[:, PACK * (r0 + c0) : PACK * (r0 + c1)].rearrange("p (c n j) -> p c j n", n=RUN, j=PACK),
-                raw[:, :, c0:c1].rearrange("p j (c n) -> p c j n", n=RUN),
+        row_factor = []
+        for g in range(ROW_PASSES):
+            spread = quarters(banks[5 + g])
+            for t in range(PACK):
+                nc.tensor.transpose(spread[:, t, :], factor_cols[:, g, t : t + 1].to_broadcast([P, P]), ident[:])
+            factor = sbuf("row_factor%d" % g, [P, K_PASS], F32)
+            nc.scalar.copy(
+                factor[:].rearrange("p (u m e) -> p u m e", u=2, e=2), spread.rearrange("p (u e) m -> p u m e", u=2)
             )
+            row_factor.append(factor)
+
+        def group_dy(c, copy, at=None):
+            grouped = sbuf("dy_grouped%d" % c, [P, CHUNK * PACK], BF16, at)
+            copy(
+                grouped[:].rearrange("p (u m e j) -> p m j u e", u=2, e=2, j=PACK),
+                dy_raw[c][:].rearrange("p j (m u e) -> p m j u e", u=2, e=2),
+            )
+            return grouped
+
+        def round_on_gpsimd(out, in_):
+            nc.gpsimd.tensor_scalar(out, in_, 1.0, 0.0, MULT, ADD)
 
         v2_tiles = [sbuf("v2_%d" % g, [P, PACK * K_PASS], BF16) for g in range(ROW_PASSES)]
 
-        def first_product(g, dy_q, into):
-            dy_codes, dy_scales = dy_q
-            for t in range(PACK):
-                v = banks[into[t]]
-                cols = slice(t * P, (t + 1) * P)
-                nc.tensor.matmul_mx(
-                    out=v[:], lhsT=bt_codes[:, cols].bitcast(E4M3), lhsT_scale=bt_scales[:, cols],
-                    rhs=dy_codes[:].bitcast(E5M2), rhs_scale=dy_scales[:], start=True, stop=True,
-                )
-                nc.vector.scalar_tensor_tensor(
-                    v2_tiles[g][:, t * K_PASS : (t + 1) * K_PASS], v[:], sc_cols[:, t : t + 1], row_factor[g][:],
-                    MULT, MULT,
-                )
-
-        def group_v2_slots(g, h, grouped):
-            rows = slice(h * K_PASS // 2, (h + 1) * K_PASS // 2)
-            nc.scalar.copy(
-                grouped[:].rearrange("p (r t) -> p r t", t=PACK)[:, rows].rearrange("p (c n) t -> p c t n", n=RUN),
-                v2_tiles[g][:].rearrange("p (t r) -> p t r", t=PACK)[:, :, rows].rearrange("p t (c n) -> p c t n", n=RUN),
+        def first_product(c, t, dy_mx):
+            g, h = divmod(c, 2)
+            v = banks[t][:, h * CHUNK : (h + 1) * CHUNK]
+            cols = slice(t * P, (t + 1) * P)
+            nc.tensor.matmul_mx(
+                out=v, lhsT=bt_codes[:, cols].bitcast(E4M3), lhsT_scale=bt_scales[:, cols],
+                rhs=dy_mx[0][:].bitcast(E5M2), rhs_scale=dy_mx[1][:], start=True, stop=True,
+            )
+            rows = slice(h * P, (h + 1) * P)
+            nc.vector.scalar_tensor_tensor(
+                v2_tiles[g][:].rearrange("p (t u n) -> p t u n", t=PACK, u=2)[:, t, :, rows],
+                v.rearrange("p (u n) -> p u n", u=2),
+                sc_cols[:, t : t + 1],
+                row_factor[g][:].rearrange("p (u n) -> p u n", u=2)[:, :, rows],
+                MULT, MULT,
             )
 
-        def turn_pairs(src, grouped, into):
-            stretches = src.shape[1] // K_PASS
-            words = src.bitcast(F32)
-            bank = banks[into][:, 0 : stretches * 2 * P].rearrange("p (b u m) -> p b u m", b=stretches, u=2)
-            for b in range(stretches):
+        def turn(words, grouped, into, copy):
+            count = len(words)
+            bank = banks[into][:, 0 : count * 2 * P].rearrange("p (b u m) -> p b u m", b=count, u=2)
+            for b in range(count):
                 for u in range(2):
-                    nc.tensor.transpose(bank[:, b, u, :], words[:, b * 2 * P + u : (b + 1) * 2 * P : 2], ident[:])
-            nc.scalar.copy(
-                grouped.bitcast(F32).rearrange("p (b m u) -> p b m u", b=stretches, u=2),
-                bank.rearrange("p b u m -> p b m u"),
+                    nc.tensor.transpose(bank[:, b, u, :], words[b][u], ident[:])
+            copy(grouped.bitcast(F32).rearrange("p (b m u) -> p b m u", b=count, u=2), bank.rearrange("p b u m -> p b m u"))
+
+        def turn_v2(g, t0, t1, into):
+            words = v2_tiles[g][:].bitcast(F32).rearrange("p (t u m) -> p t u m", t=PACK, u=2)
+            turn(
+                [[words[:, t, u, :] for u in range(2)] for t in range(t0, t1)],
+                v2_rows[g][:, t0 * K_PASS : t1 * K_PASS], into, nc.scalar.copy,
             )
 
-        def round_x(j, raw, reuses=None, on_gpsimd=False):
-            rounded = sbuf("x_rounded%d" % j, [P, R], BF16, reuses)
-            if on_gpsimd:
-                nc.gpsimd.tensor_scalar(rounded[:], raw[:], 1.0, 0.0, MULT, ADD)
-            else:
-                nc.scalar.copy(rounded[:], raw[:])
+        def quantize_v2_rows(g, t0, t1):
+            quantize(v2_rows_mx[g], v2_rows[g][:, t0 * K_PASS : t1 * K_PASS], E5M2, first=t0 * P)
+
+        def round_x(j, raw, rounder, at=None):
+            rounded = sbuf("x_rounded%d" % j, [P, R], BF16, at)
+            rounder(
+                rounded[:].rearrange("p (u m e) -> p u m e", u=2, e=2), raw[:].rearrange("p (m u e) -> p u m e", u=2, e=2)
+            )
             return rounded
 
-        def group_x(j, rounded, into):
-            grouped = sbuf("x_grouped%d" % j, [P, ROW_PASSES * K_PASS], BF16)
-            turn_pairs(rounded[:], grouped[:], into)
-            return grouped
+        def turn_x(rounded, grouped, into, copy):
+            words = rounded[:].bitcast(F32).rearrange("p (u g m) -> p g u m", u=2, g=ROW_PASSES)
+            turn([[words[:, g, u, :] for u in range(2)] for g in range(ROW_PASSES)], grouped, into, copy)
 
-        def group_v2_rows(g, into, reuses=None):
-            grouped = sbuf("v2_rows%d" % g, [P, SLOTS * PACK], BF16, reuses)
-            for h in range(2):
-                cols = slice(2 * h * K_PASS, 2 * (h + 1) * K_PASS)
-                turn_pairs(v2_tiles[g][:, cols], grouped[:, cols], into[h])
-            return grouped
+        def turn_a(listed, grouped, into):
+            words = listed[:].bitcast(F32).rearrange("p (b m u) -> p b u m", b=2, u=2)
+            turn([[words[:, b, u, :] for u in range(2)] for b in range(2)], grouped, into, nc.scalar.copy)
 
-        def gather_a(pool, listed):
-            nc.vector.tensor_copy(listed, pool[:].indirect(offsets[:]))
-
-        def second_product(x_q, v2_rows_q, into, first=0):
-            x_codes, x_scales = x_q
+        def second_product(x_mx, first, into):
             da = banks[into]
             for g in range(ROW_PASSES):
                 cols = slice(first + g * P, first + (g + 1) * P)
-                v2_codes, v2_scales = v2_rows_q[g]
                 nc.tensor.matmul_mx(
-                    out=da[:], lhsT=x_codes[:, cols].bitcast(E4M3), lhsT_scale=x_scales[:, cols],
-                    rhs=v2_codes[:].bitcast(E5M2), rhs_scale=v2_scales[:],
+                    out=da[:], lhsT=x_mx[0][:, cols].bitcast(E4M3), lhsT_scale=x_mx[1][:, cols],
+                    rhs=v2_rows_mx[g][0][:].bitcast(E5M2), rhs_scale=v2_rows_mx[g][1][:],
                     start=(g == 0), stop=(g == ROW_PASSES - 1),
                 )
             return da
 
-        def fetch(j, da, reuses=None):
-            da_sb = sbuf("da_sb%d" % j, [P, SLOTS], F32, reuses)
-            nc.scalar.copy(da_sb[:].rearrange("p (m t) -> p m t", t=PACK), quarters(da).rearrange("p t m -> p m t"))
+        def fetch(j, da, copy):
+            da_sb = sbuf("da_sb%d" % j, [P, SLOTS], F32)
+            copy(da_sb[:].rearrange("p (m t) -> p m t", t=PACK), quarters(da).rearrange("p t m -> p m t"))
             return da_sb
 
-        def scatter(j, da_sb):
-            window = windows[j % WINDOWS]
-            nc.vector.tensor_copy(window[:].indirect(offsets[:]), da_sb[:])
-            nc.sync.dma_start(out_0[j * P : (j + 1) * P, :], window[:])
+        def scatter_on_scalar(window, da_sb, between=None):
+            half = SLOTS // 2
+            for h in range(2):
+                if h == 1 and between is not None:
+                    between()
+                listed = offsets[:, h * half // LIST_ROWS : (h + 1) * half // LIST_ROWS]
+                nc.scalar.activation(window[:].indirect(listed), da_sb[:, h * half : (h + 1) * half], COPY)
 
-        def third_product(c0, v2_slots_q, a_q, into, dx):
-            v2_codes, v2_scales = v2_slots_q[c0 // PACK]
-            a_codes, a_scales = a_q
-            count = len(into)
-            for n in range(count):
-                cols = slice((c0 % PACK + n) * P, (c0 % PACK + n + 1) * P)
-                acc = banks[into[n]]
-                nc.tensor.matmul_mx(
-                    out=acc[:], lhsT=v2_codes[:, cols].bitcast(E5M2), lhsT_scale=v2_scales[:, cols],
-                    rhs=a_codes[:].bitcast(E4M3), rhs_scale=a_scales[:], start=True, stop=True,
-                )
-                nc.scalar.copy(dx[:, n, :], acc[:])
-            rows = out_1[c0 * P : (c0 + count) * P, :].rearrange("(n m) d -> m n d", m=P)
-            nc.scalar.dma_start(rows, dx)
+        def store_window(j, window, queue):
+            queue.dma_start(out_0[j * P : (j + 1) * P, :], window[:])
 
-        dy_grouped = [sbuf("dy_grouped%d" % g, [P, K_PASS * PACK], BF16) for g in range(ROW_PASSES)]
-        group_dy(dy_raw0, 0, SCALAR_DY_ROWS, dy_grouped[0], 0, nc.scalar.copy)
-        group_dy(dy_raw0, SCALAR_DY_ROWS, K_PASS, dy_grouped[0], 0, nc.vector.tensor_copy)
-        dy_q0 = quantize("dy0", dy_grouped[0][:], E5M2)
-        factor_cols = sbuf("factor_cols", [P, ROW_PASSES, PACK], F32)
-        nc.gpsimd.tensor_tensor(factor_cols[:], us_cols, wt_cols, MULT)
-        row_factor = []
-        for g in range(ROW_PASSES):
-            spread = quarters(banks[1 + g])
+        v2_rows = [sbuf("v2_rows%d" % g, [P, SLOTS * PACK], BF16) for g in range(ROW_PASSES)]
+        v2_rows_mx = [mx_tiles("v2_rows%d" % g, SLOTS) for g in range(ROW_PASSES)]
+        dy_mx = [mx_tiles("dy%d" % c, CHUNK) for c in range(CHUNKS)]
+        quantize(dy_mx[0], group_dy(0, nc.vector.tensor_copy, DY0_GROUPED)[:], E5M2)
+        x_raw2 = load_x(2, DY_RAW[0])
+
+        def chunk(c):
             for t in range(PACK):
-                nc.tensor.transpose(spread[:, t, :], factor_cols[:, g, t : t + 1].to_broadcast([P, P]), ident[:])
-            factor = sbuf("row_factor%d" % g, [P, K_PASS], F32, reuses=FIRST_DY + UNIT * g)
-            nc.scalar.copy(factor[:].rearrange("p (m t) -> p m t", t=PACK), spread.rearrange("p t m -> p m t"))
-            row_factor.append(factor)
-        second_window = zeroed_window(1, reuses="dy_grouped0")
-        group_dy(dy_raw1a, 0, K_PASS // 2, dy_grouped[1], 0, nc.scalar.copy)
-        group_dy(dy_raw1b, 0, K_PASS // 2, dy_grouped[1], K_PASS // 2, nc.scalar.copy)
-        first_product(0, dy_q0, into=(3, 4, 5, 6))
-        dy_q1 = quantize("dy1", dy_grouped[1][:], E5M2)
-        a_low = sbuf("a_low", [P, 2 * SLOTS], BF16)
-        gather_a(a_pool0, a_low[:, 0:SLOTS])
-        x_rounded1 = round_x(1, x_raw1, reuses=FIRST_A, on_gpsimd=True)
-        x_rounded2 = round_x(2, x_raw2, reuses=FIRST_A + UNIT, on_gpsimd=True)
-        first_product(1, dy_q1, into=(7, 0, 1, 2))
+                if t == 2 and c + 1 < CHUNKS:
+                    at = DY3_GROUPED if c + 2 == CHUNKS else None
+                    quantize(dy_mx[c + 1], group_dy(c + 1, nc.scalar.copy, at)[:], E5M2)
+                first_product(c, t, dy_mx[c])
 
-        v2_rows0 = group_v2_rows(0, into=(3, 5))
-        x_grouped0 = group_x(0, round_x(0, x_raw0), into=4)
-        v2_slots = [sbuf("v2_slots0", [P, K_PASS * PACK], BF16, reuses=V2_GROUPED + 2 * UNIT)]
-        v2_rows1 = group_v2_rows(1, into=(7, 1), reuses=V2_GROUPED)
-        group_v2_slots(0, 0, v2_slots[0])
-        group_v2_slots(0, 1, v2_slots[0])
-        v2_rows_q = [quantize("v2_rows0", v2_rows0[:], E5M2)]
-        x_q0 = quantize("x0", x_grouped0[:], E4M3)
-        v2_rows_q.append(quantize("v2_rows1", v2_rows1[:], E5M2))
-        v2_slots_q = [quantize("v2_slots0", v2_slots[0][:], E5M2, reuses="v2_rows0")]
-        windows = [zeroed_window(0, reuses=V2_GROUPED), second_window]
-        a_high = sbuf("a_high", [P, 2 * SLOTS], BF16, reuses=A_HIGH)
-        gather_a(a_pool1, a_low[:, SLOTS:])
-        gather_a(a_pool2, a_high[:, 0:SLOTS])
-        gather_a(a_pool3, a_high[:, SLOTS:])
-        a_slots = sbuf("a_slots", [P, D * PACK], BF16, reuses=A_SLOTS)
-        turn_pairs(a_high[:, SLOTS:], a_slots[:, 3 * K_PASS :], into=7)
-        x_grouped12 = sbuf("x_grouped12", [P, 2 * R], BF16)
-        turn_pairs(x_rounded1[:], x_grouped12[:, 0:R], into=0)
-        turn_pairs(x_rounded2[:], x_grouped12[:, R:], into=4)
-        v2_slots.append(sbuf("v2_slots1", [P, K_PASS * PACK], BF16, reuses="x_grouped0"))
-        group_v2_slots(1, 0, v2_slots[1])
-        group_v2_slots(1, 1, v2_slots[1])
-        turn_pairs(a_high[:, 0:SLOTS], a_slots[:, 2 * K_PASS : 3 * K_PASS], into=5)
-        turn_pairs(a_low[:], a_slots[:, 0 : 2 * K_PASS], into=3)
-        x_q12 = quantize("x12", x_grouped12[:], E4M3, reuses=LAST_A + 2 * UNIT)
-        v2_slots_q.append(quantize("v2_slots1", v2_slots[1][:], E5M2, reuses=LAST_A + UNIT))
-        a_q = quantize("a", a_slots[:], E4M3)
+        for c in range(3):
+            chunk(c)
+        a_pool0 = load_a(0, DY_RAW[1])
+        a_pool1 = load_a(1, DY_RAW[2] - 4 * KIB)
+        a_pool2 = load_a(2, DY_RAW[3])
+        turn_v2(0, 0, 2, 4)
+        turn_v2(0, 2, 4, 5)
+        x_rounded0 = round_x(0, x_raw0, nc.scalar.copy)
+        x_rounded1 = round_x(1, x_raw1, round_on_gpsimd, at=DY3_GROUPED)
+        chunk(3)
+        x_raw3 = load_x(3, BT_WORDS)
+        a_pool3 = load_a(3, BT_WORDS + 4 * KIB)
+        x_grouped = [sbuf("x_grouped%d" % j, [P, R], BF16, at=X2_GROUPED if j == 2 else None) for j in range(PACK)]
+        x_mx = [mx_tiles("x%d" % j, R // PACK) for j in range(PACK)]
+        turn_x(x_rounded0, x_grouped[0][:], 6, nc.scalar.copy)
+        turn_v2(1, 0, 2, 7)
+        turn_v2(1, 2, 3, 4)
+        turn_v2(1, 3, 4, 5)
+        turn_x(x_rounded1, x_grouped[1][:], 6, nc.scalar.copy)
+        quantize_v2_rows(0, 0, 4)
+        x_rounded2 = round_x(2, x_raw2, nc.vector.tensor_copy)
+        quantize(x_mx[0], x_grouped[0][:], E4M3)
+        quantize_v2_rows(1, 0, 2)
+        quantize_v2_rows(1, 2, 4)
+        turn_x(x_rounded2, x_grouped[2][:], 7, nc.scalar.copy)
+        quantize(x_mx[1], x_grouped[1][:], E4M3)
+        da_sb0 = fetch(0, second_product(x_mx[0], 0, 0), nc.scalar.copy)
+        a_low = sbuf("a_low", [P, 2 * SLOTS], BF16, at=A_LOW)
+        a_high = sbuf("a_high", [P, 2 * SLOTS], BF16)
+        quantize(x_mx[2], x_grouped[2][:], E4M3)
+        nc.vector.tensor_copy(a_low[:, 0:SLOTS], a_pool0[:].indirect(offsets[:]))
+        nc.vector.tensor_copy(a_low[:, SLOTS:], a_pool1[:].indirect(offsets[:]))
 
-        scatter(0, fetch(0, second_product(x_q0, v2_rows_q, into=6), reuses=BELOW_A_HIGH))
-        windows.append(zeroed_window(2, reuses=A_SLOTS + UNIT))
-        da1 = second_product(x_q12, v2_rows_q, into=2)
-        x_rounded3 = round_x(3, x_raw3, reuses=ABOVE_A_HIGH)
+        v2_slots = sbuf("v2_slots", [P, R * PACK], BF16, at=V2_SLOTS)
+        for g in range(ROW_PASSES):
+            to = v2_slots[:].rearrange("p (g u e m t) -> p g u e m t", g=ROW_PASSES, u=2, e=2, t=PACK)
+            src = v2_tiles[g][:].rearrange("p (t u m e) -> p u e m t", t=PACK, u=2, e=2)
+            for u in range(2):
+                if (g, u) == (1, 1):
+                    x_rounded3 = round_x(3, x_raw3, round_on_gpsimd)
+                round_on_gpsimd(to[:, g, u], src[:, u])
+
+        da_sb1 = fetch(1, second_product(x_mx[1], 0, 1), nc.vector.tensor_copy)
+        a_slots = sbuf("a_slots", [P, D * PACK], BF16)
+        da2 = second_product(x_mx[2], 0, 2)
+        scatter_on_scalar(window0, da_sb0)
+        store_window(0, window0, nc.scalar)
+        nc.vector.tensor_copy(window1[:].indirect(offsets[:]), da_sb1[:])
+        store_window(1, window1, nc.sync)
+        da_sb2 = fetch(2, da2, nc.scalar.copy)
+        turn_a(a_low, a_slots[:, 0 : 2 * K_PASS], 3)
+        nc.vector.tensor_copy(a_high[:, 0:SLOTS], a_pool2[:].indirect(offsets[:]))
+        nc.vector.tensor_copy(a_high[:, SLOTS:], a_pool3[:].indirect(offsets[:]))
+        scatter_on_scalar(window2, da_sb2, lambda: turn_x(x_rounded3, x_grouped[3][:], 5, nc.scalar.copy))
+        store_window(2, window2, nc.scalar)
+        turn_a(a_high, a_slots[:, 2 * K_PASS :], 4)
+        v2_slots_mx = mx_tiles("v2_slots", R)
+        quantize(x_mx[3], x_grouped[3][:], E4M3)
+        quantize(v2_slots_mx, v2_slots[:], E5M2)
+        da3 = second_product(x_mx[3], 0, 6)
+        a_mx = mx_tiles("a", D)
+        quantize(a_mx, a_slots[:], E4M3)
+
+        da_sb3 = fetch(3, da3, nc.scalar.copy)
         dx = sbuf("dx", [P, R // P, D], F32)
-        third_product(0, v2_slots_q, a_q, (5,), dx[:, 0:1])
-        third_product(1, v2_slots_q, a_q, (7,), dx[:, 1:2])
-        scatter(1, fetch(1, da1, reuses=A_SLOTS))
-        third_product(2, v2_slots_q, a_q, (3, 4), dx[:, 2:4])
-        third_product(4, v2_slots_q, a_q, (6,), dx[:, 4:5])
-        x_q3 = quantize("x3", group_x(3, x_rounded3, into=1)[:], E4M3, reuses=BELOW_A_HIGH)
-        scatter(2, fetch(2, second_product(x_q12, v2_rows_q, into=5, first=2 * P), reuses=ABOVE_A_HIGH))
-        third_product(5, v2_slots_q, a_q, (0, 7, 3), dx[:, 5:8])
-        scatter(3, fetch(3, second_product(x_q3, v2_rows_q, into=7)))
+        for n in range(R // P):
+            acc = banks[(7, 0, 1, 2)[n % 4]]
+            cols = slice(n * P, (n + 1) * P)
+            nc.tensor.matmul_mx(
+                out=acc[:], lhsT=v2_slots_mx[0][:, cols].bitcast(E5M2), lhsT_scale=v2_slots_mx[1][:, cols],
+                rhs=a_mx[0][:].bitcast(E4M3), rhs_scale=a_mx[1][:], start=True, stop=True,
+            )
+            (nc.scalar.copy if n == 1 else nc.vector.tensor_copy)(dx[:, n, :], acc[:])
+            if n % 2 == 1:
+                g, c = divmod(n - 1, PACK)
+                rows = out_1[g * K_PASS : (g + 1) * K_PASS, :].rearrange("(m n) d -> m n d", n=PACK)
+                nc.sync.dma_start(rows[:, c : c + 2, :], dx[:, n - 1 : n + 1, :])
+        scatter_on_scalar(window0, da_sb3)
+        store_window(3, window0, nc.scalar)

@@ -31,13 +31,21 @@ COPY = mybir.ActivationFunctionType.Copy
 
 KIB = 1024
 LAP = 64
-BT_WORDS = 0
-DY_RAW = (12 * KIB, 16 * KIB, 28 * KIB, 32 * KIB)
-WINDOW1 = 40 * KIB
-SCALES_LISTED = WINDOW1 + 8 * KIB - LAP
-DY0_GROUPED = SCALES_LISTED + SLOTS - LAP
-DY3_GROUPED = 54 * KIB
-X2_GROUPED = 60 * KIB
+X0_RAW = 0
+BT_WORDS = X0_RAW + 4 * KIB - LAP
+X1_RAW = BT_WORDS + LAP
+DY0_GROUPED = BT_WORDS + 8 * KIB - LAP
+WINDOW2 = DY0_GROUPED + 2 * KIB - LAP
+DY_RAW = (24 * KIB, 28 * KIB, 40 * KIB, 44 * KIB)
+ROW_FACTORS = 52 * KIB
+SCALES_LISTED = ROW_FACTORS + 4 * KIB - LAP
+SC_COLS = SCALES_LISTED + LAP
+BT_CODES = SCALES_LISTED + SLOTS - LAP
+DY1_GROUPED = 59 * KIB
+SCALES_DEALT = DY1_GROUPED + 2 * KIB - LAP
+DY2_GROUPED = SCALES_DEALT + SLOTS - LAP
+DA_SB1 = 64 * KIB
+X2_GROUPED = 68 * KIB
 A_LOW = X2_GROUPED - 2 * KIB + LAP
 V2_SLOTS = X2_GROUPED + 2 * KIB - LAP
 
@@ -112,11 +120,11 @@ def tile_attend_glora_ax_kernel(
             return window
 
         window0 = zeroed_window(0, nc.vector)
-        window2 = zeroed_window(2, nc.vector)
+        window1 = zeroed_window(1, nc.vector)
 
         bt_scales_listed = sbuf("bt_scales_listed", [P, SLOTS], U8, at=SCALES_LISTED)
         nc.vector.tensor_copy(bt_scales_listed[:], bt_scale_pool[:].indirect(offsets[:]))
-        bt_scales_dealt = sbuf("bt_scales_dealt", [P, SLOTS], U8)
+        bt_scales_dealt = sbuf("bt_scales_dealt", [P, SLOTS], U8, at=SCALES_DEALT)
         nc.vector.tensor_copy(
             bt_scales_dealt[:].rearrange("p (t m) -> p t m", t=PACK),
             bt_scales_listed[:].rearrange("p (m t) -> p t m", t=PACK),
@@ -131,31 +139,28 @@ def tile_attend_glora_ax_kernel(
             )
         factor_cols = sbuf("factor_cols", [P, ROW_PASSES, PACK], F32)
         nc.gpsimd.tensor_tensor(factor_cols[:], us_cols, wt_cols, MULT)
-        window1 = zeroed_window(1, nc.gpsimd, at=WINDOW1)
 
         sc_turned = quarters(banks[4])
         for t in range(PACK):
             nc.tensor.transpose(sc_turned[:, t, :], sc_row[:, t:SLOTS:PACK], ident[:])
-        sc_cols = sbuf("sc_cols", [P, PACK], F32)
+        sc_cols = sbuf("sc_cols", [P, PACK], F32, at=SC_COLS)
         nc.scalar.copy(sc_cols[:], sc_turned[:, :, P - 1])
 
-        bt_codes = sbuf("bt_codes", [P, SLOTS], U32)
+        bt_codes = sbuf("bt_codes", [P, SLOTS], U32, at=BT_CODES)
         nc.vector.tensor_copy(
             bt_codes[:].rearrange("p (t m) -> p m t", t=PACK), bt_word_pool[:].bitcast(U32).indirect(offsets[:])
         )
-        x_raw0 = load_x(0, BT_WORDS)
-        x_raw1 = load_x(1, BT_WORDS + 4 * KIB)
+        x_raw0 = load_x(0, X0_RAW)
+        x_raw1 = load_x(1, X1_RAW)
 
-        row_factor = []
+        row_factor = sbuf("row_factor", [P, ROW_PASSES, K_PASS], F32, at=ROW_FACTORS)
         for g in range(ROW_PASSES):
             spread = quarters(banks[5 + g])
             for t in range(PACK):
                 nc.tensor.transpose(spread[:, t, :], factor_cols[:, g, t : t + 1].to_broadcast([P, P]), ident[:])
-            factor = sbuf("row_factor%d" % g, [P, K_PASS], F32)
             nc.scalar.copy(
-                factor[:].rearrange("p (u m e) -> p u m e", u=2, e=2), spread.rearrange("p (u e) m -> p u m e", u=2)
+                row_factor[:, g, :].rearrange("p (u m e) -> p u m e", u=2, e=2), spread.rearrange("p (u e) m -> p u m e", u=2)
             )
-            row_factor.append(factor)
 
         def group_dy(c, copy, at=None):
             grouped = sbuf("dy_grouped%d" % c, [P, CHUNK * PACK], BF16, at)
@@ -183,7 +188,7 @@ def tile_attend_glora_ax_kernel(
                 v2_tiles[g][:].rearrange("p (t u n) -> p t u n", t=PACK, u=2)[:, t, :, rows],
                 v.rearrange("p (u n) -> p u n", u=2),
                 sc_cols[:, t : t + 1],
-                row_factor[g][:].rearrange("p (u n) -> p u n", u=2)[:, :, rows],
+                row_factor[:, g, :].rearrange("p (u n) -> p u n", u=2)[:, :, rows],
                 MULT, MULT,
             )
 
@@ -231,8 +236,8 @@ def tile_attend_glora_ax_kernel(
                 )
             return da
 
-        def fetch(j, da, copy):
-            da_sb = sbuf("da_sb%d" % j, [P, SLOTS], F32)
+        def fetch(j, da, copy, at=None):
+            da_sb = sbuf("da_sb%d" % j, [P, SLOTS], F32, at)
             copy(da_sb[:].rearrange("p (m t) -> p m t", t=PACK), quarters(da).rearrange("p t m -> p m t"))
             return da_sb
 
@@ -251,12 +256,13 @@ def tile_attend_glora_ax_kernel(
         v2_rows_mx = [mx_tiles("v2_rows%d" % g, SLOTS) for g in range(ROW_PASSES)]
         dy_mx = [mx_tiles("dy%d" % c, CHUNK) for c in range(CHUNKS)]
         quantize(dy_mx[0], group_dy(0, nc.vector.tensor_copy, DY0_GROUPED)[:], E5M2)
+        window2 = zeroed_window(2, nc.vector, at=WINDOW2)
         x_raw2 = load_x(2, DY_RAW[0])
 
         def chunk(c):
             for t in range(PACK):
                 if t == 2 and c + 1 < CHUNKS:
-                    at = DY3_GROUPED if c + 2 == CHUNKS else None
+                    at = (DY1_GROUPED, DY2_GROUPED, DY1_GROUPED)[c]
                     quantize(dy_mx[c + 1], group_dy(c + 1, nc.scalar.copy, at)[:], E5M2)
                 first_product(c, t, dy_mx[c])
 
@@ -267,11 +273,11 @@ def tile_attend_glora_ax_kernel(
         a_pool2 = load_a(2, DY_RAW[3])
         turn_v2(0, 0, 2, 4)
         turn_v2(0, 2, 4, 5)
-        x_rounded0 = round_x(0, x_raw0, nc.scalar.copy)
-        x_rounded1 = round_x(1, x_raw1, round_on_gpsimd, at=DY3_GROUPED)
+        x_rounded0 = round_x(0, x_raw0, nc.scalar.copy, at=DY2_GROUPED)
+        x_rounded1 = round_x(1, x_raw1, round_on_gpsimd, at=DY1_GROUPED)
         chunk(3)
-        x_raw3 = load_x(3, BT_WORDS)
-        a_pool3 = load_a(3, BT_WORDS + 4 * KIB)
+        x_raw3 = load_x(3, X0_RAW)
+        a_pool3 = load_a(3, X1_RAW)
         x_grouped = [sbuf("x_grouped%d" % j, [P, R], BF16, at=X2_GROUPED if j == 2 else None) for j in range(PACK)]
         x_mx = [mx_tiles("x%d" % j, R // PACK) for j in range(PACK)]
         turn_x(x_rounded0, x_grouped[0][:], 6, nc.scalar.copy)
@@ -280,7 +286,7 @@ def tile_attend_glora_ax_kernel(
         turn_v2(1, 3, 4, 5)
         turn_x(x_rounded1, x_grouped[1][:], 6, nc.scalar.copy)
         quantize_v2_rows(0, 0, 4)
-        x_rounded2 = round_x(2, x_raw2, nc.vector.tensor_copy)
+        x_rounded2 = round_x(2, x_raw2, nc.vector.tensor_copy, at=ROW_FACTORS)
         quantize(x_mx[0], x_grouped[0][:], E4M3)
         quantize_v2_rows(1, 0, 2)
         quantize_v2_rows(1, 2, 4)
@@ -288,10 +294,9 @@ def tile_attend_glora_ax_kernel(
         quantize(x_mx[1], x_grouped[1][:], E4M3)
         da_sb0 = fetch(0, second_product(x_mx[0], 0, 0), nc.scalar.copy)
         a_low = sbuf("a_low", [P, 2 * SLOTS], BF16, at=A_LOW)
-        a_high = sbuf("a_high", [P, 2 * SLOTS], BF16)
+        a_high = sbuf("a_high", [P, 2 * SLOTS], BF16, at=DA_SB1)
         quantize(x_mx[2], x_grouped[2][:], E4M3)
         nc.vector.tensor_copy(a_low[:, 0:SLOTS], a_pool0[:].indirect(offsets[:]))
-        nc.vector.tensor_copy(a_low[:, SLOTS:], a_pool1[:].indirect(offsets[:]))
 
         v2_slots = sbuf("v2_slots", [P, R * PACK], BF16, at=V2_SLOTS)
         for g in range(ROW_PASSES):
@@ -299,10 +304,11 @@ def tile_attend_glora_ax_kernel(
             src = v2_tiles[g][:].rearrange("p (t u m e) -> p u e m t", t=PACK, u=2, e=2)
             for u in range(2):
                 if (g, u) == (1, 1):
-                    x_rounded3 = round_x(3, x_raw3, round_on_gpsimd)
+                    x_rounded3 = round_x(3, x_raw3, round_on_gpsimd, at=DY_RAW[1])
                 round_on_gpsimd(to[:, g, u], src[:, u])
 
-        da_sb1 = fetch(1, second_product(x_mx[1], 0, 1), nc.vector.tensor_copy)
+        da_sb1 = fetch(1, second_product(x_mx[1], 0, 1), nc.vector.tensor_copy, at=DA_SB1)
+        nc.vector.tensor_copy(a_low[:, SLOTS:], a_pool1[:].indirect(offsets[:]))
         a_slots = sbuf("a_slots", [P, D * PACK], BF16)
         da2 = second_product(x_mx[2], 0, 2)
         scatter_on_scalar(window0, da_sb0)

@@ -1,7 +1,6 @@
 from contextlib import ExitStack
 
 import concourse.mybir as mybir
-from concourse.masks import make_identity
 
 D, E, R, SLOTS, T = 512, 512, 1024, 512, 2048
 FLOPS = 2 * (E * R * SLOTS + R * D * SLOTS + SLOTS * R * D)
@@ -29,25 +28,43 @@ CHUNKS = 4
 CHUNK = R // CHUNKS
 COPY = mybir.ActivationFunctionType.Copy
 
+HALF = SLOTS // 2
 KIB = 1024
 LAP = 64
-X0_RAW = 0
-BT_WORDS = X0_RAW + 4 * KIB - LAP
-X1_RAW = BT_WORDS + LAP
-DY0_GROUPED = BT_WORDS + 8 * KIB - LAP
-WINDOW2 = DY0_GROUPED + 2 * KIB - LAP
-DY_RAW = (24 * KIB, 28 * KIB, 40 * KIB, 44 * KIB)
-ROW_FACTORS = 52 * KIB
-SCALES_LISTED = ROW_FACTORS + 4 * KIB - LAP
-SC_COLS = SCALES_LISTED + LAP
-BT_CODES = SCALES_LISTED + SLOTS - LAP
-DY1_GROUPED = 59 * KIB
-SCALES_DEALT = DY1_GROUPED + 2 * KIB - LAP
-DY2_GROUPED = SCALES_DEALT + SLOTS - LAP
-DA_SB1 = 64 * KIB
-X2_GROUPED = 68 * KIB
-A_LOW = X2_GROUPED - 2 * KIB + LAP
-V2_SLOTS = X2_GROUPED + 2 * KIB - LAP
+
+RUNS = (
+    (("ones", 4 * P), ("window0", 8 * KIB)),
+    (("a_pool2", 8 * KIB), ("x_raw0", 4 * KIB), ("bt_word_pool", 8 * KIB), ("row_factor", 4 * KIB), ("a_pool3", 8 * KIB),
+     ("a_codes", 2 * KIB)),
+    (("dy_raw0", 4 * KIB), ("x_raw2", 4 * KIB), ("v2_rows0_codes", 2 * KIB)),
+    (("v2_rows1", 4 * KIB), ("x1_codes", KIB)),
+    (("a_slots0", 2 * KIB), ("da_sb2_0", KIB), ("da_sb0", 2 * KIB), ("da_sb2_1", KIB), ("x_grouped3", 2 * KIB)),
+    (("dy_raw1", 4 * KIB), ("a_pool0", 8 * KIB)),
+    (("dy_raw2", 4 * KIB), ("a_pool1", 8 * KIB)),
+    (("dy_raw3", 4 * KIB), ("x_raw3", 4 * KIB)),
+    (("window1", 8 * KIB), ("bt_scale_pool", T), ("bt_codes", 2 * KIB)),
+    (("spare", 2 * KIB + LAP), ("x_rounded1", 2 * KIB), ("dy_grouped3", 2 * KIB), ("dy_grouped1", 2 * KIB), ("bt_scales_dealt", SLOTS),
+     ("dy_grouped2", 2 * KIB), ("x_rounded0", 2 * KIB)),
+    (("window2", 8 * KIB), ("x_grouped2", 2 * KIB), ("a_listed1", KIB)),
+    (("x2_codes", KIB), ("v2_slots0", 4 * KIB)),
+    (("x2_scales", 2 * P), ("v2_slots1", 2 * KIB)),
+    (("a_listed2", KIB), ("da_sb1", 2 * KIB), ("a_listed3", KIB)),
+    (("a_slots1", 2 * KIB), ("x3_codes", KIB)),
+)
+INSIDE = (("a_listed0", "x_rounded1", -2 * KIB), ("v2_slots2", "a_pool3", KIB), ("v2_slots_codes", "a_pool3", 3 * KIB), ("x_rounded2", "x_rounded1", -2 * KIB), ("x_raw1", "bt_word_pool", LAP), ("factor_cols", "bt_scale_pool", 2 * LAP))
+
+
+def placement():
+    at = {}
+    top = 0
+    for run in RUNS:
+        for name, size in run:
+            at[name] = top
+            top = top + size - LAP
+        top = top + LAP
+    for name, host, offset in INSIDE:
+        at[name] = at[host] + offset
+    return at
 
 
 def tile_attend_glora_ax_kernel(
@@ -63,10 +80,12 @@ def tile_attend_glora_ax_kernel(
         def quarters(bank):
             return bank[:].rearrange("p (c m) -> p c m", c=PACK)
 
-        def sbuf(name, shape, dtype, at=None):
-            if at is None:
+        at = placement()
+
+        def sbuf(name, shape, dtype):
+            if name not in at:
                 return keep.tile(shape, dtype, name=name, align_bytes=64)
-            return placed.tile(shape, dtype, name=name, align_bytes=64, offset=at)
+            return placed.tile(shape, dtype, name=name, align_bytes=64, offset=at[name])
 
         def mx_tiles(name, width):
             return sbuf(name + "_codes", [P, width], U32), sbuf(name + "_scales", [P, width], U8)
@@ -88,87 +107,91 @@ def tile_attend_glora_ax_kernel(
         wt_cols = wt_tile[:, :, 0:PACK]
         nc.scalar.dma_start(us_cols, us.rearrange("(g p t) o -> p g (t o)", g=ROW_PASSES, t=PACK))
         nc.scalar.dma_start(wt_cols, wt.rearrange("(g p t) o -> p g (t o)", g=ROW_PASSES, t=PACK))
+        ones = sbuf("ones", [P, P], F32)
+        nc.gpsimd.memset(ones[:], 1.0)
+        ident = sbuf("ident", [P, P], F32)
+        nc.gpsimd.affine_select(
+            out=ident[:], in_=ones[:], pattern=[[-1, P]], compare_op=mybir.AluOpType.is_equal, fill=0.0, base=0,
+            channel_multiplier=1,
+        )
         sc_pool = sbuf("sc_pool", [P, T], F32)
-        nc.vector.memset(sc_pool[0 : P - 1, :].bitcast(I32), 0)
+        nc.gpsimd.memset(sc_pool[0 : P - 1, :].bitcast(I32), 0)
         nc.sync.dma_start(sc_pool[P - 1 : P, :], sc[P - 1 : P, :])
-        bt_word_pool = sbuf("bt_word_pool", [P, T], I32, at=BT_WORDS)
+        bt_word_pool = sbuf("bt_word_pool", [P, T], I32)
         nc.sync.dma_start(bt_word_pool[:], Bt_words[0].rearrange("p n t -> p (n t)").bitcast(I32))
 
         def load_dy(c):
-            raw = sbuf("dy_raw%d" % c, [P, PACK, CHUNK], F32, DY_RAW[c])
+            raw = sbuf("dy_raw%d" % c, [P, PACK, CHUNK], F32)
             nc.sync.dma_start(raw[:], dyT[:, c * CHUNK : (c + 1) * CHUNK].rearrange("(p j) r -> p j r", j=PACK))
             return raw
 
-        def load_x(j, at):
-            raw = sbuf("x_raw%d" % j, [P, R], F32, at)
+        def load_x(j):
+            raw = sbuf("x_raw%d" % j, [P, R], F32)
             nc.sync.dma_start(raw[:], xT[j * P : (j + 1) * P, :])
             return raw
 
-        def load_a(j, at):
-            pool = sbuf("a_pool%d" % j, [P, T], F32, at)
+        def load_a(j):
+            pool = sbuf("a_pool%d" % j, [P, T], F32)
             nc.sync.dma_start(pool[:], A[j * P : (j + 1) * P, :])
             return pool
 
         dy_raw = [load_dy(c) for c in range(CHUNKS)]
 
-        ident = sbuf("ident", [P, P], F32)
-        make_identity(nc, ident[:])
 
-        def zeroed_window(n, engine, at=None):
-            window = sbuf("window%d" % n, [P, T], F32, at)
+        def zeroed_window(n, engine):
+            window = sbuf("window%d" % n, [P, T], F32)
             engine.memset(window[:].bitcast(I32), 0)
             return window
 
-        window0 = zeroed_window(0, nc.vector)
-        window1 = zeroed_window(1, nc.vector)
+        window0 = zeroed_window(0, nc.gpsimd)
 
-        bt_scales_listed = sbuf("bt_scales_listed", [P, SLOTS], U8, at=SCALES_LISTED)
-        nc.vector.tensor_copy(bt_scales_listed[:], bt_scale_pool[:].indirect(offsets[:]))
-        bt_scales_dealt = sbuf("bt_scales_dealt", [P, SLOTS], U8, at=SCALES_DEALT)
+        bt_scales_dealt = sbuf("bt_scales_dealt", [P, SLOTS], U8)
         nc.vector.tensor_copy(
-            bt_scales_dealt[:].rearrange("p (t m) -> p t m", t=PACK),
-            bt_scales_listed[:].rearrange("p (m t) -> p t m", t=PACK),
+            bt_scales_dealt[:].rearrange("p (t m) -> p m t", t=PACK), bt_scale_pool[:].indirect(offsets[:])
         )
         sc_row = sbuf("sc_row", [P, SLOTS], F32)
-        nc.scalar.activation(sc_row[:], sc_pool[:].indirect(offsets[:]), COPY)
+        nc.vector.tensor_copy(sc_row[:], sc_pool[:].indirect(offsets[:]))
         for q in range(P // QUADRANT):
             first = P - SCALE_ROWS + PACK * q
             nc.scalar.dma_start(
                 bt_scales[QUADRANT * q : QUADRANT * q + PACK, :].bitcast(I32),
                 bt_scales_dealt[first : first + PACK, :].bitcast(I32),
             )
+        window1 = zeroed_window(1, nc.gpsimd)
         factor_cols = sbuf("factor_cols", [P, ROW_PASSES, PACK], F32)
-        nc.gpsimd.tensor_tensor(factor_cols[:], us_cols, wt_cols, MULT)
+        nc.vector.tensor_tensor(factor_cols[:], us_cols, wt_cols, MULT)
 
         sc_turned = quarters(banks[4])
         for t in range(PACK):
             nc.tensor.transpose(sc_turned[:, t, :], sc_row[:, t:SLOTS:PACK], ident[:])
-        sc_cols = sbuf("sc_cols", [P, PACK], F32, at=SC_COLS)
-        nc.scalar.copy(sc_cols[:], sc_turned[:, :, P - 1])
 
-        bt_codes = sbuf("bt_codes", [P, SLOTS], U32, at=BT_CODES)
+        bt_codes = sbuf("bt_codes", [P, SLOTS], U32)
         nc.vector.tensor_copy(
             bt_codes[:].rearrange("p (t m) -> p m t", t=PACK), bt_word_pool[:].bitcast(U32).indirect(offsets[:])
         )
-        x_raw0 = load_x(0, X0_RAW)
-        x_raw1 = load_x(1, X1_RAW)
+        x_raw0 = load_x(0)
+        x_raw1 = load_x(1)
 
-        row_factor = sbuf("row_factor", [P, ROW_PASSES, K_PASS], F32, at=ROW_FACTORS)
+        row_factor = sbuf("row_factor", [P, ROW_PASSES, K_PASS], F32)
         for g in range(ROW_PASSES):
             spread = quarters(banks[5 + g])
             for t in range(PACK):
                 nc.tensor.transpose(spread[:, t, :], factor_cols[:, g, t : t + 1].to_broadcast([P, P]), ident[:])
-            nc.scalar.copy(
+            nc.vector.tensor_copy(
                 row_factor[:, g, :].rearrange("p (u m e) -> p u m e", u=2, e=2), spread.rearrange("p (u e) m -> p u m e", u=2)
             )
 
-        def group_dy(c, copy, at=None):
-            grouped = sbuf("dy_grouped%d" % c, [P, CHUNK * PACK], BF16, at)
+        def group_dy(c, copy):
+            grouped = sbuf("dy_grouped%d" % c, [P, CHUNK * PACK], BF16)
             copy(
                 grouped[:].rearrange("p (u m e j) -> p m j u e", u=2, e=2, j=PACK),
                 dy_raw[c][:].rearrange("p j (m u e) -> p m j u e", u=2, e=2),
             )
             return grouped
+
+        def activation_copy(out, in_):
+            for u in range(2):
+                nc.scalar.activation(out[:, :, :, u, :], in_[:, :, :, u, :], COPY)
 
         def round_on_gpsimd(out, in_):
             nc.gpsimd.tensor_scalar(out, in_, 1.0, 0.0, MULT, ADD)
@@ -192,13 +215,19 @@ def tile_attend_glora_ax_kernel(
                 MULT, MULT,
             )
 
-        def turn(words, grouped, into, copy):
-            count = len(words)
-            bank = banks[into][:, 0 : count * 2 * P].rearrange("p (b u m) -> p b u m", b=count, u=2)
-            for b in range(count):
+        def turn_start(words, into):
+            for b in range(len(words)):
                 for u in range(2):
-                    nc.tensor.transpose(bank[:, b, u, :], words[b][u], ident[:])
-            copy(grouped.bitcast(F32).rearrange("p (b m u) -> p b m u", b=count, u=2), bank.rearrange("p b u m -> p b m u"))
+                    nc.tensor.transpose(quarters(banks[into])[:, 2 * b + u, :], words[b][u], ident[:])
+
+        def turn_finish(grouped, into, copy):
+            count = grouped.shape[1] // K_PASS
+            bank = banks[into][:, 0 : count * 2 * P].rearrange("p (b u m) -> p b m u", b=count, u=2)
+            copy(grouped.bitcast(F32).rearrange("p (b m u) -> p b m u", b=count, u=2), bank)
+
+        def turn(words, grouped, into, copy):
+            turn_start(words, into)
+            turn_finish(grouped, into, copy)
 
         def turn_v2(g, t0, t1, into):
             words = v2_tiles[g][:].bitcast(F32).rearrange("p (t u m) -> p t u m", t=PACK, u=2)
@@ -210,8 +239,8 @@ def tile_attend_glora_ax_kernel(
         def quantize_v2_rows(g, t0, t1):
             quantize(v2_rows_mx[g], v2_rows[g][:, t0 * K_PASS : t1 * K_PASS], E5M2, first=t0 * P)
 
-        def round_x(j, raw, rounder, at=None):
-            rounded = sbuf("x_rounded%d" % j, [P, R], BF16, at)
+        def round_x(j, raw, rounder):
+            rounded = sbuf("x_rounded%d" % j, [P, R], BF16)
             rounder(
                 rounded[:].rearrange("p (u m e) -> p u m e", u=2, e=2), raw[:].rearrange("p (m u e) -> p u m e", u=2, e=2)
             )
@@ -221,9 +250,31 @@ def tile_attend_glora_ax_kernel(
             words = rounded[:].bitcast(F32).rearrange("p (u g m) -> p g u m", u=2, g=ROW_PASSES)
             turn([[words[:, g, u, :] for u in range(2)] for g in range(ROW_PASSES)], grouped, into, copy)
 
-        def turn_a(listed, grouped, into):
-            words = listed[:].bitcast(F32).rearrange("p (b m u) -> p b u m", b=2, u=2)
-            turn([[words[:, b, u, :] for u in range(2)] for b in range(2)], grouped, into, nc.scalar.copy)
+        def turn_x_whole(raw, into):
+            for g in range(ROW_PASSES):
+                for t in range(PACK):
+                    nc.tensor.transpose(
+                        quarters(banks[into[g]])[:, t, :], raw[:, g * K_PASS + t : (g + 1) * K_PASS : PACK], ident[:]
+                    )
+
+        def round_x_turned(grouped, into):
+            for g in range(ROW_PASSES):
+                nc.scalar.copy(
+                    grouped[:, g * K_PASS : (g + 1) * K_PASS].rearrange("p (m t) -> p m t", t=PACK),
+                    quarters(banks[into[g]]).rearrange("p t m -> p m t"),
+                )
+
+        def gather_a(j, pool):
+            listed = sbuf("a_listed%d" % j, [P, SLOTS], BF16)
+            if j == 0:
+                nc.scalar.activation(listed[:], pool[:].indirect(offsets[:]), COPY)
+            else:
+                nc.vector.tensor_copy(listed[:], pool[:].indirect(offsets[:]))
+            return listed
+
+        def turn_a(pair, into):
+            words = [listed[:].bitcast(F32).rearrange("p (m u) -> p u m", u=2) for listed in pair]
+            turn_start([[words[b][:, u, :] for u in range(2)] for b in range(2)], into)
 
         def second_product(x_mx, first, into):
             da = banks[into]
@@ -236,18 +287,21 @@ def tile_attend_glora_ax_kernel(
                 )
             return da
 
-        def fetch(j, da, copy, at=None):
-            da_sb = sbuf("da_sb%d" % j, [P, SLOTS], F32, at)
-            copy(da_sb[:].rearrange("p (m t) -> p m t", t=PACK), quarters(da).rearrange("p t m -> p m t"))
+        def fetch(name, da, copy, h0=0, h1=2):
+            da_sb = sbuf(name, [P, (h1 - h0) * HALF], F32)
+            copy(
+                da_sb[:].rearrange("p (m t) -> p m t", t=PACK),
+                quarters(da).rearrange("p t m -> p m t")[:, h0 * HALF // PACK : h1 * HALF // PACK],
+            )
             return da_sb
 
-        def scatter_on_scalar(window, da_sb, between=None):
-            half = SLOTS // 2
+        def scatter_half(window, h, values):
+            listed = offsets[:, h * HALF // LIST_ROWS : (h + 1) * HALF // LIST_ROWS]
+            nc.scalar.activation(window[:].indirect(listed), values, COPY)
+
+        def scatter_on_scalar(window, da_sb):
             for h in range(2):
-                if h == 1 and between is not None:
-                    between()
-                listed = offsets[:, h * half // LIST_ROWS : (h + 1) * half // LIST_ROWS]
-                nc.scalar.activation(window[:].indirect(listed), da_sb[:, h * half : (h + 1) * half], COPY)
+                scatter_half(window, h, da_sb[:, h * HALF : (h + 1) * HALF])
 
         def store_window(j, window, queue):
             queue.dma_start(out_0[j * P : (j + 1) * P, :], window[:])
@@ -255,84 +309,91 @@ def tile_attend_glora_ax_kernel(
         v2_rows = [sbuf("v2_rows%d" % g, [P, SLOTS * PACK], BF16) for g in range(ROW_PASSES)]
         v2_rows_mx = [mx_tiles("v2_rows%d" % g, SLOTS) for g in range(ROW_PASSES)]
         dy_mx = [mx_tiles("dy%d" % c, CHUNK) for c in range(CHUNKS)]
-        quantize(dy_mx[0], group_dy(0, nc.vector.tensor_copy, DY0_GROUPED)[:], E5M2)
-        window2 = zeroed_window(2, nc.vector, at=WINDOW2)
-        x_raw2 = load_x(2, DY_RAW[0])
+        quantize(dy_mx[0], group_dy(0, activation_copy)[:], E5M2)
+        sc_cols = sbuf("sc_cols", [P, PACK], F32)
+        nc.vector.tensor_copy(sc_cols[:], sc_turned[:, :, P - 1])
+        x_raw2 = load_x(2)
 
         def chunk(c):
             for t in range(PACK):
                 if t == 2 and c + 1 < CHUNKS:
-                    at = (DY1_GROUPED, DY2_GROUPED, DY1_GROUPED)[c]
-                    quantize(dy_mx[c + 1], group_dy(c + 1, nc.scalar.copy, at)[:], E5M2)
+                    quantize(dy_mx[c + 1], group_dy(c + 1, nc.scalar.copy)[:], E5M2)
                 first_product(c, t, dy_mx[c])
 
         for c in range(3):
             chunk(c)
-        a_pool0 = load_a(0, DY_RAW[1])
-        a_pool1 = load_a(1, DY_RAW[2] - 4 * KIB)
-        a_pool2 = load_a(2, DY_RAW[3])
+        a_pool0 = load_a(0)
+        a_pool1 = load_a(1)
+        x_raw3 = load_x(3)
         turn_v2(0, 0, 2, 4)
         turn_v2(0, 2, 4, 5)
-        x_rounded0 = round_x(0, x_raw0, nc.scalar.copy, at=DY2_GROUPED)
-        x_rounded1 = round_x(1, x_raw1, round_on_gpsimd, at=DY1_GROUPED)
+        x_rounded0 = round_x(0, x_raw0, nc.scalar.copy)
+        x_rounded1 = round_x(1, x_raw1, round_on_gpsimd)
+        x_rounded2 = round_x(2, x_raw2, round_on_gpsimd)
         chunk(3)
-        x_raw3 = load_x(3, X0_RAW)
-        a_pool3 = load_a(3, X1_RAW)
-        x_grouped = [sbuf("x_grouped%d" % j, [P, R], BF16, at=X2_GROUPED if j == 2 else None) for j in range(PACK)]
+        a_pool2 = load_a(2)
+        x_grouped = [sbuf("x_grouped%d" % j, [P, R], BF16) for j in range(PACK)]
         x_mx = [mx_tiles("x%d" % j, R // PACK) for j in range(PACK)]
         turn_x(x_rounded0, x_grouped[0][:], 6, nc.scalar.copy)
-        turn_v2(1, 0, 2, 7)
-        turn_v2(1, 2, 3, 4)
-        turn_v2(1, 3, 4, 5)
-        turn_x(x_rounded1, x_grouped[1][:], 6, nc.scalar.copy)
+        turn_x(x_rounded1, x_grouped[1][:], 7, nc.vector.tensor_copy)
+        turn_v2(1, 0, 2, 4)
+        turn_v2(1, 2, 3, 5)
+        turn_v2(1, 3, 4, 6)
+        turn_x(x_rounded2, x_grouped[2][:], 2, nc.scalar.copy)
         quantize_v2_rows(0, 0, 4)
-        x_rounded2 = round_x(2, x_raw2, nc.vector.tensor_copy, at=ROW_FACTORS)
         quantize(x_mx[0], x_grouped[0][:], E4M3)
         quantize_v2_rows(1, 0, 2)
         quantize_v2_rows(1, 2, 4)
-        turn_x(x_rounded2, x_grouped[2][:], 7, nc.scalar.copy)
         quantize(x_mx[1], x_grouped[1][:], E4M3)
-        da_sb0 = fetch(0, second_product(x_mx[0], 0, 0), nc.scalar.copy)
-        a_low = sbuf("a_low", [P, 2 * SLOTS], BF16, at=A_LOW)
-        a_high = sbuf("a_high", [P, 2 * SLOTS], BF16, at=DA_SB1)
         quantize(x_mx[2], x_grouped[2][:], E4M3)
-        nc.vector.tensor_copy(a_low[:, 0:SLOTS], a_pool0[:].indirect(offsets[:]))
+        a_pool3 = load_a(3)
+        da0 = second_product(x_mx[0], 0, 0)
+        da1 = second_product(x_mx[1], 0, 1)
+        da2 = second_product(x_mx[2], 0, 6)
+        a_listed = [gather_a(0, a_pool0)]
+        da_sb0 = fetch("da_sb0", da0, nc.scalar.copy)
+        window2 = zeroed_window(2, nc.gpsimd)
 
-        v2_slots = sbuf("v2_slots", [P, R * PACK], BF16, at=V2_SLOTS)
-        for g in range(ROW_PASSES):
-            to = v2_slots[:].rearrange("p (g u e m t) -> p g u e m t", g=ROW_PASSES, u=2, e=2, t=PACK)
+        v2_slots = [sbuf("v2_slots%d" % n, [P, width], BF16) for n, width in enumerate((2 * R, R, R))]
+
+        def group_v2_slots(g, u, copy):
+            to = v2_slots[0][:, u * R : (u + 1) * R] if g == 0 else v2_slots[1 + u][:]
             src = v2_tiles[g][:].rearrange("p (t u m e) -> p u e m t", t=PACK, u=2, e=2)
-            for u in range(2):
-                if (g, u) == (1, 1):
-                    x_rounded3 = round_x(3, x_raw3, round_on_gpsimd, at=DY_RAW[1])
-                round_on_gpsimd(to[:, g, u], src[:, u])
+            copy(to.rearrange("p (e m t) -> p e m t", e=2, t=PACK), src[:, u])
 
-        da_sb1 = fetch(1, second_product(x_mx[1], 0, 1), nc.vector.tensor_copy, at=DA_SB1)
-        nc.vector.tensor_copy(a_low[:, SLOTS:], a_pool1[:].indirect(offsets[:]))
-        a_slots = sbuf("a_slots", [P, D * PACK], BF16)
-        da2 = second_product(x_mx[2], 0, 2)
+        for g, u in ((0, 0), (0, 1), (1, 0)):
+            group_v2_slots(g, u, round_on_gpsimd)
+        da_sb1 = fetch("da_sb1", da1, nc.vector.tensor_copy)
+        a_listed.append(gather_a(1, a_pool1))
+        turn_a(a_listed[0:2], 4)
+        turn_x_whole(x_raw3, (2, 3))
         scatter_on_scalar(window0, da_sb0)
         store_window(0, window0, nc.scalar)
         nc.vector.tensor_copy(window1[:].indirect(offsets[:]), da_sb1[:])
         store_window(1, window1, nc.sync)
-        da_sb2 = fetch(2, da2, nc.scalar.copy)
-        turn_a(a_low, a_slots[:, 0 : 2 * K_PASS], 3)
-        nc.vector.tensor_copy(a_high[:, 0:SLOTS], a_pool2[:].indirect(offsets[:]))
-        nc.vector.tensor_copy(a_high[:, SLOTS:], a_pool3[:].indirect(offsets[:]))
-        scatter_on_scalar(window2, da_sb2, lambda: turn_x(x_rounded3, x_grouped[3][:], 5, nc.scalar.copy))
+        da_sb2 = [fetch("da_sb2_%d" % h, da2, nc.scalar.copy, h, h + 1) for h in range(2)]
+        a_listed.append(gather_a(2, a_pool2))
+        a_listed.append(gather_a(3, a_pool3))
+        group_v2_slots(1, 1, nc.vector.tensor_copy)
+        a_slots = [sbuf("a_slots%d" % h, [P, 2 * K_PASS], BF16) for h in range(2)]
+        scatter_half(window2, 0, da_sb2[0][:])
+        turn_finish(a_slots[0][:], 4, nc.scalar.copy)
+        scatter_half(window2, 1, da_sb2[1][:])
         store_window(2, window2, nc.scalar)
-        turn_a(a_high, a_slots[:, 2 * K_PASS :], 4)
+        turn_a(a_listed[2:4], 5)
+        turn_finish(a_slots[1][:], 5, nc.vector.tensor_copy)
+        round_x_turned(x_grouped[3], (2, 3))
         v2_slots_mx = mx_tiles("v2_slots", R)
-        quantize(x_mx[3], x_grouped[3][:], E4M3)
-        quantize(v2_slots_mx, v2_slots[:], E5M2)
-        da3 = second_product(x_mx[3], 0, 6)
         a_mx = mx_tiles("a", D)
-        quantize(a_mx, a_slots[:], E4M3)
-
-        da_sb3 = fetch(3, da3, nc.scalar.copy)
+        quantize(a_mx, a_slots[0][:], E4M3)
+        quantize(v2_slots_mx, v2_slots[0][:], E5M2)
+        quantize(a_mx, a_slots[1][:], E4M3, 2 * P)
+        quantize(v2_slots_mx, v2_slots[1][:], E5M2, K_PASS)
+        quantize(v2_slots_mx, v2_slots[2][:], E5M2, K_PASS + CHUNK)
+        quantize(x_mx[3], x_grouped[3][:], E4M3)
         dx = sbuf("dx", [P, R // P, D], F32)
         for n in range(R // P):
-            acc = banks[(7, 0, 1, 2)[n % 4]]
+            acc = banks[(7, 0, 1, 4)[n % 4]]
             cols = slice(n * P, (n + 1) * P)
             nc.tensor.matmul_mx(
                 out=acc[:], lhsT=v2_slots_mx[0][:, cols].bitcast(E5M2), lhsT_scale=v2_slots_mx[1][:, cols],
@@ -343,5 +404,7 @@ def tile_attend_glora_ax_kernel(
                 g, c = divmod(n - 1, PACK)
                 rows = out_1[g * K_PASS : (g + 1) * K_PASS, :].rearrange("(m n) d -> m n d", n=PACK)
                 nc.sync.dma_start(rows[:, c : c + 2, :], dx[:, n - 1 : n + 1, :])
+            if n == 3:
+                da_sb3 = fetch("da_sb3", second_product(x_mx[3], 0, 6), nc.scalar.copy)
         scatter_on_scalar(window0, da_sb3)
         store_window(3, window0, nc.scalar)

@@ -24,34 +24,34 @@ BANKS = 8
 QUADRANT = 32
 SCALE_ROWS = K_PASS // 32
 LIST_ROWS = 16
-CHUNKS = 4
-CHUNK = R // CHUNKS
+CHUNK = K_PASS // 2
+SCALAR_DY_QUADS = 48
 COPY = mybir.ActivationFunctionType.Copy
 
+RUN = 4
 HALF = SLOTS // 2
 KIB = 1024
 LAP = 64
 
 RUNS = (
-    (("ones", 4 * P), ("window0", 8 * KIB)),
-    (("a_pool2", 8 * KIB), ("x_raw0", 4 * KIB), ("bt_word_pool", 8 * KIB), ("row_factor", 4 * KIB), ("a_pool3", 8 * KIB),
-     ("a_codes", 2 * KIB)),
-    (("dy_raw0", 4 * KIB), ("x_raw2", 4 * KIB), ("v2_rows0_codes", 2 * KIB)),
+    (("ones", 4 * P), ("window1", 8 * KIB)),
+    (("dy_raw0", 8 * KIB),),
+    (("dy_grouped0", 4 * KIB), ("window0", 8 * KIB)),
+    (("dy_grouped1", 4 * KIB),),
+    (("x_raw2", 4 * KIB), ("v2_rows0_codes", 2 * KIB)),
     (("v2_rows1", 4 * KIB), ("x1_codes", KIB)),
     (("a_slots0", 2 * KIB), ("da_sb2_0", KIB), ("da_sb0", 2 * KIB), ("da_sb2_1", KIB), ("x_grouped3", 2 * KIB)),
-    (("dy_raw1", 4 * KIB), ("a_pool0", 8 * KIB)),
-    (("dy_raw2", 4 * KIB), ("a_pool1", 8 * KIB)),
-    (("dy_raw3", 4 * KIB), ("x_raw3", 4 * KIB)),
-    (("window1", 8 * KIB), ("bt_scale_pool", T), ("bt_codes", 2 * KIB)),
-    (("spare", 2 * KIB + LAP), ("x_rounded1", 2 * KIB), ("dy_grouped3", 2 * KIB), ("dy_grouped1", 2 * KIB), ("bt_scales_dealt", SLOTS),
-     ("dy_grouped2", 2 * KIB), ("x_rounded0", 2 * KIB)),
+    (("a_pool3", 8 * KIB), ("a_codes", 2 * KIB)),
     (("window2", 8 * KIB), ("x_grouped2", 2 * KIB), ("a_listed1", KIB)),
     (("x2_codes", KIB), ("v2_slots0", 4 * KIB)),
     (("x2_scales", 2 * P), ("v2_slots1", 2 * KIB)),
     (("a_listed2", KIB), ("da_sb1", 2 * KIB), ("a_listed3", KIB)),
     (("a_slots1", 2 * KIB), ("x3_codes", KIB)),
 )
-INSIDE = (("a_listed0", "x_rounded1", -2 * KIB), ("v2_slots2", "a_pool3", KIB), ("v2_slots_codes", "a_pool3", 3 * KIB), ("x_rounded2", "x_rounded1", -2 * KIB), ("x_raw1", "bt_word_pool", LAP), ("factor_cols", "bt_scale_pool", 2 * LAP))
+INSIDE = (
+    ("row_factor", "dy_raw0", 0), ("x_rounded1", "dy_grouped1", 0), ("x_rounded2", "dy_grouped1", 2 * KIB),
+    ("a_listed0", "dy_grouped1", 2 * KIB), ("v2_slots2", "a_pool3", KIB), ("v2_slots_codes", "a_pool3", 3 * KIB),
+)
 
 
 def placement():
@@ -107,22 +107,15 @@ def tile_attend_glora_ax_kernel(
         wt_cols = wt_tile[:, :, 0:PACK]
         nc.scalar.dma_start(us_cols, us.rearrange("(g p t) o -> p g (t o)", g=ROW_PASSES, t=PACK))
         nc.scalar.dma_start(wt_cols, wt.rearrange("(g p t) o -> p g (t o)", g=ROW_PASSES, t=PACK))
-        ones = sbuf("ones", [P, P], F32)
-        nc.gpsimd.memset(ones[:], 1.0)
-        ident = sbuf("ident", [P, P], F32)
-        nc.gpsimd.affine_select(
-            out=ident[:], in_=ones[:], pattern=[[-1, P]], compare_op=mybir.AluOpType.is_equal, fill=0.0, base=0,
-            channel_multiplier=1,
-        )
         sc_pool = sbuf("sc_pool", [P, T], F32)
-        nc.gpsimd.memset(sc_pool[0 : P - 1, :].bitcast(I32), 0)
+        nc.vector.memset(sc_pool[0 : P - 1, :].bitcast(I32), 0)
         nc.sync.dma_start(sc_pool[P - 1 : P, :], sc[P - 1 : P, :])
         bt_word_pool = sbuf("bt_word_pool", [P, T], I32)
         nc.sync.dma_start(bt_word_pool[:], Bt_words[0].rearrange("p n t -> p (n t)").bitcast(I32))
 
-        def load_dy(c):
-            raw = sbuf("dy_raw%d" % c, [P, PACK, CHUNK], F32)
-            nc.sync.dma_start(raw[:], dyT[:, c * CHUNK : (c + 1) * CHUNK].rearrange("(p j) r -> p j r", j=PACK))
+        def load_dy(name, r0, r1):
+            raw = sbuf(name, [P, PACK, r1 - r0], F32)
+            nc.sync.dma_start(raw[:], dyT[:, r0:r1].rearrange("(p j) r -> p j r", j=PACK))
             return raw
 
         def load_x(j):
@@ -135,84 +128,83 @@ def tile_attend_glora_ax_kernel(
             nc.sync.dma_start(pool[:], A[j * P : (j + 1) * P, :])
             return pool
 
-        dy_raw = [load_dy(c) for c in range(CHUNKS)]
+        dy_raw0 = load_dy("dy_raw0", 0, K_PASS)
+        dy_raw1 = [load_dy("dy_raw1%d" % h, K_PASS + h * CHUNK, K_PASS + (h + 1) * CHUNK) for h in range(2)]
+        x_raw0 = load_x(0)
+        x_raw1 = load_x(1)
+        x_raw2 = load_x(2)
+        a_pool0 = load_a(0)
+        a_pool1 = load_a(1)
+        x_raw3 = load_x(3)
+        a_pool2 = load_a(2)
+        a_pool3 = load_a(3)
 
+        ones = sbuf("ones", [P, P], F32)
+        nc.gpsimd.memset(ones[:], 1.0)
+        ident = sbuf("ident", [P, P], F32)
+        nc.gpsimd.affine_select(
+            out=ident[:], in_=ones[:], pattern=[[-1, P]], compare_op=mybir.AluOpType.is_equal, fill=0.0, base=0,
+            channel_multiplier=1,
+        )
 
-        def zeroed_window(n, engine):
+        def zeroed_window(n):
             window = sbuf("window%d" % n, [P, T], F32)
-            engine.memset(window[:].bitcast(I32), 0)
+            nc.gpsimd.memset(window[:], 0.0)
             return window
 
-        window0 = zeroed_window(0, nc.gpsimd)
+        window1 = zeroed_window(1)
 
+        bt_scales_listed = sbuf("bt_scales_listed", [P, SLOTS], U8)
+        nc.vector.tensor_copy(bt_scales_listed[:], bt_scale_pool[:].indirect(offsets[:]))
         bt_scales_dealt = sbuf("bt_scales_dealt", [P, SLOTS], U8)
         nc.vector.tensor_copy(
-            bt_scales_dealt[:].rearrange("p (t m) -> p m t", t=PACK), bt_scale_pool[:].indirect(offsets[:])
+            bt_scales_dealt[:].rearrange("p (t m) -> p t m", t=PACK),
+            bt_scales_listed[:].rearrange("p (m t) -> p t m", t=PACK),
         )
-        sc_row = sbuf("sc_row", [P, SLOTS], F32)
-        nc.vector.tensor_copy(sc_row[:], sc_pool[:].indirect(offsets[:]))
         for q in range(P // QUADRANT):
             first = P - SCALE_ROWS + PACK * q
             nc.scalar.dma_start(
                 bt_scales[QUADRANT * q : QUADRANT * q + PACK, :].bitcast(I32),
                 bt_scales_dealt[first : first + PACK, :].bitcast(I32),
             )
-        window1 = zeroed_window(1, nc.gpsimd)
+        sc_row = sbuf("sc_row", [P, SLOTS], F32)
+        nc.vector.tensor_copy(sc_row[:], sc_pool[:].indirect(offsets[:]))
         factor_cols = sbuf("factor_cols", [P, ROW_PASSES, PACK], F32)
         nc.vector.tensor_tensor(factor_cols[:], us_cols, wt_cols, MULT)
-
         sc_turned = quarters(banks[4])
         for t in range(PACK):
             nc.tensor.transpose(sc_turned[:, t, :], sc_row[:, t:SLOTS:PACK], ident[:])
+        sc_cols = sbuf("sc_cols", [P, PACK], F32)
+        nc.scalar.copy(sc_cols[:], sc_turned[:, :, P - 1])
 
+        bt_codes_listed = sbuf("bt_codes_listed", [P, SLOTS], U32)
+        nc.vector.tensor_copy(bt_codes_listed[:], bt_word_pool[:].bitcast(U32).indirect(offsets[:]))
         bt_codes = sbuf("bt_codes", [P, SLOTS], U32)
         nc.vector.tensor_copy(
-            bt_codes[:].rearrange("p (t m) -> p m t", t=PACK), bt_word_pool[:].bitcast(U32).indirect(offsets[:])
+            bt_codes[:].bitcast(I32).rearrange("p (t c n) -> p c t n", t=PACK, n=RUN),
+            bt_codes_listed[:].bitcast(I32).rearrange("p (c n t) -> p c t n", t=PACK, n=RUN),
         )
-        x_raw0 = load_x(0)
-        x_raw1 = load_x(1)
 
-        row_factor = sbuf("row_factor", [P, ROW_PASSES, K_PASS], F32)
-        for g in range(ROW_PASSES):
-            spread = quarters(banks[5 + g])
-            for t in range(PACK):
-                nc.tensor.transpose(spread[:, t, :], factor_cols[:, g, t : t + 1].to_broadcast([P, P]), ident[:])
-            nc.vector.tensor_copy(
-                row_factor[:, g, :].rearrange("p (u m e) -> p u m e", u=2, e=2), spread.rearrange("p (u e) m -> p u m e", u=2)
-            )
-
-        def group_dy(c, copy):
-            grouped = sbuf("dy_grouped%d" % c, [P, CHUNK * PACK], BF16)
+        def group_dy(raw, m0, m1, grouped, first, copy):
             copy(
-                grouped[:].rearrange("p (u m e j) -> p m j u e", u=2, e=2, j=PACK),
-                dy_raw[c][:].rearrange("p j (m u e) -> p m j u e", u=2, e=2),
+                grouped[:].rearrange("p (u m e j) -> p m j u e", u=2, e=2, j=PACK)[:, first + m0 : first + m1],
+                raw[:].rearrange("p j (m u e) -> p m j u e", u=2, e=2)[:, m0:m1],
             )
-            return grouped
-
-        def activation_copy(out, in_):
-            for u in range(2):
-                nc.scalar.activation(out[:, :, :, u, :], in_[:, :, :, u, :], COPY)
 
         def round_on_gpsimd(out, in_):
             nc.gpsimd.tensor_scalar(out, in_, 1.0, 0.0, MULT, ADD)
 
         v2_tiles = [sbuf("v2_%d" % g, [P, PACK * K_PASS], BF16) for g in range(ROW_PASSES)]
 
-        def first_product(c, t, dy_mx):
-            g, h = divmod(c, 2)
-            v = banks[t][:, h * CHUNK : (h + 1) * CHUNK]
+        def first_product(g, t, dy_mx):
+            v = banks[t]
             cols = slice(t * P, (t + 1) * P)
             nc.tensor.matmul_mx(
-                out=v, lhsT=bt_codes[:, cols].bitcast(E4M3), lhsT_scale=bt_scales[:, cols],
+                out=v[:], lhsT=bt_codes[:, cols].bitcast(E4M3), lhsT_scale=bt_scales[:, cols],
                 rhs=dy_mx[0][:].bitcast(E5M2), rhs_scale=dy_mx[1][:], start=True, stop=True,
             )
-            rows = slice(h * P, (h + 1) * P)
             nc.vector.scalar_tensor_tensor(
-                v2_tiles[g][:].rearrange("p (t u n) -> p t u n", t=PACK, u=2)[:, t, :, rows],
-                v.rearrange("p (u n) -> p u n", u=2),
-                sc_cols[:, t : t + 1],
-                row_factor[:, g, :].rearrange("p (u n) -> p u n", u=2)[:, :, rows],
-                MULT, MULT,
+                v2_tiles[g][:, t * K_PASS : (t + 1) * K_PASS], v[:], sc_cols[:, t : t + 1], row_factor[:, g, :], MULT, MULT
             )
 
         def turn_start(words, into):
@@ -308,30 +300,32 @@ def tile_attend_glora_ax_kernel(
 
         v2_rows = [sbuf("v2_rows%d" % g, [P, SLOTS * PACK], BF16) for g in range(ROW_PASSES)]
         v2_rows_mx = [mx_tiles("v2_rows%d" % g, SLOTS) for g in range(ROW_PASSES)]
-        dy_mx = [mx_tiles("dy%d" % c, CHUNK) for c in range(CHUNKS)]
-        quantize(dy_mx[0], group_dy(0, activation_copy)[:], E5M2)
-        sc_cols = sbuf("sc_cols", [P, PACK], F32)
-        nc.vector.tensor_copy(sc_cols[:], sc_turned[:, :, P - 1])
-        x_raw2 = load_x(2)
-
-        def chunk(c):
+        dy_mx = [mx_tiles("dy%d" % g, K_PASS) for g in range(ROW_PASSES)]
+        dy_grouped = [sbuf("dy_grouped%d" % g, [P, K_PASS * PACK], BF16) for g in range(ROW_PASSES)]
+        group_dy(dy_raw0, 0, SCALAR_DY_QUADS, dy_grouped[0], 0, nc.scalar.copy)
+        group_dy(dy_raw0, SCALAR_DY_QUADS, P, dy_grouped[0], 0, nc.vector.tensor_copy)
+        quantize(dy_mx[0], dy_grouped[0][:], E5M2)
+        row_factor = sbuf("row_factor", [P, ROW_PASSES, K_PASS], F32)
+        for g in range(ROW_PASSES):
+            spread = quarters(banks[5 + g])
             for t in range(PACK):
-                if t == 2 and c + 1 < CHUNKS:
-                    quantize(dy_mx[c + 1], group_dy(c + 1, nc.scalar.copy)[:], E5M2)
-                first_product(c, t, dy_mx[c])
-
-        for c in range(3):
-            chunk(c)
-        a_pool0 = load_a(0)
-        a_pool1 = load_a(1)
-        x_raw3 = load_x(3)
+                nc.tensor.transpose(spread[:, t, :], factor_cols[:, g, t : t + 1].to_broadcast([P, P]), ident[:])
+            nc.scalar.copy(
+                row_factor[:, g, :].rearrange("p (u m e) -> p u m e", u=2, e=2), spread.rearrange("p (u e) m -> p u m e", u=2)
+            )
+        window0 = zeroed_window(0)
+        for h in range(2):
+            group_dy(dy_raw1[h], 0, P // 2, dy_grouped[1], h * P // 2, nc.scalar.copy)
+        for t in range(PACK):
+            first_product(0, t, dy_mx[0])
+        quantize(dy_mx[1], dy_grouped[1][:], E5M2)
         turn_v2(0, 0, 2, 4)
         turn_v2(0, 2, 4, 5)
         x_rounded0 = round_x(0, x_raw0, nc.scalar.copy)
         x_rounded1 = round_x(1, x_raw1, round_on_gpsimd)
         x_rounded2 = round_x(2, x_raw2, round_on_gpsimd)
-        chunk(3)
-        a_pool2 = load_a(2)
+        for t in range(PACK):
+            first_product(1, t, dy_mx[1])
         x_grouped = [sbuf("x_grouped%d" % j, [P, R], BF16) for j in range(PACK)]
         x_mx = [mx_tiles("x%d" % j, R // PACK) for j in range(PACK)]
         turn_x(x_rounded0, x_grouped[0][:], 6, nc.scalar.copy)
@@ -346,13 +340,12 @@ def tile_attend_glora_ax_kernel(
         quantize_v2_rows(1, 2, 4)
         quantize(x_mx[1], x_grouped[1][:], E4M3)
         quantize(x_mx[2], x_grouped[2][:], E4M3)
-        a_pool3 = load_a(3)
         da0 = second_product(x_mx[0], 0, 0)
         da1 = second_product(x_mx[1], 0, 1)
         da2 = second_product(x_mx[2], 0, 6)
         a_listed = [gather_a(0, a_pool0)]
         da_sb0 = fetch("da_sb0", da0, nc.scalar.copy)
-        window2 = zeroed_window(2, nc.gpsimd)
+        window2 = zeroed_window(2)
 
         v2_slots = [sbuf("v2_slots%d" % n, [P, width], BF16) for n, width in enumerate((2 * R, R, R))]
 

@@ -29,28 +29,28 @@ SCALAR_DY_QUADS = 48
 COPY = mybir.ActivationFunctionType.Copy
 
 RUN = 4
+SCALAR_OUT_TILES = (5, 7)
 HALF = SLOTS // 2
 KIB = 1024
 LAP = 64
 
 RUNS = (
     (("ones", 4 * P), ("window1", 8 * KIB)),
-    (("dy_raw0", 8 * KIB),),
-    (("dy_grouped0", 4 * KIB), ("window0", 8 * KIB)),
+    (("row_factor", 4 * KIB), ("dy_grouped0", 4 * KIB), ("window0", 8 * KIB)),
     (("dy_grouped1", 4 * KIB),),
-    (("x_raw2", 4 * KIB), ("v2_rows0_codes", 2 * KIB)),
-    (("v2_rows1", 4 * KIB), ("x1_codes", KIB)),
-    (("a_slots0", 2 * KIB), ("da_sb2_0", KIB), ("da_sb0", 2 * KIB), ("da_sb2_1", KIB), ("x_grouped3", 2 * KIB)),
+    (("x_rounded3", 2 * KIB), ("x_raw2", 4 * KIB), ("v2_rows0_codes", 2 * KIB)),
+    (("window2", 8 * KIB), ("x_grouped3", 2 * KIB), ("v2_rows1", 4 * KIB), ("x1_codes", KIB)),
+    (("v2_slots1", 2 * KIB), ("a_slots0", 2 * KIB), ("da_sb2_0", KIB), ("da_sb0_1", KIB), ("da_sb2_1", KIB), ("da_sb3_0", KIB)),
     (("a_pool3", 8 * KIB), ("a_codes", 2 * KIB)),
-    (("window2", 8 * KIB), ("x_grouped2", 2 * KIB), ("a_listed1", KIB)),
-    (("x2_codes", KIB), ("v2_slots0", 4 * KIB)),
-    (("x2_scales", 2 * P), ("v2_slots1", 2 * KIB)),
-    (("a_listed2", KIB), ("da_sb1", 2 * KIB), ("a_listed3", KIB)),
-    (("a_slots1", 2 * KIB), ("x3_codes", KIB)),
+    (("da_sb0_0", KIB), ("da_sb1", 2 * KIB), ("a_pool1", 8 * KIB)),
+    (("x_grouped2", 2 * KIB), ("v2_slots0", 2 * KIB)),
+    (("a_slots1", 2 * KIB), ("v2_slots2", 2 * KIB)),
 )
 INSIDE = (
-    ("row_factor", "dy_raw0", 0), ("x_rounded1", "dy_grouped1", 0), ("x_rounded2", "dy_grouped1", 2 * KIB),
-    ("a_listed0", "dy_grouped1", 2 * KIB), ("v2_slots2", "a_pool3", KIB), ("v2_slots_codes", "a_pool3", 3 * KIB),
+    ("x_rounded1", "dy_grouped1", 0), ("x_rounded2", "dy_grouped1", 2 * KIB), ("a_listed0", "dy_grouped1", 2 * KIB),
+    ("a_listed1", "x_grouped3", LAP),
+    ("v2_slots0_codes", "a_pool3", 3 * KIB), ("a_listed3", "da_sb1", LAP), ("a_listed2", "da_sb1", KIB + LAP),
+    ("da_sb3_1", "da_sb2_1", -LAP), ("v2_slots3", "da_sb2_1", -2 * KIB),
 )
 
 
@@ -133,9 +133,9 @@ def tile_attend_glora_ax_kernel(
         x_raw0 = load_x(0)
         x_raw1 = load_x(1)
         x_raw2 = load_x(2)
+        x_raw3 = load_x(3)
         a_pool0 = load_a(0)
         a_pool1 = load_a(1)
-        x_raw3 = load_x(3)
         a_pool2 = load_a(2)
         a_pool3 = load_a(3)
 
@@ -242,20 +242,6 @@ def tile_attend_glora_ax_kernel(
             words = rounded[:].bitcast(F32).rearrange("p (u g m) -> p g u m", u=2, g=ROW_PASSES)
             turn([[words[:, g, u, :] for u in range(2)] for g in range(ROW_PASSES)], grouped, into, copy)
 
-        def turn_x_whole(raw, into):
-            for g in range(ROW_PASSES):
-                for t in range(PACK):
-                    nc.tensor.transpose(
-                        quarters(banks[into[g]])[:, t, :], raw[:, g * K_PASS + t : (g + 1) * K_PASS : PACK], ident[:]
-                    )
-
-        def round_x_turned(grouped, into):
-            for g in range(ROW_PASSES):
-                nc.scalar.copy(
-                    grouped[:, g * K_PASS : (g + 1) * K_PASS].rearrange("p (m t) -> p m t", t=PACK),
-                    quarters(banks[into[g]]).rearrange("p t m -> p m t"),
-                )
-
         def gather_a(j, pool):
             listed = sbuf("a_listed%d" % j, [P, SLOTS], BF16)
             if j == 0:
@@ -291,9 +277,8 @@ def tile_attend_glora_ax_kernel(
             listed = offsets[:, h * HALF // LIST_ROWS : (h + 1) * HALF // LIST_ROWS]
             nc.scalar.activation(window[:].indirect(listed), values, COPY)
 
-        def scatter_on_scalar(window, da_sb):
-            for h in range(2):
-                scatter_half(window, h, da_sb[:, h * HALF : (h + 1) * HALF])
+        def fetch_halves(j, da):
+            return [fetch("da_sb%d_%d" % (j, h), da, nc.scalar.copy, h, h + 1) for h in range(2)]
 
         def store_window(j, window, queue):
             queue.dma_start(out_0[j * P : (j + 1) * P, :], window[:])
@@ -310,94 +295,104 @@ def tile_attend_glora_ax_kernel(
             spread = quarters(banks[5 + g])
             for t in range(PACK):
                 nc.tensor.transpose(spread[:, t, :], factor_cols[:, g, t : t + 1].to_broadcast([P, P]), ident[:])
-            nc.scalar.copy(
+            nc.vector.tensor_copy(
                 row_factor[:, g, :].rearrange("p (u m e) -> p u m e", u=2, e=2), spread.rearrange("p (u e) m -> p u m e", u=2)
             )
         window0 = zeroed_window(0)
         for h in range(2):
             group_dy(dy_raw1[h], 0, P // 2, dy_grouped[1], h * P // 2, nc.scalar.copy)
         for t in range(PACK):
+            if t == 2:
+                quantize(dy_mx[1], dy_grouped[1][:], E5M2)
             first_product(0, t, dy_mx[0])
-        quantize(dy_mx[1], dy_grouped[1][:], E5M2)
         turn_v2(0, 0, 2, 4)
-        turn_v2(0, 2, 4, 5)
         x_rounded0 = round_x(0, x_raw0, nc.scalar.copy)
         x_rounded1 = round_x(1, x_raw1, round_on_gpsimd)
         x_rounded2 = round_x(2, x_raw2, round_on_gpsimd)
-        for t in range(PACK):
-            first_product(1, t, dy_mx[1])
         x_grouped = [sbuf("x_grouped%d" % j, [P, R], BF16) for j in range(PACK)]
         x_mx = [mx_tiles("x%d" % j, R // PACK) for j in range(PACK)]
-        turn_x(x_rounded0, x_grouped[0][:], 6, nc.scalar.copy)
-        turn_x(x_rounded1, x_grouped[1][:], 7, nc.vector.tensor_copy)
+        for t in range(PACK):
+            if t == 2:
+                turn_x(x_rounded0, x_grouped[0][:], 6, nc.scalar.copy)
+                turn_v2(0, 2, 4, 5)
+            first_product(1, t, dy_mx[1])
         turn_v2(1, 0, 2, 4)
-        turn_v2(1, 2, 3, 5)
-        turn_v2(1, 3, 4, 6)
-        turn_x(x_rounded2, x_grouped[2][:], 2, nc.scalar.copy)
+        turn_v2(1, 2, 3, 6)
+        turn_v2(1, 3, 4, 5)
+        turn_x(x_rounded1, x_grouped[1][:], 4, nc.scalar.copy)
+        turn_x(x_rounded2, x_grouped[2][:], 6, nc.scalar.copy)
         quantize_v2_rows(0, 0, 4)
         quantize(x_mx[0], x_grouped[0][:], E4M3)
+        x_rounded3 = round_x(3, x_raw3, nc.vector.tensor_copy)
         quantize_v2_rows(1, 0, 2)
         quantize_v2_rows(1, 2, 4)
-        quantize(x_mx[1], x_grouped[1][:], E4M3)
-        quantize(x_mx[2], x_grouped[2][:], E4M3)
+        turn_x(x_rounded3, x_grouped[3][:], 3, nc.vector.tensor_copy)
+        for j in range(1, PACK):
+            quantize(x_mx[j], x_grouped[j][:], E4M3)
         da0 = second_product(x_mx[0], 0, 0)
         da1 = second_product(x_mx[1], 0, 1)
-        da2 = second_product(x_mx[2], 0, 6)
+        da2 = second_product(x_mx[2], 0, 7)
+        da3 = second_product(x_mx[3], 0, 2)
         a_listed = [gather_a(0, a_pool0)]
-        da_sb0 = fetch("da_sb0", da0, nc.scalar.copy)
+        da_sb0 = fetch_halves(0, da0)
         window2 = zeroed_window(2)
 
-        v2_slots = [sbuf("v2_slots%d" % n, [P, width], BF16) for n, width in enumerate((2 * R, R, R))]
+        def group_v2_slots(n, copy):
+            g, u = divmod(n, 2)
+            grouped = sbuf("v2_slots%d" % n, [P, R], BF16)
+            src = v2_tiles[g][:].rearrange("p (t u m e) -> p u m t e", t=PACK, u=2, e=2)
+            copy(grouped[:].rearrange("p (e m t) -> p m t e", e=2, t=PACK), src[:, u])
+            return grouped
 
-        def group_v2_slots(g, u, copy):
-            to = v2_slots[0][:, u * R : (u + 1) * R] if g == 0 else v2_slots[1 + u][:]
-            src = v2_tiles[g][:].rearrange("p (t u m e) -> p u e m t", t=PACK, u=2, e=2)
-            copy(to.rearrange("p (e m t) -> p e m t", e=2, t=PACK), src[:, u])
+        def quantize_v2_slots(n, grouped):
+            mx = mx_tiles("v2_slots%d" % n, 2 * P)
+            quantize(mx, grouped[:], E5M2)
+            return mx
 
-        for g, u in ((0, 0), (0, 1), (1, 0)):
-            group_v2_slots(g, u, round_on_gpsimd)
-        da_sb1 = fetch("da_sb1", da1, nc.vector.tensor_copy)
+        v2_slots0 = group_v2_slots(0, nc.vector.tensor_copy)
         a_listed.append(gather_a(1, a_pool1))
         turn_a(a_listed[0:2], 4)
-        turn_x_whole(x_raw3, (2, 3))
-        scatter_on_scalar(window0, da_sb0)
-        store_window(0, window0, nc.scalar)
+        scatter_half(window0, 0, da_sb0[0][:])
+        da_sb1 = fetch("da_sb1", da1, nc.vector.tensor_copy)
+        scatter_half(window0, 1, da_sb0[1][:])
+        store_window(0, window0, nc.sync)
         nc.vector.tensor_copy(window1[:].indirect(offsets[:]), da_sb1[:])
         store_window(1, window1, nc.sync)
-        da_sb2 = [fetch("da_sb2_%d" % h, da2, nc.scalar.copy, h, h + 1) for h in range(2)]
+        da_sb2 = fetch_halves(2, da2)
         a_listed.append(gather_a(2, a_pool2))
         a_listed.append(gather_a(3, a_pool3))
-        group_v2_slots(1, 1, nc.vector.tensor_copy)
         a_slots = [sbuf("a_slots%d" % h, [P, 2 * K_PASS], BF16) for h in range(2)]
         scatter_half(window2, 0, da_sb2[0][:])
         turn_finish(a_slots[0][:], 4, nc.scalar.copy)
         scatter_half(window2, 1, da_sb2[1][:])
-        store_window(2, window2, nc.scalar)
+        store_window(2, window2, nc.sync)
+        da_sb3 = fetch_halves(3, da3)
         turn_a(a_listed[2:4], 5)
-        turn_finish(a_slots[1][:], 5, nc.vector.tensor_copy)
-        round_x_turned(x_grouped[3], (2, 3))
-        v2_slots_mx = mx_tiles("v2_slots", R)
         a_mx = mx_tiles("a", D)
+        v2_slots_mx = [quantize_v2_slots(0, v2_slots0)]
         quantize(a_mx, a_slots[0][:], E4M3)
-        quantize(v2_slots_mx, v2_slots[0][:], E5M2)
+        turn_finish(a_slots[1][:], 5, nc.vector.tensor_copy)
+        v2_slots1 = group_v2_slots(1, nc.vector.tensor_copy)
         quantize(a_mx, a_slots[1][:], E4M3, 2 * P)
-        quantize(v2_slots_mx, v2_slots[1][:], E5M2, K_PASS)
-        quantize(v2_slots_mx, v2_slots[2][:], E5M2, K_PASS + CHUNK)
-        quantize(x_mx[3], x_grouped[3][:], E4M3)
+        v2_slots_mx.append(quantize_v2_slots(1, v2_slots1))
+        v2_slots_mx.append(quantize_v2_slots(2, group_v2_slots(2, nc.vector.tensor_copy)))
+        for h in range(2):
+            scatter_half(window0, h, da_sb3[h][:])
+        store_window(3, window0, nc.scalar)
+        v2_slots3 = group_v2_slots(3, nc.scalar.copy)
         dx = sbuf("dx", [P, R // P, D], F32)
         for n in range(R // P):
-            acc = banks[(7, 0, 1, 4)[n % 4]]
-            cols = slice(n * P, (n + 1) * P)
+            if n == PACK:
+                v2_slots_mx.append(quantize_v2_slots(3, v2_slots3))
+            acc = banks[(6, 0, 1, 3)[n % 4]]
+            codes, scales = v2_slots_mx[n // 2]
+            cols = slice(n % 2 * P, (n % 2 + 1) * P)
             nc.tensor.matmul_mx(
-                out=acc[:], lhsT=v2_slots_mx[0][:, cols].bitcast(E5M2), lhsT_scale=v2_slots_mx[1][:, cols],
+                out=acc[:], lhsT=codes[:, cols].bitcast(E5M2), lhsT_scale=scales[:, cols],
                 rhs=a_mx[0][:].bitcast(E4M3), rhs_scale=a_mx[1][:], start=True, stop=True,
             )
-            (nc.scalar.copy if n == 1 else nc.vector.tensor_copy)(dx[:, n, :], acc[:])
+            (nc.scalar.copy if n in SCALAR_OUT_TILES else nc.vector.tensor_copy)(dx[:, n, :], acc[:])
             if n % 2 == 1:
                 g, c = divmod(n - 1, PACK)
                 rows = out_1[g * K_PASS : (g + 1) * K_PASS, :].rearrange("(m n) d -> m n d", n=PACK)
                 nc.sync.dma_start(rows[:, c : c + 2, :], dx[:, n - 1 : n + 1, :])
-            if n == 3:
-                da_sb3 = fetch("da_sb3", second_product(x_mx[3], 0, 6), nc.scalar.copy)
-        scatter_on_scalar(window0, da_sb3)
-        store_window(3, window0, nc.scalar)

@@ -29,28 +29,28 @@ SCALAR_DY_QUADS = 48
 COPY = mybir.ActivationFunctionType.Copy
 
 RUN = 4
-SCALAR_OUT_TILES = (5, 7)
+SCALAR_OUT_TILES = (3, 5, 7)
 HALF = SLOTS // 2
 KIB = 1024
 LAP = 64
 
 RUNS = (
-    (("ones", 4 * P), ("window1", 8 * KIB)),
-    (("row_factor", 4 * KIB), ("dy_grouped0", 4 * KIB), ("window0", 8 * KIB)),
+    (("window1", 8 * KIB), ("bt_scales_listed", SLOTS)),
+    (("ones", 4 * P), ("window0", 8 * KIB)),
+    (("row_factor", 4 * KIB), ("dy_grouped0", 4 * KIB), ("window2", 8 * KIB)),
     (("dy_grouped1", 4 * KIB),),
     (("x_rounded3", 2 * KIB), ("x_raw2", 4 * KIB), ("v2_rows0_codes", 2 * KIB)),
-    (("window2", 8 * KIB), ("x_grouped3", 2 * KIB), ("v2_rows1", 4 * KIB), ("x1_codes", KIB)),
-    (("v2_slots1", 2 * KIB), ("a_slots0", 2 * KIB), ("da_sb2_0", KIB), ("da_sb0_1", KIB), ("da_sb2_1", KIB), ("da_sb3_0", KIB)),
-    (("a_pool3", 8 * KIB), ("a_codes", 2 * KIB)),
-    (("da_sb0_0", KIB), ("da_sb1", 2 * KIB), ("a_pool1", 8 * KIB)),
-    (("x_grouped2", 2 * KIB), ("v2_slots0", 2 * KIB)),
+    (("da_sb0_1", KIB), ("da_sb2_1", KIB), ("da_sb3_1", KIB), ("v2_slots3", 2 * KIB)),
+    (("a_codes", 2 * KIB), ("a_pool3", 8 * KIB), ("a_slots0", 2 * KIB)),
+    (("da_sb3_0", KIB), ("da_sb2_0", KIB), ("da_sb0_0", KIB), ("da_sb1", 2 * KIB), ("x_grouped3", 2 * KIB),
+     ("v2_rows1", 4 * KIB), ("x1_codes", KIB)),
+    (("window3", 8 * KIB), ("v2_slots0", 2 * KIB), ("x_grouped1", 2 * KIB)),
+    (("v2_slots3_codes", KIB), ("v2_slots0_codes", KIB), ("a_pool1", 8 * KIB), ("a_listed2", KIB)),
     (("a_slots1", 2 * KIB), ("v2_slots2", 2 * KIB)),
 )
 INSIDE = (
     ("x_rounded1", "dy_grouped1", 0), ("x_rounded2", "dy_grouped1", 2 * KIB), ("a_listed0", "dy_grouped1", 2 * KIB),
-    ("a_listed1", "x_grouped3", LAP),
-    ("v2_slots0_codes", "a_pool3", 3 * KIB), ("a_listed3", "da_sb1", LAP), ("a_listed2", "da_sb1", KIB + LAP),
-    ("da_sb3_1", "da_sb2_1", -LAP), ("v2_slots3", "da_sb2_1", -2 * KIB),
+    ("a_listed1", "x_grouped3", LAP), ("a_listed3", "da_sb1", LAP), ("v2_slots1", "a_pool3", KIB),
 )
 
 
@@ -152,7 +152,7 @@ def tile_attend_glora_ax_kernel(
             nc.gpsimd.memset(window[:], 0.0)
             return window
 
-        window1 = zeroed_window(1)
+        window0 = zeroed_window(0)
 
         bt_scales_listed = sbuf("bt_scales_listed", [P, SLOTS], U8)
         nc.vector.tensor_copy(bt_scales_listed[:], bt_scale_pool[:].indirect(offsets[:]))
@@ -167,6 +167,7 @@ def tile_attend_glora_ax_kernel(
                 bt_scales[QUADRANT * q : QUADRANT * q + PACK, :].bitcast(I32),
                 bt_scales_dealt[first : first + PACK, :].bitcast(I32),
             )
+        window1 = zeroed_window(1)
         sc_row = sbuf("sc_row", [P, SLOTS], F32)
         nc.vector.tensor_copy(sc_row[:], sc_pool[:].indirect(offsets[:]))
         factor_cols = sbuf("factor_cols", [P, ROW_PASSES, PACK], F32)
@@ -277,8 +278,8 @@ def tile_attend_glora_ax_kernel(
             listed = offsets[:, h * HALF // LIST_ROWS : (h + 1) * HALF // LIST_ROWS]
             nc.scalar.activation(window[:].indirect(listed), values, COPY)
 
-        def fetch_halves(j, da):
-            return [fetch("da_sb%d_%d" % (j, h), da, nc.scalar.copy, h, h + 1) for h in range(2)]
+        def fetch_half(j, h, da):
+            return fetch("da_sb%d_%d" % (j, h), da, nc.scalar.copy, h, h + 1)
 
         def store_window(j, window, queue):
             queue.dma_start(out_0[j * P : (j + 1) * P, :], window[:])
@@ -298,7 +299,7 @@ def tile_attend_glora_ax_kernel(
             nc.vector.tensor_copy(
                 row_factor[:, g, :].rearrange("p (u m e) -> p u m e", u=2, e=2), spread.rearrange("p (u e) m -> p u m e", u=2)
             )
-        window0 = zeroed_window(0)
+        window2 = zeroed_window(2)
         for h in range(2):
             group_dy(dy_raw1[h], 0, P // 2, dy_grouped[1], h * P // 2, nc.scalar.copy)
         for t in range(PACK):
@@ -334,8 +335,7 @@ def tile_attend_glora_ax_kernel(
         da2 = second_product(x_mx[2], 0, 7)
         da3 = second_product(x_mx[3], 0, 2)
         a_listed = [gather_a(0, a_pool0)]
-        da_sb0 = fetch_halves(0, da0)
-        window2 = zeroed_window(2)
+        da_sb0 = [fetch_half(0, h, da0) for h in range(2)]
 
         def group_v2_slots(n, copy):
             g, u = divmod(n, 2)
@@ -354,35 +354,38 @@ def tile_attend_glora_ax_kernel(
         turn_a(a_listed[0:2], 4)
         scatter_half(window0, 0, da_sb0[0][:])
         da_sb1 = fetch("da_sb1", da1, nc.vector.tensor_copy)
+        v2_slots_mx = [quantize_v2_slots(0, v2_slots0)]
+        window3 = zeroed_window(3)
+        da_sb2 = [fetch_half(2, 0, da2)]
         scatter_half(window0, 1, da_sb0[1][:])
         store_window(0, window0, nc.sync)
         nc.vector.tensor_copy(window1[:].indirect(offsets[:]), da_sb1[:])
         store_window(1, window1, nc.sync)
-        da_sb2 = fetch_halves(2, da2)
         a_listed.append(gather_a(2, a_pool2))
         a_listed.append(gather_a(3, a_pool3))
-        a_slots = [sbuf("a_slots%d" % h, [P, 2 * K_PASS], BF16) for h in range(2)]
         scatter_half(window2, 0, da_sb2[0][:])
-        turn_finish(a_slots[0][:], 4, nc.scalar.copy)
+        da_sb2.append(fetch_half(2, 1, da2))
+        da_sb3 = [fetch_half(3, 0, da3)]
         scatter_half(window2, 1, da_sb2[1][:])
         store_window(2, window2, nc.sync)
-        da_sb3 = fetch_halves(3, da3)
+        a_slots = [sbuf("a_slots%d" % h, [P, 2 * K_PASS], BF16) for h in range(2)]
+        scatter_half(window3, 0, da_sb3[0][:])
+        da_sb3.append(fetch_half(3, 1, da3))
+        scatter_half(window3, 1, da_sb3[1][:])
+        store_window(3, window3, nc.scalar)
         turn_a(a_listed[2:4], 5)
         a_mx = mx_tiles("a", D)
-        v2_slots_mx = [quantize_v2_slots(0, v2_slots0)]
-        quantize(a_mx, a_slots[0][:], E4M3)
-        turn_finish(a_slots[1][:], 5, nc.vector.tensor_copy)
         v2_slots1 = group_v2_slots(1, nc.vector.tensor_copy)
-        quantize(a_mx, a_slots[1][:], E4M3, 2 * P)
+        turn_finish(a_slots[0][:], 4, nc.vector.tensor_copy)
+        turn_finish(a_slots[1][:], 5, nc.vector.tensor_copy)
         v2_slots_mx.append(quantize_v2_slots(1, v2_slots1))
+        quantize(a_mx, a_slots[0][:], E4M3)
+        quantize(a_mx, a_slots[1][:], E4M3, 2 * P)
         v2_slots_mx.append(quantize_v2_slots(2, group_v2_slots(2, nc.vector.tensor_copy)))
-        for h in range(2):
-            scatter_half(window0, h, da_sb3[h][:])
-        store_window(3, window0, nc.scalar)
         v2_slots3 = group_v2_slots(3, nc.scalar.copy)
         dx = sbuf("dx", [P, R // P, D], F32)
         for n in range(R // P):
-            if n == PACK:
+            if n == 2:
                 v2_slots_mx.append(quantize_v2_slots(3, v2_slots3))
             acc = banks[(6, 0, 1, 3)[n % 4]]
             codes, scales = v2_slots_mx[n // 2]

@@ -15,6 +15,7 @@ E4M3 = mybir.dt.float8_e4m3fn_x4
 E5M2 = mybir.dt.float8_e5m2_x4
 MULT = mybir.AluOpType.mult
 ADD = mybir.AluOpType.add
+COPY = mybir.ActivationFunctionType.Copy
 
 P = 128
 PACK = 4
@@ -24,46 +25,62 @@ BANKS = 8
 QUADRANT = 32
 SCALE_ROWS = K_PASS // 32
 LIST_ROWS = 16
-CHUNK = K_PASS // 2
-SCALAR_DY_QUADS = 48
-COPY = mybir.ActivationFunctionType.Copy
-
+PIECE = K_PASS // 2
+PIECES = R // PIECE
+SCALAR_DY_QUADS = 24
 RUN = 4
-SCALAR_OUT_TILES = (3, 5, 7)
-HALF = SLOTS // 2
 KIB = 1024
 LAP = 64
 
-RUNS = (
-    (("window1", 8 * KIB), ("bt_scales_listed", SLOTS)),
-    (("ones", 4 * P), ("window0", 8 * KIB)),
-    (("row_factor", 4 * KIB), ("dy_grouped0", 4 * KIB), ("window2", 8 * KIB)),
-    (("dy_grouped1", 4 * KIB),),
-    (("x_rounded3", 2 * KIB), ("x_raw2", 4 * KIB), ("v2_rows0_codes", 2 * KIB)),
-    (("da_sb0_1", KIB), ("da_sb2_1", KIB), ("da_sb3_1", KIB), ("v2_slots3", 2 * KIB)),
-    (("a_codes", 2 * KIB), ("a_pool3", 8 * KIB), ("a_slots0", 2 * KIB)),
-    (("da_sb3_0", KIB), ("da_sb2_0", KIB), ("da_sb0_0", KIB), ("da_sb1", 2 * KIB), ("x_grouped3", 2 * KIB),
-     ("v2_rows1", 4 * KIB), ("x1_codes", KIB)),
-    (("window3", 8 * KIB), ("v2_slots0", 2 * KIB), ("x_grouped1", 2 * KIB)),
-    (("v2_slots3_codes", KIB), ("v2_slots0_codes", KIB), ("a_pool1", 8 * KIB), ("a_listed2", KIB)),
-    (("a_slots1", 2 * KIB), ("v2_slots2", 2 * KIB)),
-)
-INSIDE = (
-    ("x_rounded1", "dy_grouped1", 0), ("x_rounded2", "dy_grouped1", 2 * KIB), ("a_listed0", "dy_grouped1", 2 * KIB),
-    ("a_listed1", "x_grouped3", LAP), ("a_listed3", "da_sb1", LAP), ("v2_slots1", "a_pool3", KIB),
-)
+SIZES = {
+    "bt_scales_listed": SLOTS, "window0": 8 * KIB, "dy_grouped0": 2 * KIB, "sc_cols": LAP, "row_factor1": 2 * KIB,
+    "v2_slots1": 2 * KIB, "dy_grouped3": 2 * KIB, "v2_slots0": 2 * KIB, "v2_rows1a": 2 * KIB, "a_listed0": KIB,
+    "x_grouped0": 2 * KIB, "x_rounded1": 2 * KIB, "v2_rows1b": 2 * KIB, "a_listed1": KIB, "window1": 8 * KIB,
+    "x0_codes": KIB, "x_grouped1": 2 * KIB, "a_listed2": KIB, "x0_scales": 256, "x1_codes": KIB, "x1_scales": 256,
+    "x_rounded2": 2 * KIB, "x_raw2": 4 * KIB, "x_grouped2": 2 * KIB, "a_pool3": 8 * KIB, "a_slots0": 2 * KIB,
+    "v2_slots1_codes": KIB, "a_codes": 2 * KIB, "a_slots1": 2 * KIB, "v2_slots2": 2 * KIB, "v2_slots3": 2 * KIB,
+    "x_raw3": 4 * KIB, "da_sb2": 2 * KIB, "x_grouped3": 2 * KIB, "v2_slots2_codes": KIB, "v2_slots0_codes": KIB,
+}
+TAKEN_OVER_BY = {
+    "bt_scales_listed": ("window0",),
+    "dy_grouped0": ("sc_cols", "row_factor1"),
+    "row_factor1": ("v2_slots1",),
+    "dy_grouped3": ("v2_slots0",),
+    "v2_rows1a": ("a_listed0",),
+    "x_grouped0": ("x_rounded1",),
+    "v2_rows1b": ("a_listed1", "window1"),
+    "x0_codes": ("x_grouped1",),
+    "x_grouped1": ("a_listed2",),
+    "x0_scales": ("x1_codes",),
+    "x1_scales": ("x_rounded2",),
+    "x_raw2": ("x_grouped2",),
+    "a_pool3": ("a_slots0",),
+    "x_grouped2": ("v2_slots1_codes", "a_codes"),
+    "a_slots1": ("v2_slots2",),
+    "v2_slots1": ("v2_slots3",),
+    "x_raw3": ("da_sb2",),
+    "x_grouped3": ("v2_slots2_codes",),
+    "a_listed0": ("v2_slots0_codes",),
+}
 
 
 def placement():
     at = {}
+
+    def place(name, start):
+        at[name] = start
+        end = start + SIZES[name]
+        heirs = TAKEN_OVER_BY.get(name, ())
+        inside = start + LAP
+        for heir in heirs[:-1]:
+            inside = place(heir, inside)
+            assert inside <= end - LAP
+        return place(heirs[-1], end - LAP) if heirs else end
+
     top = 0
-    for run in RUNS:
-        for name, size in run:
-            at[name] = top
-            top = top + size - LAP
-        top = top + LAP
-    for name, host, offset in INSIDE:
-        at[name] = at[host] + offset
+    for name in TAKEN_OVER_BY:
+        if name not in at:
+            top = place(name, top)
     return at
 
 
@@ -76,11 +93,10 @@ def tile_attend_glora_ax_kernel(
         placed = ctx.enter_context(tc.tile_pool(name="placed", bufs=1))
         psum = ctx.enter_context(tc.psum_pool(name="psum", bufs=1))
         banks = [psum.tile([P, K_PASS], F32, name="bank%d" % n) for n in range(BANKS)]
+        at = placement()
 
         def quarters(bank):
             return bank[:].rearrange("p (c m) -> p c m", c=PACK)
-
-        at = placement()
 
         def sbuf(name, shape, dtype):
             if name not in at:
@@ -107,15 +123,19 @@ def tile_attend_glora_ax_kernel(
         wt_cols = wt_tile[:, :, 0:PACK]
         nc.scalar.dma_start(us_cols, us.rearrange("(g p t) o -> p g (t o)", g=ROW_PASSES, t=PACK))
         nc.scalar.dma_start(wt_cols, wt.rearrange("(g p t) o -> p g (t o)", g=ROW_PASSES, t=PACK))
+        ones = sbuf("ones", [P, P], F32)
+        nc.vector.memset(ones[:], 1.0)
+        one = sbuf("one", [P, 1], F32)
+        nc.vector.memset(one[:], 1.0)
         sc_pool = sbuf("sc_pool", [P, T], F32)
         nc.vector.memset(sc_pool[0 : P - 1, :].bitcast(I32), 0)
         nc.sync.dma_start(sc_pool[P - 1 : P, :], sc[P - 1 : P, :])
         bt_word_pool = sbuf("bt_word_pool", [P, T], I32)
         nc.sync.dma_start(bt_word_pool[:], Bt_words[0].rearrange("p n t -> p (n t)").bitcast(I32))
 
-        def load_dy(name, r0, r1):
-            raw = sbuf(name, [P, PACK, r1 - r0], F32)
-            nc.sync.dma_start(raw[:], dyT[:, r0:r1].rearrange("(p j) r -> p j r", j=PACK))
+        def load_dy(n):
+            raw = sbuf("dy_raw%d" % n, [P, PACK, PIECE], F32)
+            nc.sync.dma_start(raw[:], dyT[:, n * PIECE : (n + 1) * PIECE].rearrange("(p j) r -> p j r", j=PACK))
             return raw
 
         def load_x(j):
@@ -128,34 +148,27 @@ def tile_attend_glora_ax_kernel(
             nc.sync.dma_start(pool[:], A[j * P : (j + 1) * P, :])
             return pool
 
-        dy_raw0 = load_dy("dy_raw0", 0, K_PASS)
-        dy_raw1 = [load_dy("dy_raw1%d" % h, K_PASS + h * CHUNK, K_PASS + (h + 1) * CHUNK) for h in range(2)]
+        dy_raw = [load_dy(n) for n in range(PIECES)]
         x_raw0 = load_x(0)
-        x_raw1 = load_x(1)
-        x_raw2 = load_x(2)
-        x_raw3 = load_x(3)
         a_pool0 = load_a(0)
+        x_raw1 = load_x(1)
         a_pool1 = load_a(1)
         a_pool2 = load_a(2)
+        x_raw2 = load_x(2)
         a_pool3 = load_a(3)
+        x_raw3 = load_x(3)
 
-        ones = sbuf("ones", [P, P], F32)
-        nc.gpsimd.memset(ones[:], 1.0)
+        windows = [sbuf("window%d" % n, [P, T], F32) for n in range(2)]
         ident = sbuf("ident", [P, P], F32)
         nc.gpsimd.affine_select(
             out=ident[:], in_=ones[:], pattern=[[-1, P]], compare_op=mybir.AluOpType.is_equal, fill=0.0, base=0,
             channel_multiplier=1,
         )
 
-        def zeroed_window(n):
-            window = sbuf("window%d" % n, [P, T], F32)
-            nc.gpsimd.memset(window[:], 0.0)
-            return window
-
-        window0 = zeroed_window(0)
-
         bt_scales_listed = sbuf("bt_scales_listed", [P, SLOTS], U8)
         nc.vector.tensor_copy(bt_scales_listed[:], bt_scale_pool[:].indirect(offsets[:]))
+        factor_cols = sbuf("factor_cols", [P, ROW_PASSES, PACK], F32)
+        nc.vector.tensor_tensor(factor_cols[:], us_cols, wt_cols, MULT)
         bt_scales_dealt = sbuf("bt_scales_dealt", [P, SLOTS], U8)
         nc.vector.tensor_copy(
             bt_scales_dealt[:].rearrange("p (t m) -> p t m", t=PACK),
@@ -167,17 +180,9 @@ def tile_attend_glora_ax_kernel(
                 bt_scales[QUADRANT * q : QUADRANT * q + PACK, :].bitcast(I32),
                 bt_scales_dealt[first : first + PACK, :].bitcast(I32),
             )
-        window1 = zeroed_window(1)
+        nc.gpsimd.memset(windows[0][:], 0.0)
         sc_row = sbuf("sc_row", [P, SLOTS], F32)
         nc.vector.tensor_copy(sc_row[:], sc_pool[:].indirect(offsets[:]))
-        factor_cols = sbuf("factor_cols", [P, ROW_PASSES, PACK], F32)
-        nc.vector.tensor_tensor(factor_cols[:], us_cols, wt_cols, MULT)
-        sc_turned = quarters(banks[4])
-        for t in range(PACK):
-            nc.tensor.transpose(sc_turned[:, t, :], sc_row[:, t:SLOTS:PACK], ident[:])
-        sc_cols = sbuf("sc_cols", [P, PACK], F32)
-        nc.scalar.copy(sc_cols[:], sc_turned[:, :, P - 1])
-
         bt_codes_listed = sbuf("bt_codes_listed", [P, SLOTS], U32)
         nc.vector.tensor_copy(bt_codes_listed[:], bt_word_pool[:].bitcast(U32).indirect(offsets[:]))
         bt_codes = sbuf("bt_codes", [P, SLOTS], U32)
@@ -186,26 +191,53 @@ def tile_attend_glora_ax_kernel(
             bt_codes_listed[:].bitcast(I32).rearrange("p (c n t) -> p c t n", t=PACK, n=RUN),
         )
 
-        def group_dy(raw, m0, m1, grouped, first, copy):
+        row_factor = [sbuf("row_factor%d" % g, [P, K_PASS], F32) for g in range(ROW_PASSES)]
+
+        for g in range(ROW_PASSES):
+            for t in range(PACK):
+                nc.tensor.transpose(
+                    quarters(banks[5 + g])[:, t, :], factor_cols[:, g, t : t + 1].to_broadcast([P, P]), ident[:]
+                )
+        sc_turned = quarters(banks[4])
+        for t in range(PACK):
+            nc.tensor.transpose(sc_turned[:, t, :], sc_row[:, t:SLOTS:PACK], ident[:])
+
+        def spread_factor(g, copy):
+            spread = quarters(banks[5 + g])
             copy(
-                grouped[:].rearrange("p (u m e j) -> p m j u e", u=2, e=2, j=PACK)[:, first + m0 : first + m1],
-                raw[:].rearrange("p j (m u e) -> p m j u e", u=2, e=2)[:, m0:m1],
+                row_factor[g][:].rearrange("p (u m e) -> p u m e", u=2, e=2), spread.rearrange("p (u e) m -> p u m e", u=2)
             )
 
-        def round_on_gpsimd(out, in_):
-            nc.gpsimd.tensor_scalar(out, in_, 1.0, 0.0, MULT, ADD)
+        sc_cols = sbuf("sc_cols", [P, PACK], F32)
 
         v2_tiles = [sbuf("v2_%d" % g, [P, PACK * K_PASS], BF16) for g in range(ROW_PASSES)]
+        v2_rows_mx = [mx_tiles("v2_rows%d" % g, SLOTS) for g in range(ROW_PASSES)]
+        dy_mx = [mx_tiles("dy%d" % n, PIECE) for n in range(PIECES)]
 
-        def first_product(g, t, dy_mx):
-            v = banks[t]
+        dy_grouped = [sbuf("dy_grouped%d" % n, [P, PIECE * PACK], BF16) for n in range(PIECES)]
+
+        def group_dy(n, copy, m0=0, m1=PIECE // PACK):
+            copy(
+                dy_grouped[n][:].rearrange("p (u m e j) -> p m j u e", u=2, e=2, j=PACK)[:, m0:m1],
+                dy_raw[n][:].rearrange("p j (m u e) -> p m j u e", u=2, e=2)[:, m0:m1],
+            )
+
+        def first_pass(n, t):
+            v = banks[2 * (n % 2) + t // 2][:, t % 2 * PIECE : (t % 2 + 1) * PIECE]
             cols = slice(t * P, (t + 1) * P)
             nc.tensor.matmul_mx(
-                out=v[:], lhsT=bt_codes[:, cols].bitcast(E4M3), lhsT_scale=bt_scales[:, cols],
-                rhs=dy_mx[0][:].bitcast(E5M2), rhs_scale=dy_mx[1][:], start=True, stop=True,
+                out=v, lhsT=bt_codes[:, cols].bitcast(E4M3), lhsT_scale=bt_scales[:, cols],
+                rhs=dy_mx[n][0][:].bitcast(E5M2), rhs_scale=dy_mx[n][1][:], start=True, stop=True,
             )
+
+        def scale_v(n, t):
+            g, h = divmod(n, 2)
+            v = banks[2 * (n % 2) + t // 2][:, t % 2 * PIECE : (t % 2 + 1) * PIECE]
+            rows = slice(h * P, (h + 1) * P)
             nc.vector.scalar_tensor_tensor(
-                v2_tiles[g][:, t * K_PASS : (t + 1) * K_PASS], v[:], sc_cols[:, t : t + 1], row_factor[:, g, :], MULT, MULT
+                v2_tiles[g][:].rearrange("p (t u w) -> p t u w", t=PACK, u=2)[:, t, :, rows],
+                v.rearrange("p (u w) -> p u w", u=2), sc_cols[:, t : t + 1],
+                row_factor[g][:].rearrange("p (u w) -> p u w", u=2)[:, :, rows], MULT, MULT,
             )
 
         def turn_start(words, into):
@@ -218,19 +250,10 @@ def tile_attend_glora_ax_kernel(
             bank = banks[into][:, 0 : count * 2 * P].rearrange("p (b u m) -> p b m u", b=count, u=2)
             copy(grouped.bitcast(F32).rearrange("p (b m u) -> p b m u", b=count, u=2), bank)
 
-        def turn(words, grouped, into, copy):
-            turn_start(words, into)
-            turn_finish(grouped, into, copy)
-
-        def turn_v2(g, t0, t1, into):
+        def turn_v2(g, t0, t1, into, grouped):
             words = v2_tiles[g][:].bitcast(F32).rearrange("p (t u m) -> p t u m", t=PACK, u=2)
-            turn(
-                [[words[:, t, u, :] for u in range(2)] for t in range(t0, t1)],
-                v2_rows[g][:, t0 * K_PASS : t1 * K_PASS], into, nc.scalar.copy,
-            )
-
-        def quantize_v2_rows(g, t0, t1):
-            quantize(v2_rows_mx[g], v2_rows[g][:, t0 * K_PASS : t1 * K_PASS], E5M2, first=t0 * P)
+            turn_start([[words[:, t, u, :] for u in range(2)] for t in range(t0, t1)], into)
+            turn_finish(grouped, into, nc.scalar.copy)
 
         def round_x(j, raw, rounder):
             rounded = sbuf("x_rounded%d" % j, [P, R], BF16)
@@ -239,26 +262,42 @@ def tile_attend_glora_ax_kernel(
             )
             return rounded
 
-        def turn_x(rounded, grouped, into, copy):
+        def turn_x(rounded, into):
             words = rounded[:].bitcast(F32).rearrange("p (u g m) -> p g u m", u=2, g=ROW_PASSES)
-            turn([[words[:, g, u, :] for u in range(2)] for g in range(ROW_PASSES)], grouped, into, copy)
+            turn_start([[words[:, g, u, :] for u in range(2)] for g in range(ROW_PASSES)], into)
 
-        def gather_a(j, pool):
+        def group_x(j, into, copy):
+            grouped = sbuf("x_grouped%d" % j, [P, R], BF16)
+            turn_finish(grouped[:], into, copy)
+            return grouped
+
+        def quantize_x(j, grouped):
+            mx = mx_tiles("x%d" % j, R // PACK)
+            quantize(mx, grouped[:], E4M3)
+            return mx
+
+        def gather_a(j, pool, on_scalar):
             listed = sbuf("a_listed%d" % j, [P, SLOTS], BF16)
-            if j == 0:
+            if on_scalar:
                 nc.scalar.activation(listed[:], pool[:].indirect(offsets[:]), COPY)
             else:
                 nc.vector.tensor_copy(listed[:], pool[:].indirect(offsets[:]))
             return listed
 
-        def turn_a(pair, into):
-            words = [listed[:].bitcast(F32).rearrange("p (m u) -> p u m", u=2) for listed in pair]
-            turn_start([[words[b][:, u, :] for u in range(2)] for b in range(2)], into)
+        def turn_a(j, listed, into):
+            words = listed[:].bitcast(F32).rearrange("p (m u) -> p u m", u=2)
+            for u in range(2):
+                nc.tensor.transpose(quarters(banks[into])[:, 2 * (j % 2) + u, :], words[:, u, :], ident[:])
 
-        def second_product(x_mx, first, into):
+        def group_a(h, into, copy):
+            grouped = sbuf("a_slots%d" % h, [P, 2 * K_PASS], BF16)
+            turn_finish(grouped[:], into, copy)
+            return grouped
+
+        def second_product(x_mx, into):
             da = banks[into]
             for g in range(ROW_PASSES):
-                cols = slice(first + g * P, first + (g + 1) * P)
+                cols = slice(g * P, (g + 1) * P)
                 nc.tensor.matmul_mx(
                     out=da[:], lhsT=x_mx[0][:, cols].bitcast(E4M3), lhsT_scale=x_mx[1][:, cols],
                     rhs=v2_rows_mx[g][0][:].bitcast(E5M2), rhs_scale=v2_rows_mx[g][1][:],
@@ -266,82 +305,23 @@ def tile_attend_glora_ax_kernel(
                 )
             return da
 
-        def fetch(name, da, copy, h0=0, h1=2):
-            da_sb = sbuf(name, [P, (h1 - h0) * HALF], F32)
-            copy(
-                da_sb[:].rearrange("p (m t) -> p m t", t=PACK),
-                quarters(da).rearrange("p t m -> p m t")[:, h0 * HALF // PACK : h1 * HALF // PACK],
-            )
+        def fetch(name, da, copy):
+            da_sb = sbuf(name, [P, SLOTS], F32)
+            copy(da_sb[:].rearrange("p (m t) -> p m t", t=PACK), quarters(da).rearrange("p t m -> p m t"))
             return da_sb
 
-        def scatter_half(window, h, values):
-            listed = offsets[:, h * HALF // LIST_ROWS : (h + 1) * HALF // LIST_ROWS]
-            nc.scalar.activation(window[:].indirect(listed), values, COPY)
+        def scatter_and_store(j, da_sb):
+            nc.scalar.activation(windows[j % 2][:].indirect(offsets[:]), da_sb[:], COPY, scale=one[:])
+            (nc.sync if j < 2 else nc.scalar).dma_start(out_0[j * P : (j + 1) * P, :], windows[j % 2][:])
 
-        def fetch_half(j, h, da):
-            return fetch("da_sb%d_%d" % (j, h), da, nc.scalar.copy, h, h + 1)
+        def copy_on_gpsimd(out, in_):
+            nc.gpsimd.tensor_scalar(out, in_, 1.0, 0.0, MULT, ADD)
 
-        def store_window(j, window, queue):
-            queue.dma_start(out_0[j * P : (j + 1) * P, :], window[:])
-
-        v2_rows = [sbuf("v2_rows%d" % g, [P, SLOTS * PACK], BF16) for g in range(ROW_PASSES)]
-        v2_rows_mx = [mx_tiles("v2_rows%d" % g, SLOTS) for g in range(ROW_PASSES)]
-        dy_mx = [mx_tiles("dy%d" % g, K_PASS) for g in range(ROW_PASSES)]
-        dy_grouped = [sbuf("dy_grouped%d" % g, [P, K_PASS * PACK], BF16) for g in range(ROW_PASSES)]
-        group_dy(dy_raw0, 0, SCALAR_DY_QUADS, dy_grouped[0], 0, nc.scalar.copy)
-        group_dy(dy_raw0, SCALAR_DY_QUADS, P, dy_grouped[0], 0, nc.vector.tensor_copy)
-        quantize(dy_mx[0], dy_grouped[0][:], E5M2)
-        row_factor = sbuf("row_factor", [P, ROW_PASSES, K_PASS], F32)
-        for g in range(ROW_PASSES):
-            spread = quarters(banks[5 + g])
-            for t in range(PACK):
-                nc.tensor.transpose(spread[:, t, :], factor_cols[:, g, t : t + 1].to_broadcast([P, P]), ident[:])
-            nc.vector.tensor_copy(
-                row_factor[:, g, :].rearrange("p (u m e) -> p u m e", u=2, e=2), spread.rearrange("p (u e) m -> p u m e", u=2)
-            )
-        window2 = zeroed_window(2)
-        for h in range(2):
-            group_dy(dy_raw1[h], 0, P // 2, dy_grouped[1], h * P // 2, nc.scalar.copy)
-        for t in range(PACK):
-            if t == 2:
-                quantize(dy_mx[1], dy_grouped[1][:], E5M2)
-            first_product(0, t, dy_mx[0])
-        turn_v2(0, 0, 2, 4)
-        x_rounded0 = round_x(0, x_raw0, nc.scalar.copy)
-        x_rounded1 = round_x(1, x_raw1, round_on_gpsimd)
-        x_rounded2 = round_x(2, x_raw2, round_on_gpsimd)
-        x_grouped = [sbuf("x_grouped%d" % j, [P, R], BF16) for j in range(PACK)]
-        x_mx = [mx_tiles("x%d" % j, R // PACK) for j in range(PACK)]
-        for t in range(PACK):
-            if t == 2:
-                turn_x(x_rounded0, x_grouped[0][:], 6, nc.scalar.copy)
-                turn_v2(0, 2, 4, 5)
-            first_product(1, t, dy_mx[1])
-        turn_v2(1, 0, 2, 4)
-        turn_v2(1, 2, 3, 6)
-        turn_v2(1, 3, 4, 5)
-        turn_x(x_rounded1, x_grouped[1][:], 4, nc.scalar.copy)
-        turn_x(x_rounded2, x_grouped[2][:], 6, nc.scalar.copy)
-        quantize_v2_rows(0, 0, 4)
-        quantize(x_mx[0], x_grouped[0][:], E4M3)
-        x_rounded3 = round_x(3, x_raw3, nc.vector.tensor_copy)
-        quantize_v2_rows(1, 0, 2)
-        quantize_v2_rows(1, 2, 4)
-        turn_x(x_rounded3, x_grouped[3][:], 3, nc.vector.tensor_copy)
-        for j in range(1, PACK):
-            quantize(x_mx[j], x_grouped[j][:], E4M3)
-        da0 = second_product(x_mx[0], 0, 0)
-        da1 = second_product(x_mx[1], 0, 1)
-        da2 = second_product(x_mx[2], 0, 7)
-        da3 = second_product(x_mx[3], 0, 2)
-        a_listed = [gather_a(0, a_pool0)]
-        da_sb0 = [fetch_half(0, h, da0) for h in range(2)]
-
-        def group_v2_slots(n, copy):
+        def group_v2_slots(n, copy, order):
             g, u = divmod(n, 2)
             grouped = sbuf("v2_slots%d" % n, [P, R], BF16)
-            src = v2_tiles[g][:].rearrange("p (t u m e) -> p u m t e", t=PACK, u=2, e=2)
-            copy(grouped[:].rearrange("p (e m t) -> p m t e", e=2, t=PACK), src[:, u])
+            src = v2_tiles[g][:].rearrange("p (t u m e) -> p u " + order, t=PACK, u=2, e=2)
+            copy(grouped[:].rearrange("p (e m t) -> p " + order, e=2, t=PACK), src[:, u])
             return grouped
 
         def quantize_v2_slots(n, grouped):
@@ -349,53 +329,109 @@ def tile_attend_glora_ax_kernel(
             quantize(mx, grouped[:], E5M2)
             return mx
 
-        v2_slots0 = group_v2_slots(0, nc.vector.tensor_copy)
-        a_listed.append(gather_a(1, a_pool1))
-        turn_a(a_listed[0:2], 4)
-        scatter_half(window0, 0, da_sb0[0][:])
-        da_sb1 = fetch("da_sb1", da1, nc.vector.tensor_copy)
-        v2_slots_mx = [quantize_v2_slots(0, v2_slots0)]
-        window3 = zeroed_window(3)
-        da_sb2 = [fetch_half(2, 0, da2)]
-        scatter_half(window0, 1, da_sb0[1][:])
-        store_window(0, window0, nc.sync)
-        nc.vector.tensor_copy(window1[:].indirect(offsets[:]), da_sb1[:])
-        store_window(1, window1, nc.sync)
-        a_listed.append(gather_a(2, a_pool2))
-        a_listed.append(gather_a(3, a_pool3))
-        scatter_half(window2, 0, da_sb2[0][:])
-        da_sb2.append(fetch_half(2, 1, da2))
-        da_sb3 = [fetch_half(3, 0, da3)]
-        scatter_half(window2, 1, da_sb2[1][:])
-        store_window(2, window2, nc.sync)
-        a_slots = [sbuf("a_slots%d" % h, [P, 2 * K_PASS], BF16) for h in range(2)]
-        scatter_half(window3, 0, da_sb3[0][:])
-        da_sb3.append(fetch_half(3, 1, da3))
-        scatter_half(window3, 1, da_sb3[1][:])
-        store_window(3, window3, nc.scalar)
-        turn_a(a_listed[2:4], 5)
-        a_mx = mx_tiles("a", D)
-        v2_slots1 = group_v2_slots(1, nc.vector.tensor_copy)
-        turn_finish(a_slots[0][:], 4, nc.vector.tensor_copy)
-        turn_finish(a_slots[1][:], 5, nc.vector.tensor_copy)
-        v2_slots_mx.append(quantize_v2_slots(1, v2_slots1))
-        quantize(a_mx, a_slots[0][:], E4M3)
-        quantize(a_mx, a_slots[1][:], E4M3, 2 * P)
-        v2_slots_mx.append(quantize_v2_slots(2, group_v2_slots(2, nc.vector.tensor_copy)))
-        v2_slots3 = group_v2_slots(3, nc.scalar.copy)
         dx = sbuf("dx", [P, R // P, D], F32)
-        for n in range(R // P):
-            if n == 2:
-                v2_slots_mx.append(quantize_v2_slots(3, v2_slots3))
-            acc = banks[(6, 0, 1, 3)[n % 4]]
+        a_mx = mx_tiles("a", D)
+
+        def third_pass(n, into):
+            acc = banks[into]
             codes, scales = v2_slots_mx[n // 2]
             cols = slice(n % 2 * P, (n % 2 + 1) * P)
             nc.tensor.matmul_mx(
                 out=acc[:], lhsT=codes[:, cols].bitcast(E5M2), lhsT_scale=scales[:, cols],
                 rhs=a_mx[0][:].bitcast(E4M3), rhs_scale=a_mx[1][:], start=True, stop=True,
             )
-            (nc.scalar.copy if n in SCALAR_OUT_TILES else nc.vector.tensor_copy)(dx[:, n, :], acc[:])
+
+        def put_out(n, into, copy):
+            copy(dx[:, n, :], banks[into][:])
             if n % 2 == 1:
                 g, c = divmod(n - 1, PACK)
                 rows = out_1[g * K_PASS : (g + 1) * K_PASS, :].rearrange("(m n) d -> m n d", n=PACK)
                 nc.sync.dma_start(rows[:, c : c + 2, :], dx[:, n - 1 : n + 1, :])
+
+        spread_factor(0, nc.scalar.copy)
+        group_dy(0, nc.scalar.copy, 0, SCALAR_DY_QUADS)
+        group_dy(0, nc.vector.tensor_copy, SCALAR_DY_QUADS)
+        quantize(dy_mx[0], dy_grouped[0][:], E5M2)
+        nc.vector.tensor_copy(sc_cols[:], sc_turned[:, :, P - 1])
+        spread_factor(1, nc.vector.tensor_copy)
+        for n in range(PIECES):
+            for t in range(PACK):
+                first_pass(n, t)
+            if n + 1 < PIECES:
+                group_dy(n + 1, nc.scalar.copy)
+                quantize(dy_mx[n + 1], dy_grouped[n + 1][:], E5M2)
+            for t in range(PACK):
+                scale_v(n, t)
+            if n == 2:
+                v2_slots = [group_v2_slots(0, copy_on_gpsimd, "e m t")]
+                x_rounded0 = round_x(0, x_raw0, nc.scalar.copy)
+                v2_rows0 = sbuf("v2_rows0", [P, SLOTS * PACK], BF16)
+                turn_v2(0, 0, 2, 4, v2_rows0[:, 0 : 2 * K_PASS])
+                turn_v2(0, 2, 4, 5, v2_rows0[:, 2 * K_PASS :])
+        V, S = nc.vector.tensor_copy, nc.scalar.copy
+        turn_x(x_rounded0, 7)
+        x_grouped0 = group_x(0, 7, S)
+        v2_rows1 = [sbuf("v2_rows1" + half, [P, 2 * K_PASS], BF16) for half in "ab"]
+        turn_v2(1, 0, 2, 0, v2_rows1[0][:])
+        turn_v2(1, 2, 4, 1, v2_rows1[1][:])
+        quantize(v2_rows_mx[0], v2_rows0[:], E5M2)
+        x_mx0 = quantize_x(0, x_grouped0)
+        quantize(v2_rows_mx[1], v2_rows1[0][:], E5M2)
+        v2_slots.append(group_v2_slots(1, V, "m t e"))
+        quantize(v2_rows_mx[1], v2_rows1[1][:], E5M2, 2 * P)
+        nc.gpsimd.memset(windows[1][:], 0.0)
+        da0 = second_product(x_mx0, 2)
+        x_rounded1 = round_x(1, x_raw1, S)
+        a_listed0 = gather_a(0, a_pool0, False)
+        a_listed1 = gather_a(1, a_pool1, True)
+        turn_x(x_rounded1, 6)
+        scatter_and_store(0, fetch("da_sb0", da0, V))
+        x_grouped1 = group_x(1, 6, V)
+        x_mx1 = quantize_x(1, x_grouped1)
+        turn_a(0, a_listed0, 2)
+        turn_a(1, a_listed1, 2)
+        a_listed2 = gather_a(2, a_pool2, False)
+        da1 = second_product(x_mx1, 1)
+        v2_slots_mx = [quantize_v2_slots(0, v2_slots[0])]
+        turn_a(2, a_listed2, 4)
+        scatter_and_store(1, fetch("da_sb1", da1, V))
+        x_rounded2 = round_x(2, x_raw2, V)
+        turn_x(x_rounded2, 7)
+        a_listed3 = gather_a(3, a_pool3, False)
+        turn_a(3, a_listed3, 4)
+        x_grouped2 = group_x(2, 7, V)
+        a_slots0 = group_a(0, 2, V)
+        x_mx2 = quantize_x(2, x_grouped2)
+        a_slots1 = group_a(1, 4, V)
+        da2 = second_product(x_mx2, 3)
+        quantize(a_mx, a_slots0[:], E4M3)
+        quantize(a_mx, a_slots1[:], E4M3, 2 * P)
+        v2_slots_mx.append(quantize_v2_slots(1, v2_slots[1]))
+        x_rounded3 = round_x(3, x_raw3, S)
+        v2_slots += [group_v2_slots(n, copy_on_gpsimd, "e m t") for n in (2, 3)]
+        third_pass(0, 0)
+        third_pass(1, 1)
+        third_pass(2, 5)
+        third_pass(3, 7)
+        da_sb2 = fetch("da_sb2", da2, S)
+        put_out(0, 0, V)
+        turn_x(x_rounded3, 0)
+        put_out(1, 1, V)
+        x_grouped3 = group_x(3, 0, V)
+        put_out(2, 5, V)
+        put_out(3, 7, V)
+        x_mx3 = quantize_x(3, x_grouped3)
+        v2_slots_mx.append(quantize_v2_slots(2, v2_slots[2]))
+        da3 = second_product(x_mx3, 6)
+        third_pass(4, 2)
+        third_pass(5, 4)
+        scatter_and_store(2, da_sb2)
+        da_sb3 = fetch("da_sb3", da3, V)
+        v2_slots_mx.append(quantize_v2_slots(3, v2_slots[3]))
+        put_out(4, 2, V)
+        third_pass(6, 1)
+        third_pass(7, 0)
+        put_out(5, 4, V)
+        put_out(6, 1, V)
+        put_out(7, 0, V)
+        scatter_and_store(3, da_sb3)

@@ -25,42 +25,38 @@ BANKS = 8
 QUADRANT = 32
 SCALE_ROWS = K_PASS // 32
 LIST_ROWS = 16
-PIECE = K_PASS // 2
-PIECES = R // PIECE
-SCALAR_DY_QUADS = 24
+SCALAR_DY_QUADS = 48
+VECTOR_OUT_TILES = (3, 4, 6)
+OUT_BANKS = (0, 1, 5, 6, 3, 4, 7, 2)
+CHUNK = K_PASS // 2
 RUN = 4
 KIB = 1024
 LAP = 64
 
 SIZES = {
-    "bt_scales_listed": SLOTS, "window0": 8 * KIB, "dy_grouped0": 2 * KIB, "sc_cols": LAP, "row_factor1": 2 * KIB,
-    "v2_slots1": 2 * KIB, "dy_grouped3": 2 * KIB, "v2_slots0": 2 * KIB, "v2_rows1a": 2 * KIB, "a_listed0": KIB,
-    "x_grouped0": 2 * KIB, "x_rounded1": 2 * KIB, "v2_rows1b": 2 * KIB, "a_listed1": KIB, "window1": 8 * KIB,
-    "x0_codes": KIB, "x_grouped1": 2 * KIB, "a_listed2": KIB, "x0_scales": 256, "x1_codes": KIB, "x1_scales": 256,
-    "x_rounded2": 2 * KIB, "x_raw2": 4 * KIB, "x_grouped2": 2 * KIB, "a_pool3": 8 * KIB, "a_slots0": 2 * KIB,
-    "v2_slots1_codes": KIB, "a_codes": 2 * KIB, "a_slots1": 2 * KIB, "v2_slots2": 2 * KIB, "v2_slots3": 2 * KIB,
-    "x_raw3": 4 * KIB, "da_sb2": 2 * KIB, "x_grouped3": 2 * KIB, "v2_slots2_codes": KIB, "v2_slots0_codes": KIB,
+    "a_pool3": 8 * KIB, "a_slots": 4 * KIB, "v2_slots0": 4 * KIB, "a_pool0": 8 * KIB, "da_sb0": 2 * KIB,
+    "a_pool1": 8 * KIB, "da_sb1": 2 * KIB, "x2_codes": KIB, "x_grouped3": 2 * KIB, "bt_scales_listed": SLOTS,
+    "window0": 8 * KIB, "dy_raw0": 8 * KIB, "sc_cols0": LAP, "row_factor1": 2 * KIB, "dy_grouped0": 4 * KIB,
+    "window1": 8 * KIB, "dy_grouped1": 4 * KIB, "x_rounded2": 2 * KIB, "x_rounded3": 2 * KIB, "v2_rows1a": 2 * KIB,
+    "a_listed1": KIB, "a_listed0": KIB, "v2_rows1b": 2 * KIB, "window2": 8 * KIB, "v2_slots1": 4 * KIB,
+    "dy_raw1b": 4 * KIB, "sc_cols1": LAP, "x_rounded0": 2 * KIB, "x3_codes": KIB, "a_listed3": KIB, "x3_scales": 256,
+    "a_listed2": KIB, "window3": 8 * KIB,
 }
 TAKEN_OVER_BY = {
+    "a_pool3": ("a_slots", "v2_slots0"),
+    "a_pool0": ("da_sb0",),
+    "a_pool1": ("da_sb1", "x2_codes", "x_grouped3"),
     "bt_scales_listed": ("window0",),
-    "dy_grouped0": ("sc_cols", "row_factor1"),
-    "row_factor1": ("v2_slots1",),
-    "dy_grouped3": ("v2_slots0",),
-    "v2_rows1a": ("a_listed0",),
-    "x_grouped0": ("x_rounded1",),
-    "v2_rows1b": ("a_listed1", "window1"),
-    "x0_codes": ("x_grouped1",),
-    "x_grouped1": ("a_listed2",),
-    "x0_scales": ("x1_codes",),
-    "x1_scales": ("x_rounded2",),
-    "x_raw2": ("x_grouped2",),
-    "a_pool3": ("a_slots0",),
-    "x_grouped2": ("v2_slots1_codes", "a_codes"),
-    "a_slots1": ("v2_slots2",),
-    "v2_slots1": ("v2_slots3",),
-    "x_raw3": ("da_sb2",),
-    "x_grouped3": ("v2_slots2_codes",),
-    "a_listed0": ("v2_slots0_codes",),
+    "dy_raw0": ("sc_cols0", "row_factor1"),
+    "dy_grouped0": ("window1",),
+    "dy_grouped1": ("x_rounded2", "x_rounded3"),
+    "v2_rows1a": ("a_listed1", "a_listed0"),
+    "v2_rows1b": ("window2",),
+    "v2_slots0": ("v2_slots1",),
+    "dy_raw1b": ("sc_cols1", "x_rounded0"),
+    "x3_codes": ("a_listed3",),
+    "x3_scales": ("a_listed2",),
+    "x_grouped3": ("window3",),
 }
 
 
@@ -112,6 +108,8 @@ def tile_attend_glora_ax_kernel(
 
         offsets = keep.tile([P, SLOTS // LIST_ROWS], U16, name="offsets")
         nc.sync.dma_start(offsets[:], offs)
+        ones = sbuf("ones", [P, P], F32)
+        nc.vector.memset(ones[:], 1.0)
         bt_scale_pool = sbuf("bt_scale_pool", [P, T], U8)
         nc.vector.memset(bt_scale_pool[0 : P - SCALE_ROWS, :].bitcast(I32), 0)
         nc.scalar.dma_start(bt_scale_pool[P - SCALE_ROWS : P, :].bitcast(I32), Bt_scales[0].bitcast(I32))
@@ -123,19 +121,20 @@ def tile_attend_glora_ax_kernel(
         wt_cols = wt_tile[:, :, 0:PACK]
         nc.scalar.dma_start(us_cols, us.rearrange("(g p t) o -> p g (t o)", g=ROW_PASSES, t=PACK))
         nc.scalar.dma_start(wt_cols, wt.rearrange("(g p t) o -> p g (t o)", g=ROW_PASSES, t=PACK))
-        ones = sbuf("ones", [P, P], F32)
-        nc.vector.memset(ones[:], 1.0)
-        one = sbuf("one", [P, 1], F32)
-        nc.vector.memset(one[:], 1.0)
+        ident = sbuf("ident", [P, P], F32)
+        nc.gpsimd.affine_select(
+            out=ident[:], in_=ones[:], pattern=[[-1, P]], compare_op=mybir.AluOpType.is_equal, fill=0.0, base=0,
+            channel_multiplier=1,
+        )
         sc_pool = sbuf("sc_pool", [P, T], F32)
         nc.vector.memset(sc_pool[0 : P - 1, :].bitcast(I32), 0)
         nc.sync.dma_start(sc_pool[P - 1 : P, :], sc[P - 1 : P, :])
         bt_word_pool = sbuf("bt_word_pool", [P, T], I32)
         nc.sync.dma_start(bt_word_pool[:], Bt_words[0].rearrange("p n t -> p (n t)").bitcast(I32))
 
-        def load_dy(n):
-            raw = sbuf("dy_raw%d" % n, [P, PACK, PIECE], F32)
-            nc.sync.dma_start(raw[:], dyT[:, n * PIECE : (n + 1) * PIECE].rearrange("(p j) r -> p j r", j=PACK))
+        def load_dy(name, r0, r1):
+            raw = sbuf(name, [P, PACK, r1 - r0], F32)
+            nc.sync.dma_start(raw[:], dyT[:, r0:r1].rearrange("(p j) r -> p j r", j=PACK))
             return raw
 
         def load_x(j):
@@ -148,22 +147,12 @@ def tile_attend_glora_ax_kernel(
             nc.sync.dma_start(pool[:], A[j * P : (j + 1) * P, :])
             return pool
 
-        dy_raw = [load_dy(n) for n in range(PIECES)]
-        x_raw0 = load_x(0)
-        a_pool0 = load_a(0)
-        x_raw1 = load_x(1)
-        a_pool1 = load_a(1)
-        a_pool2 = load_a(2)
-        x_raw2 = load_x(2)
-        a_pool3 = load_a(3)
-        x_raw3 = load_x(3)
+        dy_raw0 = load_dy("dy_raw0", 0, K_PASS)
+        dy_raw1 = [load_dy("dy_raw1" + "ab"[h], K_PASS + h * CHUNK, K_PASS + (h + 1) * CHUNK) for h in range(2)]
+        x_raw = [load_x(j) for j in range(PACK)]
+        a_pool = [load_a(j) for j in range(PACK)]
 
-        windows = [sbuf("window%d" % n, [P, T], F32) for n in range(2)]
-        ident = sbuf("ident", [P, P], F32)
-        nc.gpsimd.affine_select(
-            out=ident[:], in_=ones[:], pattern=[[-1, P]], compare_op=mybir.AluOpType.is_equal, fill=0.0, base=0,
-            channel_multiplier=1,
-        )
+        windows = [sbuf("window%d" % n, [P, T], F32) for n in range(PACK)]
 
         bt_scales_listed = sbuf("bt_scales_listed", [P, SLOTS], U8)
         nc.vector.tensor_copy(bt_scales_listed[:], bt_scale_pool[:].indirect(offsets[:]))
@@ -198,9 +187,9 @@ def tile_attend_glora_ax_kernel(
                 nc.tensor.transpose(
                     quarters(banks[5 + g])[:, t, :], factor_cols[:, g, t : t + 1].to_broadcast([P, P]), ident[:]
                 )
-        sc_turned = quarters(banks[4])
+        sc_turned = [quarters(banks[4 + 3 * h]) for h in range(2)]
         for t in range(PACK):
-            nc.tensor.transpose(sc_turned[:, t, :], sc_row[:, t:SLOTS:PACK], ident[:])
+            nc.tensor.transpose(sc_turned[t // 2][:, t % 2, :], sc_row[:, t:SLOTS:PACK], ident[:])
 
         def spread_factor(g, copy):
             spread = quarters(banks[5 + g])
@@ -208,36 +197,29 @@ def tile_attend_glora_ax_kernel(
                 row_factor[g][:].rearrange("p (u m e) -> p u m e", u=2, e=2), spread.rearrange("p (u e) m -> p u m e", u=2)
             )
 
-        sc_cols = sbuf("sc_cols", [P, PACK], F32)
+        sc_cols = [sbuf("sc_cols%d" % h, [P, 2], F32) for h in range(2)]
 
         v2_tiles = [sbuf("v2_%d" % g, [P, PACK * K_PASS], BF16) for g in range(ROW_PASSES)]
         v2_rows_mx = [mx_tiles("v2_rows%d" % g, SLOTS) for g in range(ROW_PASSES)]
-        dy_mx = [mx_tiles("dy%d" % n, PIECE) for n in range(PIECES)]
+        dy_mx = [mx_tiles("dy%d" % g, K_PASS) for g in range(ROW_PASSES)]
+        dy_grouped = [sbuf("dy_grouped%d" % g, [P, K_PASS * PACK], BF16) for g in range(ROW_PASSES)]
 
-        dy_grouped = [sbuf("dy_grouped%d" % n, [P, PIECE * PACK], BF16) for n in range(PIECES)]
-
-        def group_dy(n, copy, m0=0, m1=PIECE // PACK):
+        def group_dy(g, raw, copy, m0, m1, first=0):
             copy(
-                dy_grouped[n][:].rearrange("p (u m e j) -> p m j u e", u=2, e=2, j=PACK)[:, m0:m1],
-                dy_raw[n][:].rearrange("p j (m u e) -> p m j u e", u=2, e=2)[:, m0:m1],
+                dy_grouped[g][:].rearrange("p (u m e j) -> p m j u e", u=2, e=2, j=PACK)[:, first + m0 : first + m1],
+                raw[:].rearrange("p j (m u e) -> p m j u e", u=2, e=2)[:, m0:m1],
             )
 
-        def first_pass(n, t):
-            v = banks[2 * (n % 2) + t // 2][:, t % 2 * PIECE : (t % 2 + 1) * PIECE]
+        def first_pass(g, t):
             cols = slice(t * P, (t + 1) * P)
             nc.tensor.matmul_mx(
-                out=v, lhsT=bt_codes[:, cols].bitcast(E4M3), lhsT_scale=bt_scales[:, cols],
-                rhs=dy_mx[n][0][:].bitcast(E5M2), rhs_scale=dy_mx[n][1][:], start=True, stop=True,
+                out=banks[PACK * g + t][:], lhsT=bt_codes[:, cols].bitcast(E4M3), lhsT_scale=bt_scales[:, cols],
+                rhs=dy_mx[g][0][:].bitcast(E5M2), rhs_scale=dy_mx[g][1][:], start=True, stop=True,
             )
 
-        def scale_v(n, t):
-            g, h = divmod(n, 2)
-            v = banks[2 * (n % 2) + t // 2][:, t % 2 * PIECE : (t % 2 + 1) * PIECE]
-            rows = slice(h * P, (h + 1) * P)
+        def scale_v(g, t):
             nc.vector.scalar_tensor_tensor(
-                v2_tiles[g][:].rearrange("p (t u w) -> p t u w", t=PACK, u=2)[:, t, :, rows],
-                v.rearrange("p (u w) -> p u w", u=2), sc_cols[:, t : t + 1],
-                row_factor[g][:].rearrange("p (u w) -> p u w", u=2)[:, :, rows], MULT, MULT,
+                v2_tiles[g][:, t * K_PASS : (t + 1) * K_PASS], banks[PACK * g + t][:], sc_cols[t // 2][:, t % 2 : t % 2 + 1], row_factor[g][:], MULT, MULT
             )
 
         def turn_start(words, into):
@@ -266,15 +248,14 @@ def tile_attend_glora_ax_kernel(
             words = rounded[:].bitcast(F32).rearrange("p (u g m) -> p g u m", u=2, g=ROW_PASSES)
             turn_start([[words[:, g, u, :] for u in range(2)] for g in range(ROW_PASSES)], into)
 
-        def group_x(j, into, copy):
-            grouped = sbuf("x_grouped%d" % j, [P, R], BF16)
-            turn_finish(grouped[:], into, copy)
-            return grouped
+        x_grouped01 = sbuf("x_grouped01", [P, 2 * R], BF16)
+        x_grouped = [x_grouped01[:, 0:R], x_grouped01[:, R:]] + [sbuf("x_grouped%d" % j, [P, R], BF16)[:] for j in (2, 3)]
+        x_mx01 = mx_tiles("x01", 2 * R // PACK)
+        x_mx = [[part[:, j * R // PACK : (j + 1) * R // PACK] for part in x_mx01] for j in range(2)]
+        x_mx += [mx_tiles("x%d" % j, R // PACK) for j in (2, 3)]
 
-        def quantize_x(j, grouped):
-            mx = mx_tiles("x%d" % j, R // PACK)
-            quantize(mx, grouped[:], E4M3)
-            return mx
+        def group_x(j, into, copy):
+            turn_finish(x_grouped[j], into, copy)
 
         def gather_a(j, pool, on_scalar):
             listed = sbuf("a_listed%d" % j, [P, SLOTS], BF16)
@@ -289,17 +270,18 @@ def tile_attend_glora_ax_kernel(
             for u in range(2):
                 nc.tensor.transpose(quarters(banks[into])[:, 2 * (j % 2) + u, :], words[:, u, :], ident[:])
 
-        def group_a(h, into, copy):
-            grouped = sbuf("a_slots%d" % h, [P, 2 * K_PASS], BF16)
-            turn_finish(grouped[:], into, copy)
-            return grouped
+        a_slots = sbuf("a_slots", [P, PACK * K_PASS], BF16)
 
-        def second_product(x_mx, into):
+        def group_a(h, into, copy):
+            turn_finish(a_slots[:, 2 * h * K_PASS : 2 * (h + 1) * K_PASS], into, copy)
+
+        def second_product(j, into):
             da = banks[into]
+            codes, scales = x_mx[j]
             for g in range(ROW_PASSES):
                 cols = slice(g * P, (g + 1) * P)
                 nc.tensor.matmul_mx(
-                    out=da[:], lhsT=x_mx[0][:, cols].bitcast(E4M3), lhsT_scale=x_mx[1][:, cols],
+                    out=da[:], lhsT=codes[:, cols].bitcast(E4M3), lhsT_scale=scales[:, cols],
                     rhs=v2_rows_mx[g][0][:].bitcast(E5M2), rhs_scale=v2_rows_mx[g][1][:],
                     start=(g == 0), stop=(g == ROW_PASSES - 1),
                 )
@@ -310,32 +292,31 @@ def tile_attend_glora_ax_kernel(
             copy(da_sb[:].rearrange("p (m t) -> p m t", t=PACK), quarters(da).rearrange("p t m -> p m t"))
             return da_sb
 
-        def scatter_and_store(j, da_sb):
-            nc.scalar.activation(windows[j % 2][:].indirect(offsets[:]), da_sb[:], COPY, scale=one[:])
-            (nc.sync if j < 2 else nc.scalar).dma_start(out_0[j * P : (j + 1) * P, :], windows[j % 2][:])
+        def scatter_on_scalar(j, da_sb):
+            nc.scalar.activation(windows[j][:].indirect(offsets[:]), da_sb[:], COPY, scale=ones[:, 0:1])
+
+        def store_window(j, queue):
+            queue.dma_start(out_0[j * P : (j + 1) * P, :], windows[j][:])
 
         def copy_on_gpsimd(out, in_):
             nc.gpsimd.tensor_scalar(out, in_, 1.0, 0.0, MULT, ADD)
 
-        def group_v2_slots(n, copy, order):
-            g, u = divmod(n, 2)
-            grouped = sbuf("v2_slots%d" % n, [P, R], BF16)
-            src = v2_tiles[g][:].rearrange("p (t u m e) -> p u " + order, t=PACK, u=2, e=2)
-            copy(grouped[:].rearrange("p (e m t) -> p " + order, e=2, t=PACK), src[:, u])
-            return grouped
+        v2_slots = [sbuf("v2_slots%d" % g, [P, K_PASS * PACK], BF16) for g in range(ROW_PASSES)]
+        v2_slots_mx = [mx_tiles("v2_slots%d" % g, K_PASS) for g in range(ROW_PASSES)]
 
-        def quantize_v2_slots(n, grouped):
-            mx = mx_tiles("v2_slots%d" % n, 2 * P)
-            quantize(mx, grouped[:], E5M2)
-            return mx
+        def group_v2_slots(g, copy):
+            copy(
+                v2_slots[g][:].rearrange("p (u e m t) -> p u m t e", u=2, e=2, t=PACK),
+                v2_tiles[g][:].rearrange("p (t u m e) -> p u m t e", t=PACK, u=2, e=2),
+            )
 
         dx = sbuf("dx", [P, R // P, D], F32)
         a_mx = mx_tiles("a", D)
 
         def third_pass(n, into):
             acc = banks[into]
-            codes, scales = v2_slots_mx[n // 2]
-            cols = slice(n % 2 * P, (n % 2 + 1) * P)
+            codes, scales = v2_slots_mx[n // PACK]
+            cols = slice(n % PACK * P, (n % PACK + 1) * P)
             nc.tensor.matmul_mx(
                 out=acc[:], lhsT=codes[:, cols].bitcast(E5M2), lhsT_scale=scales[:, cols],
                 rhs=a_mx[0][:].bitcast(E4M3), rhs_scale=a_mx[1][:], start=True, stop=True,
@@ -348,90 +329,83 @@ def tile_attend_glora_ax_kernel(
                 rows = out_1[g * K_PASS : (g + 1) * K_PASS, :].rearrange("(m n) d -> m n d", n=PACK)
                 nc.sync.dma_start(rows[:, c : c + 2, :], dx[:, n - 1 : n + 1, :])
 
-        spread_factor(0, nc.scalar.copy)
-        group_dy(0, nc.scalar.copy, 0, SCALAR_DY_QUADS)
-        group_dy(0, nc.vector.tensor_copy, SCALAR_DY_QUADS)
-        quantize(dy_mx[0], dy_grouped[0][:], E5M2)
-        nc.vector.tensor_copy(sc_cols[:], sc_turned[:, :, P - 1])
-        spread_factor(1, nc.vector.tensor_copy)
-        for n in range(PIECES):
-            for t in range(PACK):
-                first_pass(n, t)
-            if n + 1 < PIECES:
-                group_dy(n + 1, nc.scalar.copy)
-                quantize(dy_mx[n + 1], dy_grouped[n + 1][:], E5M2)
-            for t in range(PACK):
-                scale_v(n, t)
-            if n == 2:
-                v2_slots = [group_v2_slots(0, copy_on_gpsimd, "e m t")]
-                x_rounded0 = round_x(0, x_raw0, nc.scalar.copy)
-                v2_rows0 = sbuf("v2_rows0", [P, SLOTS * PACK], BF16)
-                turn_v2(0, 0, 2, 4, v2_rows0[:, 0 : 2 * K_PASS])
-                turn_v2(0, 2, 4, 5, v2_rows0[:, 2 * K_PASS :])
         V, S = nc.vector.tensor_copy, nc.scalar.copy
-        turn_x(x_rounded0, 7)
-        x_grouped0 = group_x(0, 7, S)
-        v2_rows1 = [sbuf("v2_rows1" + half, [P, 2 * K_PASS], BF16) for half in "ab"]
-        turn_v2(1, 0, 2, 0, v2_rows1[0][:])
-        turn_v2(1, 2, 4, 1, v2_rows1[1][:])
-        quantize(v2_rows_mx[0], v2_rows0[:], E5M2)
-        x_mx0 = quantize_x(0, x_grouped0)
-        quantize(v2_rows_mx[1], v2_rows1[0][:], E5M2)
-        v2_slots.append(group_v2_slots(1, V, "m t e"))
-        quantize(v2_rows_mx[1], v2_rows1[1][:], E5M2, 2 * P)
+        spread_factor(0, S)
+        group_dy(0, dy_raw0, S, 0, SCALAR_DY_QUADS)
+        group_dy(0, dy_raw0, V, SCALAR_DY_QUADS, P)
+        quantize(dy_mx[0], dy_grouped[0][:], E5M2)
+        V(sc_cols[0][:], sc_turned[0][:, 0:2, P - 1])
+        spread_factor(1, V)
         nc.gpsimd.memset(windows[1][:], 0.0)
-        da0 = second_product(x_mx0, 2)
-        x_rounded1 = round_x(1, x_raw1, S)
-        a_listed0 = gather_a(0, a_pool0, False)
-        a_listed1 = gather_a(1, a_pool1, True)
-        turn_x(x_rounded1, 6)
-        scatter_and_store(0, fetch("da_sb0", da0, V))
-        x_grouped1 = group_x(1, 6, V)
-        x_mx1 = quantize_x(1, x_grouped1)
-        turn_a(0, a_listed0, 2)
-        turn_a(1, a_listed1, 2)
-        a_listed2 = gather_a(2, a_pool2, False)
-        da1 = second_product(x_mx1, 1)
-        v2_slots_mx = [quantize_v2_slots(0, v2_slots[0])]
-        turn_a(2, a_listed2, 4)
-        scatter_and_store(1, fetch("da_sb1", da1, V))
-        x_rounded2 = round_x(2, x_raw2, V)
-        turn_x(x_rounded2, 7)
-        a_listed3 = gather_a(3, a_pool3, False)
-        turn_a(3, a_listed3, 4)
-        x_grouped2 = group_x(2, 7, V)
-        a_slots0 = group_a(0, 2, V)
-        x_mx2 = quantize_x(2, x_grouped2)
-        a_slots1 = group_a(1, 4, V)
-        da2 = second_product(x_mx2, 3)
-        quantize(a_mx, a_slots0[:], E4M3)
-        quantize(a_mx, a_slots1[:], E4M3, 2 * P)
-        v2_slots_mx.append(quantize_v2_slots(1, v2_slots[1]))
-        x_rounded3 = round_x(3, x_raw3, S)
-        v2_slots += [group_v2_slots(n, copy_on_gpsimd, "e m t") for n in (2, 3)]
-        third_pass(0, 0)
-        third_pass(1, 1)
-        third_pass(2, 5)
-        third_pass(3, 7)
-        da_sb2 = fetch("da_sb2", da2, S)
-        put_out(0, 0, V)
-        turn_x(x_rounded3, 0)
-        put_out(1, 1, V)
-        x_grouped3 = group_x(3, 0, V)
-        put_out(2, 5, V)
-        put_out(3, 7, V)
-        x_mx3 = quantize_x(3, x_grouped3)
-        v2_slots_mx.append(quantize_v2_slots(2, v2_slots[2]))
-        da3 = second_product(x_mx3, 6)
-        third_pass(4, 2)
-        third_pass(5, 4)
-        scatter_and_store(2, da_sb2)
+        for h in range(2):
+            group_dy(1, dy_raw1[h], S, 0, P // 2, h * P // 2)
+        S(sc_cols[1][:], sc_turned[1][:, 0:2, P - 1])
+        for t in range(PACK):
+            first_pass(0, t)
+        scale_v(0, 0)
+        scale_v(0, 1)
+        quantize(dy_mx[1], dy_grouped[1][:], E5M2)
+        scale_v(0, 2)
+        scale_v(0, 3)
+        for t in range(PACK):
+            first_pass(1, t)
+        x_rounded = [round_x(0, x_raw[0], S)]
+        v2_rows0 = sbuf("v2_rows0", [P, SLOTS * PACK], BF16)
+        v2_rows1 = [sbuf("v2_rows1" + half, [P, 2 * K_PASS], BF16) for half in "ab"]
+        turn_v2(0, 0, 2, 0, v2_rows0[:, 0 : 2 * K_PASS])
+        x_rounded += [round_x(j, x_raw[j], S if j == 1 else copy_on_gpsimd) for j in range(1, PACK)]
+        turn_x(x_rounded[0], 1)
+        group_x(0, 1, S)
+        turn_v2(0, 2, 4, 2, v2_rows0[:, 2 * K_PASS :])
+        for t in range(PACK):
+            scale_v(1, t)
+        turn_x(x_rounded[1], 3)
+        group_x(1, 3, S)
+        turn_v2(1, 0, 2, 4, v2_rows1[0][:])
+        turn_x(x_rounded[2], 1)
+        turn_v2(1, 2, 4, 6, v2_rows1[1][:])
+        group_x(2, 1, S)
+        quantize(v2_rows_mx[0], v2_rows0[:], E5M2)
+        quantize(x_mx01, x_grouped01[:], E4M3)
+        quantize(v2_rows_mx[1], v2_rows1[0][:], E5M2)
+        quantize(v2_rows_mx[1], v2_rows1[1][:], E5M2, 2 * P)
+        nc.gpsimd.memset(windows[2][:], 0.0)
+        da0 = second_product(0, 0)
+        da1 = second_product(1, 5)
+        turn_x(x_rounded[3], 1)
+        a_listed = [gather_a(0, a_pool[0], True), gather_a(1, a_pool[1], False)]
+        scatter_on_scalar(0, fetch("da_sb0", da0, S))
+        store_window(0, nc.sync)
+        da_sb1 = fetch("da_sb1", da1, V)
+        group_x(3, 1, V)
+        quantize(x_mx[2], x_grouped[2], E4M3)
+        quantize(x_mx[3], x_grouped[3], E4M3)
+        nc.gpsimd.memset(windows[3][:], 0.0)
+        nc.vector.tensor_copy(windows[1][:].indirect(offsets[:]), da_sb1[:])
+        store_window(1, nc.sync)
+        turn_a(0, a_listed[0], 7)
+        turn_a(1, a_listed[1], 7)
+        da2 = second_product(2, 3)
+        da3 = second_product(3, 4)
+        scatter_on_scalar(2, fetch("da_sb2", da2, S))
+        store_window(2, nc.sync)
         da_sb3 = fetch("da_sb3", da3, V)
-        v2_slots_mx.append(quantize_v2_slots(3, v2_slots[3]))
-        put_out(4, 2, V)
-        third_pass(6, 1)
-        third_pass(7, 0)
-        put_out(5, 4, V)
-        put_out(6, 1, V)
-        put_out(7, 0, V)
-        scatter_and_store(3, da_sb3)
+        for j in range(2, PACK):
+            a_listed.append(gather_a(j, a_pool[j], False))
+            turn_a(j, a_listed[j], 2)
+        scatter_on_scalar(3, da_sb3)
+        store_window(3, nc.sync)
+        group_a(0, 7, V)
+        group_v2_slots(0, V)
+        group_a(1, 2, V)
+        quantize(v2_slots_mx[0], v2_slots[0][:], E5M2)
+        quantize(a_mx, a_slots[:], E4M3)
+        group_v2_slots(1, V)
+        for n in range(PACK):
+            third_pass(n, OUT_BANKS[n])
+        put_out(0, OUT_BANKS[0], V)
+        quantize(v2_slots_mx[1], v2_slots[1][:], E5M2)
+        for n in range(PACK, 2 * PACK):
+            third_pass(n, OUT_BANKS[n])
+        for n in range(1, 2 * PACK):
+            put_out(n, OUT_BANKS[n], V if n in VECTOR_OUT_TILES else S)

@@ -26,7 +26,7 @@ QUADRANT = 32
 SCALE_ROWS = K_PASS // 32
 LIST_ROWS = 16
 SCALAR_DY_QUADS = 48
-VECTOR_OUT_TILES = (3, 4, 6)
+VECTOR_OUT_TILES = (2, 4, 6)
 OUT_BANKS = (0, 1, 5, 6, 3, 4, 7, 2)
 CHUNK = K_PASS // 2
 RUN = 4
@@ -34,29 +34,35 @@ KIB = 1024
 LAP = 64
 
 SIZES = {
-    "a_pool3": 8 * KIB, "a_slots": 4 * KIB, "v2_slots0": 4 * KIB, "a_pool0": 8 * KIB, "da_sb0": 2 * KIB,
-    "a_pool1": 8 * KIB, "da_sb1": 2 * KIB, "x2_codes": KIB, "x_grouped3": 2 * KIB, "bt_scales_listed": SLOTS,
-    "window0": 8 * KIB, "dy_raw0": 8 * KIB, "sc_cols0": LAP, "row_factor1": 2 * KIB, "dy_grouped0": 4 * KIB,
-    "window1": 8 * KIB, "dy_grouped1": 4 * KIB, "x_rounded2": 2 * KIB, "x_rounded3": 2 * KIB, "v2_rows1a": 2 * KIB,
-    "a_listed1": KIB, "a_listed0": KIB, "v2_rows1b": 2 * KIB, "window2": 8 * KIB, "v2_slots1": 4 * KIB,
-    "dy_raw1b": 4 * KIB, "sc_cols1": LAP, "x_rounded0": 2 * KIB, "x3_codes": KIB, "a_listed3": KIB, "x3_scales": 256,
-    "a_listed2": KIB, "window3": 8 * KIB,
+    "a_pool3": 8 * KIB, "v2_slots0b": 2 * KIB, "a_pool0": 8 * KIB, "da_sb0": 2 * KIB, "a_pool1": 8 * KIB,
+    "da_sb1": 2 * KIB, "v2_slots0a": 2 * KIB, "x_grouped3": 2 * KIB, "bt_scales_listed": SLOTS, "window0": 8 * KIB,
+    "dy_raw0": 8 * KIB, "sc_cols0": LAP, "row_factor1": 2 * KIB, "dy_grouped0": 4 * KIB, "window1": 8 * KIB,
+    "dy_grouped1": 4 * KIB, "x_rounded2": 2 * KIB, "x_rounded3": 2 * KIB, "v2_rows1a": 2 * KIB, "a_listed0": KIB,
+    "a_listed1": KIB, "x2_codes": KIB, "dy_raw1b": 4 * KIB, "sc_cols1": LAP, "x3_codes": KIB, "a_listed3": KIB,
+    "x3_scales": 256, "a_listed2": KIB, "window3": 8 * KIB, "x_grouped2": 2 * KIB, "window2": 8 * KIB,
+    "v2_slots0_codes": KIB, "v2_slots1_codes": KIB, "a_slots": 4 * KIB, "v2_slots1a": 2 * KIB, "da_sb3": 2 * KIB,
+    "v2_slots1b": 2 * KIB, "v2_slots3_codes": KIB,
 }
 TAKEN_OVER_BY = {
-    "a_pool3": ("a_slots", "v2_slots0"),
+    "a_pool3": ("v2_slots0b",),
     "a_pool0": ("da_sb0",),
-    "a_pool1": ("da_sb1", "x2_codes", "x_grouped3"),
+    "a_pool1": ("da_sb1", "v2_slots0a", "x_grouped3"),
     "bt_scales_listed": ("window0",),
     "dy_raw0": ("sc_cols0", "row_factor1"),
     "dy_grouped0": ("window1",),
     "dy_grouped1": ("x_rounded2", "x_rounded3"),
-    "v2_rows1a": ("a_listed1", "a_listed0"),
-    "v2_rows1b": ("window2",),
-    "v2_slots0": ("v2_slots1",),
-    "dy_raw1b": ("sc_cols1", "x_rounded0"),
+    "v2_rows1a": ("a_listed0", "a_listed1"),
+    "a_listed1": ("x2_codes",),
+    "dy_raw1b": ("sc_cols1",),
     "x3_codes": ("a_listed3",),
     "x3_scales": ("a_listed2",),
     "x_grouped3": ("window3",),
+    "x_grouped2": ("window2",),
+    "a_listed3": ("v2_slots0_codes",),
+    "v2_slots0a": ("v2_slots1_codes",),
+    "a_slots": ("v2_slots1a",),
+    "da_sb3": ("v2_slots1b",),
+    "v2_slots1a": ("v2_slots3_codes",),
 }
 
 
@@ -113,8 +119,6 @@ def tile_attend_glora_ax_kernel(
         bt_scale_pool = sbuf("bt_scale_pool", [P, T], U8)
         nc.vector.memset(bt_scale_pool[0 : P - SCALE_ROWS, :].bitcast(I32), 0)
         nc.scalar.dma_start(bt_scale_pool[P - SCALE_ROWS : P, :].bitcast(I32), Bt_scales[0].bitcast(I32))
-        bt_scales = sbuf("bt_scales", [P, SLOTS], U8)
-        nc.vector.memset(bt_scales[:].bitcast(I32), 0)
         us_tile = sbuf("us_tile", [P, ROW_PASSES, 2 * PACK], F32)
         us_cols = us_tile[:, :, 0:PACK]
         wt_tile = sbuf("wt_tile", [P, ROW_PASSES, 2 * PACK], F32)
@@ -158,16 +162,16 @@ def tile_attend_glora_ax_kernel(
         nc.vector.tensor_copy(bt_scales_listed[:], bt_scale_pool[:].indirect(offsets[:]))
         factor_cols = sbuf("factor_cols", [P, ROW_PASSES, PACK], F32)
         nc.vector.tensor_tensor(factor_cols[:], us_cols, wt_cols, MULT)
-        bt_scales_dealt = sbuf("bt_scales_dealt", [P, SLOTS], U8)
+        bt_scales = sbuf("bt_scales", [P, SLOTS], U8)
         nc.vector.tensor_copy(
-            bt_scales_dealt[:].rearrange("p (t m) -> p t m", t=PACK),
+            bt_scales[:].rearrange("p (t m) -> p t m", t=PACK),
             bt_scales_listed[:].rearrange("p (m t) -> p t m", t=PACK),
         )
         for q in range(P // QUADRANT):
             first = P - SCALE_ROWS + PACK * q
             nc.scalar.dma_start(
                 bt_scales[QUADRANT * q : QUADRANT * q + PACK, :].bitcast(I32),
-                bt_scales_dealt[first : first + PACK, :].bitcast(I32),
+                bt_scales[first : first + PACK, :].bitcast(I32),
             )
         nc.gpsimd.memset(windows[0][:], 0.0)
         sc_row = sbuf("sc_row", [P, SLOTS], F32)
@@ -301,22 +305,25 @@ def tile_attend_glora_ax_kernel(
         def copy_on_gpsimd(out, in_):
             nc.gpsimd.tensor_scalar(out, in_, 1.0, 0.0, MULT, ADD)
 
-        v2_slots = [sbuf("v2_slots%d" % g, [P, K_PASS * PACK], BF16) for g in range(ROW_PASSES)]
-        v2_slots_mx = [mx_tiles("v2_slots%d" % g, K_PASS) for g in range(ROW_PASSES)]
+        v2_slots_mx = [mx_tiles("v2_slots%d" % n, 2 * P) for n in range(PACK)]
 
-        def group_v2_slots(g, copy):
-            copy(
-                v2_slots[g][:].rearrange("p (u e m t) -> p u m t e", u=2, e=2, t=PACK),
-                v2_tiles[g][:].rearrange("p (t u m e) -> p u m t e", t=PACK, u=2, e=2),
-            )
+        def group_v2_slots(name, g, u0, u1, copy, order="m t e"):
+            grouped = sbuf(name, [P, (u1 - u0) * R], BF16)
+            src = v2_tiles[g][:].rearrange("p (t u m e) -> p u " + order, t=PACK, u=2, e=2)
+            dst = grouped[:].rearrange("p (u e m t) -> p u " + order, e=2, m=P, t=PACK)
+            if u1 - u0 == 1:
+                copy(dst[:, 0], src[:, u0])
+            else:
+                copy(dst, src)
+            return grouped
 
         dx = sbuf("dx", [P, R // P, D], F32)
         a_mx = mx_tiles("a", D)
 
         def third_pass(n, into):
             acc = banks[into]
-            codes, scales = v2_slots_mx[n // PACK]
-            cols = slice(n % PACK * P, (n % PACK + 1) * P)
+            codes, scales = v2_slots_mx[n // 2]
+            cols = slice(n % 2 * P, (n % 2 + 1) * P)
             nc.tensor.matmul_mx(
                 out=acc[:], lhsT=codes[:, cols].bitcast(E5M2), lhsT_scale=scales[:, cols],
                 rhs=a_mx[0][:].bitcast(E4M3), rhs_scale=a_mx[1][:], start=True, stop=True,
@@ -339,11 +346,11 @@ def tile_attend_glora_ax_kernel(
         nc.gpsimd.memset(windows[1][:], 0.0)
         for h in range(2):
             group_dy(1, dy_raw1[h], S, 0, P // 2, h * P // 2)
-        S(sc_cols[1][:], sc_turned[1][:, 0:2, P - 1])
         for t in range(PACK):
             first_pass(0, t)
         scale_v(0, 0)
         scale_v(0, 1)
+        V(sc_cols[1][:], sc_turned[1][:, 0:2, P - 1])
         quantize(dy_mx[1], dy_grouped[1][:], E5M2)
         scale_v(0, 2)
         scale_v(0, 3)
@@ -369,22 +376,24 @@ def tile_attend_glora_ax_kernel(
         quantize(x_mx01, x_grouped01[:], E4M3)
         quantize(v2_rows_mx[1], v2_rows1[0][:], E5M2)
         quantize(v2_rows_mx[1], v2_rows1[1][:], E5M2, 2 * P)
-        nc.gpsimd.memset(windows[2][:], 0.0)
         da0 = second_product(0, 0)
         da1 = second_product(1, 5)
         turn_x(x_rounded[3], 1)
         a_listed = [gather_a(0, a_pool[0], True), gather_a(1, a_pool[1], False)]
         scatter_on_scalar(0, fetch("da_sb0", da0, S))
         store_window(0, nc.sync)
+        turn_a(0, a_listed[0], 7)
+        turn_a(1, a_listed[1], 7)
+        v2_slots0a = group_v2_slots("v2_slots0a", 0, 0, 1, copy_on_gpsimd, "e m t")
         da_sb1 = fetch("da_sb1", da1, V)
         group_x(3, 1, V)
+        group_a(0, 7, V)
         quantize(x_mx[2], x_grouped[2], E4M3)
         quantize(x_mx[3], x_grouped[3], E4M3)
+        nc.gpsimd.memset(windows[2][:], 0.0)
         nc.gpsimd.memset(windows[3][:], 0.0)
         nc.vector.tensor_copy(windows[1][:].indirect(offsets[:]), da_sb1[:])
         store_window(1, nc.sync)
-        turn_a(0, a_listed[0], 7)
-        turn_a(1, a_listed[1], 7)
         da2 = second_product(2, 3)
         da3 = second_product(3, 4)
         scatter_on_scalar(2, fetch("da_sb2", da2, S))
@@ -395,17 +404,20 @@ def tile_attend_glora_ax_kernel(
             turn_a(j, a_listed[j], 2)
         scatter_on_scalar(3, da_sb3)
         store_window(3, nc.sync)
-        group_a(0, 7, V)
-        group_v2_slots(0, V)
+        v2_slots0b = group_v2_slots("v2_slots0b", 0, 1, 2, V)
         group_a(1, 2, V)
-        quantize(v2_slots_mx[0], v2_slots[0][:], E5M2)
+        quantize(v2_slots_mx[0], v2_slots0a[:], E5M2)
         quantize(a_mx, a_slots[:], E4M3)
-        group_v2_slots(1, V)
+        quantize(v2_slots_mx[1], v2_slots0b[:], E5M2)
+        v2_slots1b = group_v2_slots("v2_slots1b", 1, 1, 2, S)
+        v2_slots1a = group_v2_slots("v2_slots1a", 1, 0, 1, V)
         for n in range(PACK):
             third_pass(n, OUT_BANKS[n])
         put_out(0, OUT_BANKS[0], V)
-        quantize(v2_slots_mx[1], v2_slots[1][:], E5M2)
+        quantize(v2_slots_mx[2], v2_slots1a[:], E5M2)
+        put_out(1, OUT_BANKS[1], S)
+        quantize(v2_slots_mx[3], v2_slots1b[:], E5M2)
         for n in range(PACK, 2 * PACK):
             third_pass(n, OUT_BANKS[n])
-        for n in range(1, 2 * PACK):
+        for n in range(2, 2 * PACK):
             put_out(n, OUT_BANKS[n], V if n in VECTOR_OUT_TILES else S)

@@ -29,24 +29,25 @@ SCALAR_DY_QUADS = 48
 VECTOR_OUT_TILES = (2, 4, 6)
 OUT_BANKS = (0, 1, 5, 6, 3, 4, 7, 2)
 CHUNK = K_PASS // 2
+WINDOWS = 3
 RUN = 4
 KIB = 1024
 LAP = 64
 
 SIZES = {
-    "a_pool3": 8 * KIB, "v2_slots0b": 2 * KIB, "a_pool0": 8 * KIB, "da_sb0": 2 * KIB, "a_pool1": 8 * KIB,
-    "da_sb1": 2 * KIB, "v2_slots0a": 2 * KIB, "x_grouped3": 2 * KIB, "bt_scales_listed": SLOTS, "window0": 8 * KIB,
-    "dy_raw0": 8 * KIB, "sc_cols0": LAP, "row_factor1": 2 * KIB, "dy_grouped0": 4 * KIB, "window1": 8 * KIB,
-    "dy_grouped1": 4 * KIB, "x_rounded2": 2 * KIB, "x_rounded3": 2 * KIB, "v2_rows1a": 2 * KIB, "a_listed0": KIB,
-    "a_listed1": KIB, "x2_codes": KIB, "dy_raw1b": 4 * KIB, "sc_cols1": LAP, "x3_codes": KIB, "a_listed3": KIB,
-    "x3_scales": 256, "a_listed2": KIB, "window3": 8 * KIB, "x_grouped2": 2 * KIB, "window2": 8 * KIB,
-    "v2_slots0_codes": KIB, "v2_slots1_codes": KIB, "a_slots": 4 * KIB, "v2_slots1a": 2 * KIB, "da_sb3": 2 * KIB,
-    "v2_slots1b": 2 * KIB, "v2_slots3_codes": KIB,
+    "a_pool3": 8 * KIB, "v2_slots0a": 2 * KIB, "v2_slots0b": 2 * KIB, "a_pool0": 8 * KIB, "da_sb0": 2 * KIB,
+    "a_pool1": 8 * KIB, "da_sb1": 2 * KIB, "x_grouped3": 2 * KIB, "window2": 8 * KIB, "bt_scales_listed": SLOTS,
+    "window0": 8 * KIB, "dy_raw0": 8 * KIB, "sc_cols0": LAP, "row_factor1": 2 * KIB, "dy_grouped0": 4 * KIB,
+    "window1": 8 * KIB, "dy_grouped1": 4 * KIB, "x_rounded2": 2 * KIB, "x_rounded3": 2 * KIB, "v2_rows1a": 2 * KIB,
+    "a_listed0": KIB, "a_listed1": KIB, "x2_codes": KIB, "dy_raw1b": 4 * KIB, "sc_cols1": LAP, "x3_codes": KIB,
+    "a_listed3": KIB, "x3_scales": 256, "a_listed2": KIB, "a_slots": 4 * KIB, "v2_slots1a": 2 * KIB,
+    "v2_slots3_codes": KIB, "da_sb3": 2 * KIB, "v2_slots1b": 2 * KIB,
 }
 TAKEN_OVER_BY = {
-    "a_pool3": ("v2_slots0b",),
+    "a_pool3": ("v2_slots0a",),
+    "v2_slots0a": ("v2_slots0b",),
     "a_pool0": ("da_sb0",),
-    "a_pool1": ("da_sb1", "v2_slots0a", "x_grouped3"),
+    "a_pool1": ("da_sb1", "x_grouped3", "window2"),
     "bt_scales_listed": ("window0",),
     "dy_raw0": ("sc_cols0", "row_factor1"),
     "dy_grouped0": ("window1",),
@@ -56,13 +57,9 @@ TAKEN_OVER_BY = {
     "dy_raw1b": ("sc_cols1",),
     "x3_codes": ("a_listed3",),
     "x3_scales": ("a_listed2",),
-    "x_grouped3": ("window3",),
-    "x_grouped2": ("window2",),
-    "a_listed3": ("v2_slots0_codes",),
-    "v2_slots0a": ("v2_slots1_codes",),
     "a_slots": ("v2_slots1a",),
-    "da_sb3": ("v2_slots1b",),
     "v2_slots1a": ("v2_slots3_codes",),
+    "da_sb3": ("v2_slots1b",),
 }
 
 
@@ -156,7 +153,7 @@ def tile_attend_glora_ax_kernel(
         x_raw = [load_x(j) for j in range(PACK)]
         a_pool = [load_a(j) for j in range(PACK)]
 
-        windows = [sbuf("window%d" % n, [P, T], F32) for n in range(PACK)]
+        windows = [sbuf("window%d" % n, [P, T], F32) for n in range(WINDOWS)]
 
         bt_scales_listed = sbuf("bt_scales_listed", [P, SLOTS], U8)
         nc.vector.tensor_copy(bt_scales_listed[:], bt_scale_pool[:].indirect(offsets[:]))
@@ -297,10 +294,10 @@ def tile_attend_glora_ax_kernel(
             return da_sb
 
         def scatter_on_scalar(j, da_sb):
-            nc.scalar.activation(windows[j][:].indirect(offsets[:]), da_sb[:], COPY, scale=ones[:, 0:1])
+            nc.scalar.activation(windows[j % WINDOWS][:].indirect(offsets[:]), da_sb[:], COPY, scale=ones[:, 0:1])
 
         def store_window(j, queue):
-            queue.dma_start(out_0[j * P : (j + 1) * P, :], windows[j][:])
+            queue.dma_start(out_0[j * P : (j + 1) * P, :], windows[j % WINDOWS][:])
 
         def copy_on_gpsimd(out, in_):
             nc.gpsimd.tensor_scalar(out, in_, 1.0, 0.0, MULT, ADD)
@@ -384,14 +381,12 @@ def tile_attend_glora_ax_kernel(
         store_window(0, nc.sync)
         turn_a(0, a_listed[0], 7)
         turn_a(1, a_listed[1], 7)
-        v2_slots0a = group_v2_slots("v2_slots0a", 0, 0, 1, copy_on_gpsimd, "e m t")
+        nc.gpsimd.memset(windows[2][:], 0.0)
         da_sb1 = fetch("da_sb1", da1, V)
         group_x(3, 1, V)
         group_a(0, 7, V)
         quantize(x_mx[2], x_grouped[2], E4M3)
         quantize(x_mx[3], x_grouped[3], E4M3)
-        nc.gpsimd.memset(windows[2][:], 0.0)
-        nc.gpsimd.memset(windows[3][:], 0.0)
         nc.vector.tensor_copy(windows[1][:].indirect(offsets[:]), da_sb1[:])
         store_window(1, nc.sync)
         da2 = second_product(2, 3)
@@ -404,13 +399,14 @@ def tile_attend_glora_ax_kernel(
             turn_a(j, a_listed[j], 2)
         scatter_on_scalar(3, da_sb3)
         store_window(3, nc.sync)
-        v2_slots0b = group_v2_slots("v2_slots0b", 0, 1, 2, V)
+        v2_slots0a = group_v2_slots("v2_slots0a", 0, 0, 1, V)
         group_a(1, 2, V)
         quantize(v2_slots_mx[0], v2_slots0a[:], E5M2)
         quantize(a_mx, a_slots[:], E4M3)
+        v2_slots0b = group_v2_slots("v2_slots0b", 0, 1, 2, V)
+        v2_slots1a = group_v2_slots("v2_slots1a", 1, 0, 1, V)
         quantize(v2_slots_mx[1], v2_slots0b[:], E5M2)
         v2_slots1b = group_v2_slots("v2_slots1b", 1, 1, 2, S)
-        v2_slots1a = group_v2_slots("v2_slots1a", 1, 0, 1, V)
         for n in range(PACK):
             third_pass(n, OUT_BANKS[n])
         put_out(0, OUT_BANKS[0], V)

@@ -29,25 +29,26 @@ SCALAR_DY_QUADS = 48
 VECTOR_OUT_TILES = (2, 4, 6)
 OUT_BANKS = (0, 1, 5, 6, 3, 4, 7, 2)
 CHUNK = K_PASS // 2
-WINDOWS = 3
 RUN = 4
 KIB = 1024
 LAP = 64
 
 SIZES = {
     "a_pool3": 8 * KIB, "v2_slots0a": 2 * KIB, "v2_slots0b": 2 * KIB, "a_pool0": 8 * KIB, "da_sb0": 2 * KIB,
-    "a_pool1": 8 * KIB, "da_sb1": 2 * KIB, "x_grouped3": 2 * KIB, "window2": 8 * KIB, "bt_scales_listed": SLOTS,
-    "window0": 8 * KIB, "dy_raw0": 8 * KIB, "sc_cols0": LAP, "row_factor1": 2 * KIB, "dy_grouped0": 4 * KIB,
-    "window1": 8 * KIB, "dy_grouped1": 4 * KIB, "x_rounded2": 2 * KIB, "x_rounded3": 2 * KIB, "v2_rows1a": 2 * KIB,
-    "a_listed0": KIB, "a_listed1": KIB, "x2_codes": KIB, "dy_raw1b": 4 * KIB, "sc_cols1": LAP, "x3_codes": KIB,
-    "a_listed3": KIB, "x3_scales": 256, "a_listed2": KIB, "a_slots": 4 * KIB, "v2_slots1a": 2 * KIB,
-    "v2_slots3_codes": KIB, "da_sb3": 2 * KIB, "v2_slots1b": 2 * KIB,
+    "a_pool1": 8 * KIB, "da_sb1": 2 * KIB, "x_grouped3": 2 * KIB, "window3": 8 * KIB, "v2_rows1b": 2 * KIB,
+    "window2": 8 * KIB, "bt_scales_listed": SLOTS, "window0": 8 * KIB, "dy_raw0": 8 * KIB, "sc_cols0": LAP,
+    "row_factor1": 2 * KIB, "dy_grouped0": 4 * KIB, "window1": 8 * KIB, "dy_grouped1": 4 * KIB, "x_rounded2": 2 * KIB,
+    "x_rounded3": 2 * KIB, "v2_rows1a": 2 * KIB, "a_listed0": KIB, "a_listed1": KIB, "x2_codes": KIB,
+    "dy_raw1b": 4 * KIB, "sc_cols1": LAP, "x3_codes": KIB, "a_listed3": KIB, "x3_scales": 256, "a_listed2": KIB,
+    "a_slots": 4 * KIB, "v2_slots1a": 2 * KIB, "v2_slots3_codes": KIB, "da_sb3": 2 * KIB, "v2_slots1b": 2 * KIB,
 }
 TAKEN_OVER_BY = {
     "a_pool3": ("v2_slots0a",),
     "v2_slots0a": ("v2_slots0b",),
     "a_pool0": ("da_sb0",),
-    "a_pool1": ("da_sb1", "x_grouped3", "window2"),
+    "a_pool1": ("da_sb1", "x_grouped3"),
+    "x_grouped3": ("window3",),
+    "v2_rows1b": ("window2",),
     "bt_scales_listed": ("window0",),
     "dy_raw0": ("sc_cols0", "row_factor1"),
     "dy_grouped0": ("window1",),
@@ -153,7 +154,7 @@ def tile_attend_glora_ax_kernel(
         x_raw = [load_x(j) for j in range(PACK)]
         a_pool = [load_a(j) for j in range(PACK)]
 
-        windows = [sbuf("window%d" % n, [P, T], F32) for n in range(WINDOWS)]
+        windows = [sbuf("window%d" % n, [P, T], F32) for n in range(PACK)]
 
         bt_scales_listed = sbuf("bt_scales_listed", [P, SLOTS], U8)
         nc.vector.tensor_copy(bt_scales_listed[:], bt_scale_pool[:].indirect(offsets[:]))
@@ -294,10 +295,10 @@ def tile_attend_glora_ax_kernel(
             return da_sb
 
         def scatter_on_scalar(j, da_sb):
-            nc.scalar.activation(windows[j % WINDOWS][:].indirect(offsets[:]), da_sb[:], COPY, scale=ones[:, 0:1])
+            nc.scalar.activation(windows[j][:].indirect(offsets[:]), da_sb[:], COPY, scale=ones[:, 0:1])
 
         def store_window(j, queue):
-            queue.dma_start(out_0[j * P : (j + 1) * P, :], windows[j % WINDOWS][:])
+            queue.dma_start(out_0[j * P : (j + 1) * P, :], windows[j][:])
 
         def copy_on_gpsimd(out, in_):
             nc.gpsimd.tensor_scalar(out, in_, 1.0, 0.0, MULT, ADD)
@@ -373,6 +374,7 @@ def tile_attend_glora_ax_kernel(
         quantize(x_mx01, x_grouped01[:], E4M3)
         quantize(v2_rows_mx[1], v2_rows1[0][:], E5M2)
         quantize(v2_rows_mx[1], v2_rows1[1][:], E5M2, 2 * P)
+        nc.gpsimd.memset(windows[2][:], 0.0)
         da0 = second_product(0, 0)
         da1 = second_product(1, 5)
         turn_x(x_rounded[3], 1)
@@ -381,12 +383,12 @@ def tile_attend_glora_ax_kernel(
         store_window(0, nc.sync)
         turn_a(0, a_listed[0], 7)
         turn_a(1, a_listed[1], 7)
-        nc.gpsimd.memset(windows[2][:], 0.0)
         da_sb1 = fetch("da_sb1", da1, V)
         group_x(3, 1, V)
         group_a(0, 7, V)
         quantize(x_mx[2], x_grouped[2], E4M3)
         quantize(x_mx[3], x_grouped[3], E4M3)
+        nc.gpsimd.memset(windows[3][:], 0.0)
         nc.vector.tensor_copy(windows[1][:].indirect(offsets[:]), da_sb1[:])
         store_window(1, nc.sync)
         da2 = second_product(2, 3)

@@ -34,19 +34,21 @@ KIB = 1024
 LAP = 64
 
 SIZES = {
-    "a_pool3": 8 * KIB, "v2_slots0a": 2 * KIB, "v2_slots0b": 2 * KIB, "a_pool0": 8 * KIB, "da_sb0": 2 * KIB,
-    "a_pool1": 8 * KIB, "da_sb1": 2 * KIB, "x_grouped3": 2 * KIB, "window3": 8 * KIB, "v2_rows1b": 2 * KIB,
-    "window2": 8 * KIB, "bt_scales_listed": SLOTS, "window0": 8 * KIB, "dy_raw0": 8 * KIB, "sc_cols0": LAP,
-    "row_factor1": 2 * KIB, "dy_grouped0": 4 * KIB, "window1": 8 * KIB, "dy_grouped1": 4 * KIB, "x_rounded2": 2 * KIB,
-    "x_rounded3": 2 * KIB, "v2_rows1a": 2 * KIB, "a_listed0": KIB, "a_listed1": KIB, "x2_codes": KIB,
-    "dy_raw1b": 4 * KIB, "sc_cols1": LAP, "x3_codes": KIB, "a_listed3": KIB, "x3_scales": 256, "a_listed2": KIB,
-    "a_slots": 4 * KIB, "v2_slots1a": 2 * KIB, "v2_slots3_codes": KIB, "da_sb3": 2 * KIB, "v2_slots1b": 2 * KIB,
+    "x2_scales": 256, "a_slots": 4 * KIB, "a_pool3": 8 * KIB, "v2_slots0a": 2 * KIB, "v2_slots0b": 2 * KIB,
+    "a_pool0": 8 * KIB, "da_sb0": 2 * KIB, "a_pool1": 8 * KIB, "da_sb1": 2 * KIB, "x2_codes": KIB,
+    "x_grouped3": 2 * KIB, "window3": 8 * KIB, "v2_rows1b": 2 * KIB, "window2": 8 * KIB, "bt_scales_listed": SLOTS,
+    "window0": 8 * KIB, "dy_raw0": 8 * KIB, "sc_cols0": LAP, "row_factor1": 2 * KIB, "dy_grouped0": 4 * KIB,
+    "window1": 8 * KIB, "dy_grouped1": 4 * KIB, "x_rounded2": 2 * KIB, "x_rounded3": 2 * KIB, "v2_rows1a": 2 * KIB,
+    "a_listed0": KIB, "a_listed1": KIB, "dy_raw1b": 4 * KIB, "sc_cols1": LAP, "x3_codes": KIB, "a_listed3": KIB,
+    "x3_scales": 256, "a_listed2": KIB, "v2_slots1a": 2 * KIB, "v2_slots3_codes": KIB, "da_sb3": 2 * KIB,
+    "v2_slots1b": 2 * KIB,
 }
 TAKEN_OVER_BY = {
+    "x2_scales": ("a_slots",),
     "a_pool3": ("v2_slots0a",),
     "v2_slots0a": ("v2_slots0b",),
     "a_pool0": ("da_sb0",),
-    "a_pool1": ("da_sb1", "x_grouped3"),
+    "a_pool1": ("da_sb1", "x2_codes", "x_grouped3"),
     "x_grouped3": ("window3",),
     "v2_rows1b": ("window2",),
     "bt_scales_listed": ("window0",),
@@ -54,7 +56,6 @@ TAKEN_OVER_BY = {
     "dy_grouped0": ("window1",),
     "dy_grouped1": ("x_rounded2", "x_rounded3"),
     "v2_rows1a": ("a_listed0", "a_listed1"),
-    "a_listed1": ("x2_codes",),
     "dy_raw1b": ("sc_cols1",),
     "x3_codes": ("a_listed3",),
     "x3_scales": ("a_listed2",),
@@ -385,7 +386,6 @@ def tile_attend_glora_ax_kernel(
         turn_a(1, a_listed[1], 7)
         da_sb1 = fetch("da_sb1", da1, V)
         group_x(3, 1, V)
-        group_a(0, 7, V)
         quantize(x_mx[2], x_grouped[2], E4M3)
         quantize(x_mx[3], x_grouped[3], E4M3)
         nc.gpsimd.memset(windows[3][:], 0.0)
@@ -393,7 +393,9 @@ def tile_attend_glora_ax_kernel(
         store_window(1, nc.sync)
         da2 = second_product(2, 3)
         da3 = second_product(3, 4)
-        scatter_on_scalar(2, fetch("da_sb2", da2, S))
+        da_sb2 = fetch("da_sb2", da2, S)
+        group_a(0, 7, S)
+        scatter_on_scalar(2, da_sb2)
         store_window(2, nc.sync)
         da_sb3 = fetch("da_sb3", da3, V)
         for j in range(2, PACK):

@@ -36,12 +36,12 @@ LAP = 64
 SIZES = {
     "x2_scales": 256, "a_slots": 4 * KIB, "a_pool3": 8 * KIB, "v2_slots0a": 2 * KIB, "v2_slots0b": 2 * KIB,
     "a_pool0": 8 * KIB, "da_sb0": 2 * KIB, "a_pool1": 8 * KIB, "da_sb1": 2 * KIB, "x2_codes": KIB,
-    "x_grouped3": 2 * KIB, "window3": 8 * KIB, "v2_rows1b": 2 * KIB, "window2": 8 * KIB, "bt_scales_listed": SLOTS,
+    "x_grouped3": 2 * KIB, "window2": 8 * KIB, "v2_rows1b": 2 * KIB, "x_grouped2": 2 * KIB, "bt_scales_listed": SLOTS,
     "window0": 8 * KIB, "dy_raw0": 8 * KIB, "sc_cols0": LAP, "row_factor1": 2 * KIB, "dy_grouped0": 4 * KIB,
     "window1": 8 * KIB, "dy_grouped1": 4 * KIB, "x_rounded2": 2 * KIB, "x_rounded3": 2 * KIB, "v2_rows1a": 2 * KIB,
-    "a_listed0": KIB, "a_listed1": KIB, "dy_raw1b": 4 * KIB, "sc_cols1": LAP, "x3_codes": KIB, "a_listed3": KIB,
-    "x3_scales": 256, "a_listed2": KIB, "v2_slots1a": 2 * KIB, "v2_slots3_codes": KIB, "da_sb3": 2 * KIB,
-    "v2_slots1b": 2 * KIB,
+    "a_listed0": KIB, "dy_raw1b": 4 * KIB, "sc_cols1": LAP, "x3_codes": KIB, "window3": 8 * KIB, "x3_scales": 256,
+    "a_listed2": KIB, "v2_slots1a": 2 * KIB, "v2_slots3_codes": KIB, "da_sb3": 2 * KIB, "v2_slots1b": 2 * KIB,
+    "a_listed3": KIB,
 }
 TAKEN_OVER_BY = {
     "x2_scales": ("a_slots",),
@@ -49,19 +49,20 @@ TAKEN_OVER_BY = {
     "v2_slots0a": ("v2_slots0b",),
     "a_pool0": ("da_sb0",),
     "a_pool1": ("da_sb1", "x2_codes", "x_grouped3"),
-    "x_grouped3": ("window3",),
-    "v2_rows1b": ("window2",),
+    "x_grouped3": ("window2",),
+    "v2_rows1b": ("x_grouped2",),
     "bt_scales_listed": ("window0",),
     "dy_raw0": ("sc_cols0", "row_factor1"),
     "dy_grouped0": ("window1",),
     "dy_grouped1": ("x_rounded2", "x_rounded3"),
-    "v2_rows1a": ("a_listed0", "a_listed1"),
+    "v2_rows1a": ("a_listed0",),
     "dy_raw1b": ("sc_cols1",),
-    "x3_codes": ("a_listed3",),
+    "x3_codes": ("window3",),
     "x3_scales": ("a_listed2",),
     "a_slots": ("v2_slots1a",),
     "v2_slots1a": ("v2_slots3_codes",),
     "da_sb3": ("v2_slots1b",),
+    "da_sb1": ("a_listed3",),
 }
 
 
@@ -370,12 +371,11 @@ def tile_attend_glora_ax_kernel(
         turn_v2(1, 0, 2, 4, v2_rows1[0][:])
         turn_x(x_rounded[2], 1)
         turn_v2(1, 2, 4, 6, v2_rows1[1][:])
-        group_x(2, 1, S)
         quantize(v2_rows_mx[0], v2_rows0[:], E5M2)
         quantize(x_mx01, x_grouped01[:], E4M3)
         quantize(v2_rows_mx[1], v2_rows1[0][:], E5M2)
         quantize(v2_rows_mx[1], v2_rows1[1][:], E5M2, 2 * P)
-        nc.gpsimd.memset(windows[2][:], 0.0)
+        group_x(2, 1, V)
         da0 = second_product(0, 0)
         da1 = second_product(1, 5)
         turn_x(x_rounded[3], 1)
@@ -388,6 +388,7 @@ def tile_attend_glora_ax_kernel(
         group_x(3, 1, V)
         quantize(x_mx[2], x_grouped[2], E4M3)
         quantize(x_mx[3], x_grouped[3], E4M3)
+        nc.gpsimd.memset(windows[2][:], 0.0)
         nc.gpsimd.memset(windows[3][:], 0.0)
         nc.vector.tensor_copy(windows[1][:].indirect(offsets[:]), da_sb1[:])
         store_window(1, nc.sync)

@@ -29,6 +29,7 @@ SCALAR_DY_QUADS = 48
 VECTOR_OUT_TILES = (2, 4, 6)
 OUT_BANKS = (0, 1, 5, 6, 3, 4, 7, 2)
 CHUNK = K_PASS // 2
+WINDOWS = 3
 RUN = 4
 KIB = 1024
 LAP = 64
@@ -39,9 +40,8 @@ SIZES = {
     "x_grouped3": 2 * KIB, "window2": 8 * KIB, "v2_rows1b": 2 * KIB, "x_grouped2": 2 * KIB, "bt_scales_listed": SLOTS,
     "window0": 8 * KIB, "dy_raw0": 8 * KIB, "sc_cols0": LAP, "row_factor1": 2 * KIB, "dy_grouped0": 4 * KIB,
     "window1": 8 * KIB, "dy_grouped1": 4 * KIB, "x_rounded2": 2 * KIB, "x_rounded3": 2 * KIB, "v2_rows1a": 2 * KIB,
-    "a_listed0": KIB, "dy_raw1b": 4 * KIB, "sc_cols1": LAP, "x3_codes": KIB, "window3": 8 * KIB, "x3_scales": 256,
+    "a_listed0": KIB, "dy_raw1b": 4 * KIB, "sc_cols1": LAP, "x3_codes": KIB, "a_listed3": KIB, "x3_scales": 256,
     "a_listed2": KIB, "v2_slots1a": 2 * KIB, "v2_slots3_codes": KIB, "da_sb3": 2 * KIB, "v2_slots1b": 2 * KIB,
-    "a_listed3": KIB,
 }
 TAKEN_OVER_BY = {
     "x2_scales": ("a_slots",),
@@ -57,12 +57,11 @@ TAKEN_OVER_BY = {
     "dy_grouped1": ("x_rounded2", "x_rounded3"),
     "v2_rows1a": ("a_listed0",),
     "dy_raw1b": ("sc_cols1",),
-    "x3_codes": ("window3",),
+    "x3_codes": ("a_listed3",),
     "x3_scales": ("a_listed2",),
     "a_slots": ("v2_slots1a",),
     "v2_slots1a": ("v2_slots3_codes",),
     "da_sb3": ("v2_slots1b",),
-    "da_sb1": ("a_listed3",),
 }
 
 
@@ -156,7 +155,7 @@ def tile_attend_glora_ax_kernel(
         x_raw = [load_x(j) for j in range(PACK)]
         a_pool = [load_a(j) for j in range(PACK)]
 
-        windows = [sbuf("window%d" % n, [P, T], F32) for n in range(PACK)]
+        windows = [sbuf("window%d" % n, [P, T], F32) for n in range(WINDOWS)]
 
         bt_scales_listed = sbuf("bt_scales_listed", [P, SLOTS], U8)
         nc.vector.tensor_copy(bt_scales_listed[:], bt_scale_pool[:].indirect(offsets[:]))
@@ -297,10 +296,10 @@ def tile_attend_glora_ax_kernel(
             return da_sb
 
         def scatter_on_scalar(j, da_sb):
-            nc.scalar.activation(windows[j][:].indirect(offsets[:]), da_sb[:], COPY, scale=ones[:, 0:1])
+            nc.scalar.activation(windows[j % WINDOWS][:].indirect(offsets[:]), da_sb[:], COPY, scale=ones[:, 0:1])
 
         def store_window(j, queue):
-            queue.dma_start(out_0[j * P : (j + 1) * P, :], windows[j][:])
+            queue.dma_start(out_0[j * P : (j + 1) * P, :], windows[j % WINDOWS][:])
 
         def copy_on_gpsimd(out, in_):
             nc.gpsimd.tensor_scalar(out, in_, 1.0, 0.0, MULT, ADD)
@@ -389,7 +388,6 @@ def tile_attend_glora_ax_kernel(
         quantize(x_mx[2], x_grouped[2], E4M3)
         quantize(x_mx[3], x_grouped[3], E4M3)
         nc.gpsimd.memset(windows[2][:], 0.0)
-        nc.gpsimd.memset(windows[3][:], 0.0)
         nc.vector.tensor_copy(windows[1][:].indirect(offsets[:]), da_sb1[:])
         store_window(1, nc.sync)
         da2 = second_product(2, 3)

from contextlib import ExitStack

import concourse.mybir as mybir

D, E, R, SLOTS, T = 512, 512, 1024, 512, 2048
FLOPS = 2 * (E * R * SLOTS + R * D * SLOTS + SLOTS * R * D)

F32 = mybir.dt.float32
BF16 = mybir.dt.bfloat16
I32 = mybir.dt.int32
U32 = mybir.dt.uint32
U16 = mybir.dt.uint16
U8 = mybir.dt.uint8
E4M3 = mybir.dt.float8_e4m3fn_x4
E5M2 = mybir.dt.float8_e5m2_x4
MULT = mybir.AluOpType.mult
ADD = mybir.AluOpType.add
COPY = mybir.ActivationFunctionType.Copy

P = 128
PACK = 4
K_PASS = P * PACK
ROW_PASSES = R // K_PASS
BANKS = 8
QUADRANT = 32
SCALE_ROWS = K_PASS // 32
LIST_ROWS = 16
SCALAR_DY_QUADS = 48
VECTOR_OUT_TILES = (2, 4, 6)
OUT_BANKS = (0, 1, 5, 6, 3, 4, 7, 2)
CHUNK = K_PASS // 2
WINDOWS = 3
RUN = 4
KIB = 1024
LAP = 64

SIZES = {
    "x2_scales": 256, "a_slots": 4 * KIB, "a_pool3": 8 * KIB, "v2_slots0a": 2 * KIB, "v2_slots0b": 2 * KIB,
    "a_pool0": 8 * KIB, "da_sb0": 2 * KIB, "a_pool1": 8 * KIB, "da_sb1": 2 * KIB, "x2_codes": KIB,
    "x_grouped3": 2 * KIB, "window2": 8 * KIB, "v2_rows1b": 2 * KIB, "x_grouped2": 2 * KIB, "bt_scales_listed": SLOTS,
    "window0": 8 * KIB, "dy_raw0": 8 * KIB, "sc_cols0": LAP, "row_factor1": 2 * KIB, "dy_grouped0": 4 * KIB,
    "window1": 8 * KIB, "dy_grouped1": 4 * KIB, "x_rounded2": 2 * KIB, "x_rounded3": 2 * KIB, "v2_rows1a": 2 * KIB,
    "a_listed0": KIB, "dy_raw1b": 4 * KIB, "sc_cols1": LAP, "x3_codes": KIB, "a_listed3": KIB, "x3_scales": 256,
    "a_listed2": KIB, "v2_slots1a": 2 * KIB, "v2_slots3_codes": KIB, "da_sb3": 2 * KIB, "v2_slots1b": 2 * KIB,
}
TAKEN_OVER_BY = {
    "x2_scales": ("a_slots",),
    "a_pool3": ("v2_slots0a",),
    "v2_slots0a": ("v2_slots0b",),
    "a_pool0": ("da_sb0",),
    "a_pool1": ("da_sb1", "x2_codes", "x_grouped3"),
    "x_grouped3": ("window2",),
    "v2_rows1b": ("x_grouped2",),
    "bt_scales_listed": ("window0",),
    "dy_raw0": ("sc_cols0", "row_factor1"),
    "dy_grouped0": ("window1",),
    "dy_grouped1": ("x_rounded2", "x_rounded3"),
    "v2_rows1a": ("a_listed0",),
    "dy_raw1b": ("sc_cols1",),
    "x3_codes": ("a_listed3",),
    "x3_scales": ("a_listed2",),
    "a_slots": ("v2_slots1a",),
    "v2_slots1a": ("v2_slots3_codes",),
    "da_sb3": ("v2_slots1b",),
}


def placement():
    at = {}

    def place(name, start):
        at[name] = start
        end = start + SIZES[name]
        heirs = TAKEN_OVER_BY.get(name, ())
        inside = start + LAP
        for heir in heirs[:-1]:
            inside = place(heir, inside)
            assert inside <= end - LAP
        return place(heirs[-1], end - LAP) if heirs else end

    top = 0
    for name in TAKEN_OVER_BY:
        if name not in at:
            top = place(name, top)
    return at


def tile_attend_glora_ax_kernel(
    tc, xT, A, dyT, Bt_words, Bt_scales, us, sc, wt, offs, out_0, out_1
):
    nc = tc.nc
    with ExitStack() as ctx:
        keep = ctx.enter_context(tc.tile_pool(name="keep", bufs=1))
        placed = ctx.enter_context(tc.tile_pool(name="placed", bufs=1))
        psum = ctx.enter_context(tc.psum_pool(name="psum", bufs=1))
        banks = [psum.tile([P, K_PASS], F32, name="bank%d" % n) for n in range(BANKS)]
        at = placement()

        def quarters(bank):
            return bank[:].rearrange("p (c m) -> p c m", c=PACK)

        def sbuf(name, shape, dtype):
            if name not in at:
                return keep.tile(shape, dtype, name=name, align_bytes=64)
            return placed.tile(shape, dtype, name=name, align_bytes=64, offset=at[name])

        def mx_tiles(name, width):
            return sbuf(name + "_codes", [P, width], U32), sbuf(name + "_scales", [P, width], U8)

        def quantize(mx, grouped, fmt, first=0):
            cols = slice(first, first + grouped.shape[1] // PACK)
            nc.vector.quantize_mx(out=mx[0][:, cols].bitcast(fmt), scales=mx[1][:, cols], in_=grouped)

        offsets = keep.tile([P, SLOTS // LIST_ROWS], U16, name="offsets")
        nc.sync.dma_start(offsets[:], offs)
        ones = sbuf("ones", [P, P], F32)
        nc.vector.memset(ones[:], 1.0)
        bt_scale_pool = sbuf("bt_scale_pool", [P, T], U8)
        nc.vector.memset(bt_scale_pool[0 : P - SCALE_ROWS, :].bitcast(I32), 0)
        nc.scalar.dma_start(bt_scale_pool[P - SCALE_ROWS : P, :].bitcast(I32), Bt_scales[0].bitcast(I32))
        us_tile = sbuf("us_tile", [P, ROW_PASSES, 2 * PACK], F32)
        us_cols = us_tile[:, :, 0:PACK]
        wt_tile = sbuf("wt_tile", [P, ROW_PASSES, 2 * PACK], F32)
        wt_cols = wt_tile[:, :, 0:PACK]
        nc.scalar.dma_start(us_cols, us.rearrange("(g p t) o -> p g (t o)", g=ROW_PASSES, t=PACK))
        nc.scalar.dma_start(wt_cols, wt.rearrange("(g p t) o -> p g (t o)", g=ROW_PASSES, t=PACK))
        ident = sbuf("ident", [P, P], F32)
        nc.gpsimd.affine_select(
            out=ident[:], in_=ones[:], pattern=[[-1, P]], compare_op=mybir.AluOpType.is_equal, fill=0.0, base=0,
            channel_multiplier=1,
        )
        sc_pool = sbuf("sc_pool", [P, T], F32)
        nc.vector.memset(sc_pool[0 : P - 1, :].bitcast(I32), 0)
        nc.sync.dma_start(sc_pool[P - 1 : P, :], sc[P - 1 : P, :])
        bt_word_pool = sbuf("bt_word_pool", [P, T], I32)
        nc.sync.dma_start(bt_word_pool[:], Bt_words[0].rearrange("p n t -> p (n t)").bitcast(I32))

        def load_dy(name, r0, r1):
            raw = sbuf(name, [P, PACK, r1 - r0], F32)
            nc.sync.dma_start(raw[:], dyT[:, r0:r1].rearrange("(p j) r -> p j r", j=PACK))
            return raw

        def load_x(j):
            raw = sbuf("x_raw%d" % j, [P, R], F32)
            nc.sync.dma_start(raw[:], xT[j * P : (j + 1) * P, :])
            return raw

        def load_a(j):
            pool = sbuf("a_pool%d" % j, [P, T], F32)
            nc.sync.dma_start(pool[:], A[j * P : (j + 1) * P, :])
            return pool

        dy_raw0 = load_dy("dy_raw0", 0, K_PASS)
        dy_raw1 = [load_dy("dy_raw1" + "ab"[h], K_PASS + h * CHUNK, K_PASS + (h + 1) * CHUNK) for h in range(2)]
        x_raw = [load_x(j) for j in range(PACK)]
        a_pool = [load_a(j) for j in range(PACK)]

        windows = [sbuf("window%d" % n, [P, T], F32) for n in range(WINDOWS)]

        bt_scales_listed = sbuf("bt_scales_listed", [P, SLOTS], U8)
        nc.vector.tensor_copy(bt_scales_listed[:], bt_scale_pool[:].indirect(offsets[:]))
        factor_cols = sbuf("factor_cols", [P, ROW_PASSES, PACK], F32)
        nc.vector.tensor_tensor(factor_cols[:], us_cols, wt_cols, MULT)
        bt_scales = sbuf("bt_scales", [P, SLOTS], U8)
        nc.vector.tensor_copy(
            bt_scales[:].rearrange("p (t m) -> p t m", t=PACK),
            bt_scales_listed[:].rearrange("p (m t) -> p t m", t=PACK),
        )
        for q in range(P // QUADRANT):
            first = P - SCALE_ROWS + PACK * q
            nc.scalar.dma_start(
                bt_scales[QUADRANT * q : QUADRANT * q + PACK, :].bitcast(I32),
                bt_scales[first : first + PACK, :].bitcast(I32),
            )
        nc.gpsimd.memset(windows[0][:], 0.0)
        sc_row = sbuf("sc_row", [P, SLOTS], F32)
        nc.vector.tensor_copy(sc_row[:], sc_pool[:].indirect(offsets[:]))
        bt_codes_listed = sbuf("bt_codes_listed", [P, SLOTS], U32)
        nc.vector.tensor_copy(bt_codes_listed[:], bt_word_pool[:].bitcast(U32).indirect(offsets[:]))
        bt_codes = sbuf("bt_codes", [P, SLOTS], U32)
        nc.vector.tensor_copy(
            bt_codes[:].bitcast(I32).rearrange("p (t c n) -> p c t n", t=PACK, n=RUN),
            bt_codes_listed[:].bitcast(I32).rearrange("p (c n t) -> p c t n", t=PACK, n=RUN),
        )

        row_factor = [sbuf("row_factor%d" % g, [P, K_PASS], F32) for g in range(ROW_PASSES)]

        for g in range(ROW_PASSES):
            for t in range(PACK):
                nc.tensor.transpose(
                    quarters(banks[5 + g])[:, t, :], factor_cols[:, g, t : t + 1].to_broadcast([P, P]), ident[:]
                )
        sc_turned = [quarters(banks[4 + 3 * h]) for h in range(2)]
        for t in range(PACK):
            nc.tensor.transpose(sc_turned[t // 2][:, t % 2, :], sc_row[:, t:SLOTS:PACK], ident[:])

        def spread_factor(g, copy):
            spread = quarters(banks[5 + g])
            copy(
                row_factor[g][:].rearrange("p (u m e) -> p u m e", u=2, e=2), spread.rearrange("p (u e) m -> p u m e", u=2)
            )

        sc_cols = [sbuf("sc_cols%d" % h, [P, 2], F32) for h in range(2)]

        v2_tiles = [sbuf("v2_%d" % g, [P, PACK * K_PASS], BF16) for g in range(ROW_PASSES)]
        v2_rows_mx = [mx_tiles("v2_rows%d" % g, SLOTS) for g in range(ROW_PASSES)]
        dy_mx = [mx_tiles("dy%d" % g, K_PASS) for g in range(ROW_PASSES)]
        dy_grouped = [sbuf("dy_grouped%d" % g, [P, K_PASS * PACK], BF16) for g in range(ROW_PASSES)]

        def group_dy(g, raw, copy, m0, m1, first=0):
            copy(
                dy_grouped[g][:].rearrange("p (u m e j) -> p m j u e", u=2, e=2, j=PACK)[:, first + m0 : first + m1],
                raw[:].rearrange("p j (m u e) -> p m j u e", u=2, e=2)[:, m0:m1],
            )

        def first_pass(g, t):
            cols = slice(t * P, (t + 1) * P)
            nc.tensor.matmul_mx(
                out=banks[PACK * g + t][:], lhsT=bt_codes[:, cols].bitcast(E4M3), lhsT_scale=bt_scales[:, cols],
                rhs=dy_mx[g][0][:].bitcast(E5M2), rhs_scale=dy_mx[g][1][:], start=True, stop=True,
            )

        def scale_v(g, t):
            nc.vector.scalar_tensor_tensor(
                v2_tiles[g][:, t * K_PASS : (t + 1) * K_PASS], banks[PACK * g + t][:], sc_cols[t // 2][:, t % 2 : t % 2 + 1], row_factor[g][:], MULT, MULT
            )

        def turn_start(words, into):
            for b in range(len(words)):
                for u in range(2):
                    nc.tensor.transpose(quarters(banks[into])[:, 2 * b + u, :], words[b][u], ident[:])

        def turn_finish(grouped, into, copy):
            count = grouped.shape[1] // K_PASS
            bank = banks[into][:, 0 : count * 2 * P].rearrange("p (b u m) -> p b m u", b=count, u=2)
            copy(grouped.bitcast(F32).rearrange("p (b m u) -> p b m u", b=count, u=2), bank)

        def turn_v2(g, t0, t1, into, grouped):
            words = v2_tiles[g][:].bitcast(F32).rearrange("p (t u m) -> p t u m", t=PACK, u=2)
            turn_start([[words[:, t, u, :] for u in range(2)] for t in range(t0, t1)], into)
            turn_finish(grouped, into, nc.scalar.copy)

        def round_x(j, raw, rounder):
            rounded = sbuf("x_rounded%d" % j, [P, R], BF16)
            rounder(
                rounded[:].rearrange("p (u m e) -> p u m e", u=2, e=2), raw[:].rearrange("p (m u e) -> p u m e", u=2, e=2)
            )
            return rounded

        def turn_x(rounded, into):
            words = rounded[:].bitcast(F32).rearrange("p (u g m) -> p g u m", u=2, g=ROW_PASSES)
            turn_start([[words[:, g, u, :] for u in range(2)] for g in range(ROW_PASSES)], into)

        x_grouped01 = sbuf("x_grouped01", [P, 2 * R], BF16)
        x_grouped = [x_grouped01[:, 0:R], x_grouped01[:, R:]] + [sbuf("x_grouped%d" % j, [P, R], BF16)[:] for j in (2, 3)]
        x_mx01 = mx_tiles("x01", 2 * R // PACK)
        x_mx = [[part[:, j * R // PACK : (j + 1) * R // PACK] for part in x_mx01] for j in range(2)]
        x_mx += [mx_tiles("x%d" % j, R // PACK) for j in (2, 3)]

        def group_x(j, into, copy):
            turn_finish(x_grouped[j], into, copy)

        def gather_a(j, pool, on_scalar):
            listed = sbuf("a_listed%d" % j, [P, SLOTS], BF16)
            if on_scalar:
                nc.scalar.activation(listed[:], pool[:].indirect(offsets[:]), COPY)
            else:
                nc.vector.tensor_copy(listed[:], pool[:].indirect(offsets[:]))
            return listed

        def turn_a(j, listed, into):
            words = listed[:].bitcast(F32).rearrange("p (m u) -> p u m", u=2)
            for u in range(2):
                nc.tensor.transpose(quarters(banks[into])[:, 2 * (j % 2) + u, :], words[:, u, :], ident[:])

        a_slots = sbuf("a_slots", [P, PACK * K_PASS], BF16)

        def group_a(h, into, copy):
            turn_finish(a_slots[:, 2 * h * K_PASS : 2 * (h + 1) * K_PASS], into, copy)

        def second_product(j, into):
            da = banks[into]
            codes, scales = x_mx[j]
            for g in range(ROW_PASSES):
                cols = slice(g * P, (g + 1) * P)
                nc.tensor.matmul_mx(
                    out=da[:], lhsT=codes[:, cols].bitcast(E4M3), lhsT_scale=scales[:, cols],
                    rhs=v2_rows_mx[g][0][:].bitcast(E5M2), rhs_scale=v2_rows_mx[g][1][:],
                    start=(g == 0), stop=(g == ROW_PASSES - 1),
                )
            return da

        def fetch(name, da, copy):
            da_sb = sbuf(name, [P, SLOTS], F32)
            copy(da_sb[:].rearrange("p (m t) -> p m t", t=PACK), quarters(da).rearrange("p t m -> p m t"))
            return da_sb

        def scatter_on_scalar(j, da_sb):
            nc.scalar.activation(windows[j % WINDOWS][:].indirect(offsets[:]), da_sb[:], COPY, scale=ones[:, 0:1])

        def store_window(j, queue):
            queue.dma_start(out_0[j * P : (j + 1) * P, :], windows[j % WINDOWS][:])

        def copy_on_gpsimd(out, in_):
            nc.gpsimd.tensor_scalar(out, in_, 1.0, 0.0, MULT, ADD)

        v2_slots_mx = [mx_tiles("v2_slots%d" % n, 2 * P) for n in range(PACK)]

        def group_v2_slots(name, g, u0, u1, copy, order="m t e"):
            grouped = sbuf(name, [P, (u1 - u0) * R], BF16)
            src = v2_tiles[g][:].rearrange("p (t u m e) -> p u " + order, t=PACK, u=2, e=2)
            dst = grouped[:].rearrange("p (u e m t) -> p u " + order, e=2, m=P, t=PACK)
            if u1 - u0 == 1:
                copy(dst[:, 0], src[:, u0])
            else:
                copy(dst, src)
            return grouped

        dx = sbuf("dx", [P, R // P, D], F32)
        a_mx = mx_tiles("a", D)

        def third_pass(n, into):
            acc = banks[into]
            codes, scales = v2_slots_mx[n // 2]
            cols = slice(n % 2 * P, (n % 2 + 1) * P)
            nc.tensor.matmul_mx(
                out=acc[:], lhsT=codes[:, cols].bitcast(E5M2), lhsT_scale=scales[:, cols],
                rhs=a_mx[0][:].bitcast(E4M3), rhs_scale=a_mx[1][:], start=True, stop=True,
            )

        def put_out(n, into, copy):
            copy(dx[:, n, :], banks[into][:])
            if n % 2 == 1:
                g, c = divmod(n - 1, PACK)
                rows = out_1[g * K_PASS : (g + 1) * K_PASS, :].rearrange("(m n) d -> m n d", n=PACK)
                nc.sync.dma_start(rows[:, c : c + 2, :], dx[:, n - 1 : n + 1, :])

        V, S = nc.vector.tensor_copy, nc.scalar.copy
        spread_factor(0, S)
        group_dy(0, dy_raw0, S, 0, SCALAR_DY_QUADS)
        group_dy(0, dy_raw0, V, SCALAR_DY_QUADS, P)
        quantize(dy_mx[0], dy_grouped[0][:], E5M2)
        V(sc_cols[0][:], sc_turned[0][:, 0:2, P - 1])
        spread_factor(1, V)
        nc.gpsimd.memset(windows[1][:], 0.0)
        for h in range(2):
            group_dy(1, dy_raw1[h], S, 0, P // 2, h * P // 2)
        for t in range(PACK):
            first_pass(0, t)
        scale_v(0, 0)
        scale_v(0, 1)
        V(sc_cols[1][:], sc_turned[1][:, 0:2, P - 1])
        quantize(dy_mx[1], dy_grouped[1][:], E5M2)
        scale_v(0, 2)
        scale_v(0, 3)
        for t in range(PACK):
            first_pass(1, t)
        x_rounded = [round_x(0, x_raw[0], S)]
        v2_rows0 = sbuf("v2_rows0", [P, SLOTS * PACK], BF16)
        v2_rows1 = [sbuf("v2_rows1" + half, [P, 2 * K_PASS], BF16) for half in "ab"]
        turn_v2(0, 0, 2, 0, v2_rows0[:, 0 : 2 * K_PASS])
        x_rounded += [round_x(j, x_raw[j], S if j == 1 else copy_on_gpsimd) for j in range(1, PACK)]
        turn_x(x_rounded[0], 1)
        group_x(0, 1, S)
        turn_v2(0, 2, 4, 2, v2_rows0[:, 2 * K_PASS :])
        for t in range(PACK):
            scale_v(1, t)
        turn_x(x_rounded[1], 3)
        group_x(1, 3, S)
        turn_v2(1, 0, 2, 4, v2_rows1[0][:])
        turn_x(x_rounded[2], 1)
        turn_v2(1, 2, 4, 6, v2_rows1[1][:])
        quantize(v2_rows_mx[0], v2_rows0[:], E5M2)
        quantize(x_mx01, x_grouped01[:], E4M3)
        quantize(v2_rows_mx[1], v2_rows1[0][:], E5M2)
        quantize(v2_rows_mx[1], v2_rows1[1][:], E5M2, 2 * P)
        group_x(2, 1, V)
        da0 = second_product(0, 0)
        da1 = second_product(1, 5)
        turn_x(x_rounded[3], 1)
        a_listed = [gather_a(0, a_pool[0], True), gather_a(1, a_pool[1], False)]
        scatter_on_scalar(0, fetch("da_sb0", da0, S))
        store_window(0, nc.sync)
        turn_a(0, a_listed[0], 7)
        turn_a(1, a_listed[1], 7)
        da_sb1 = fetch("da_sb1", da1, V)
        group_x(3, 1, V)
        quantize(x_mx[2], x_grouped[2], E4M3)
        quantize(x_mx[3], x_grouped[3], E4M3)
        nc.gpsimd.memset(windows[2][:], 0.0)
        nc.vector.tensor_copy(windows[1][:].indirect(offsets[:]), da_sb1[:])
        store_window(1, nc.sync)
        da2 = second_product(2, 3)
        da3 = second_product(3, 4)
        da_sb2 = fetch("da_sb2", da2, S)
        group_a(0, 7, S)
        scatter_on_scalar(2, da_sb2)
        store_window(2, nc.sync)
        da_sb3 = fetch("da_sb3", da3, V)
        for j in range(2, PACK):
            a_listed.append(gather_a(j, a_pool[j], False))
            turn_a(j, a_listed[j], 2)
        scatter_on_scalar(3, da_sb3)
        store_window(3, nc.sync)
        v2_slots0a = group_v2_slots("v2_slots0a", 0, 0, 1, V)
        group_a(1, 2, V)
        quantize(v2_slots_mx[0], v2_slots0a[:], E5M2)
        quantize(a_mx, a_slots[:], E4M3)
        v2_slots0b = group_v2_slots("v2_slots0b", 0, 1, 2, V)
        v2_slots1a = group_v2_slots("v2_slots1a", 1, 0, 1, V)
        quantize(v2_slots_mx[1], v2_slots0b[:], E5M2)
        v2_slots1b = group_v2_slots("v2_slots1b", 1, 1, 2, S)
        for n in range(PACK):
            third_pass(n, OUT_BANKS[n])
        put_out(0, OUT_BANKS[0], V)
        quantize(v2_slots_mx[2], v2_slots1a[:], E5M2)
        put_out(1, OUT_BANKS[1], S)
        quantize(v2_slots_mx[3], v2_slots1b[:], E5M2)
        for n in range(PACK, 2 * PACK):
            third_pass(n, OUT_BANKS[n])
        for n in range(2, 2 * PACK):
            put_out(n, OUT_BANKS[n], V if n in VECTOR_OUT_TILES else S)
